import numpy as np
import ml_dtypes


def mxq(x, axis, fmt="e4m3"):
    dtype, down = {"e4m3": (ml_dtypes.float8_e4m3fn, 7), "e5m2": (ml_dtypes.float8_e5m2, 14)}[fmt]
    v = np.moveaxis(np.asarray(x, np.float32).astype(ml_dtypes.bfloat16).astype(np.float64), axis, -1)
    blocks = v.reshape(v.shape[:-1] + (-1, 32))
    amax = np.abs(blocks).max(-1, keepdims=True)
    byte = np.maximum(np.where(amax > 0, np.frexp(amax)[1] - 1 + 127, 0) - down, 1)
    scale = np.exp2(byte - 127.0)
    codes = (blocks / scale).astype(np.float32).astype(dtype).astype(np.float64)
    return np.moveaxis((codes * scale).reshape(v.shape), -1, axis)


WIDE = False


def mx_kscale(k):
    if not WIDE:
        return np.ones(k)
    levels = np.array([10, -10, 5, -5, 0])
    if k % 512:
        return np.exp2(np.random.permutation(np.resize(levels, k // 32))).repeat(32)
    a = np.empty((k // 512, 16))
    for p in range(k // 512):
        a[p, :8] = np.random.permutation(np.resize(levels, 8))
        for g in range(8):
            far = levels[np.abs(levels - a[p, g]) >= 10]
            a[p, g + 8] = far[np.random.randint(len(far))]
    return np.exp2(a.ravel()).repeat(32)


def f64(x):
    return np.asarray(x).astype(np.float64)


def striped(idx):
    return np.tile(idx.reshape(-1, 16).T, (8, 1)).astype(np.uint16)


def unstriped(offs):
    return offs[:16].T.reshape(-1).astype(np.int64)


E2M1 = np.array([0.0, 0.5, 1.0, 1.5, 2.0, 3.0, 4.0, 6.0, -0.0, -0.5, -1.0, -1.5, -2.0, -3.0, -4.0, -6.0])


def pack_weight(w, fmt):
    k, n = w.shape
    w = f64(np.asarray(w, np.float32).astype(ml_dtypes.bfloat16)).reshape(k // 32, 32, n)
    amax = np.abs(w).max(1)
    if fmt == "e4m3":
        byte = np.frexp(amax)[1] - 1 + 127 - 7
    else:
        mant, ex = np.frexp(amax / 6.0)
        byte = np.where(mant > 0.5, ex, ex - 1) + 127
    byte = np.clip(np.where(amax > 0, byte, 1), 1, 254)
    scaled = (w * np.exp2(127.0 - byte)[:, None, :]).reshape(k, n).astype(np.float32)
    by_word = np.ascontiguousarray(scaled.reshape(k // 512, 128, 4, n).transpose(0, 1, 3, 2))
    if fmt == "e4m3":
        words = by_word.astype(ml_dtypes.float8_e4m3fn).view(np.uint8)
    else:
        c = by_word.astype(ml_dtypes.float4_e2m1fn).view(np.uint8) & 0xF
        words = (c[..., 0::2] | (c[..., 1::2] << 4)).reshape(k // 512, 128, 2 * n)
    return np.ascontiguousarray(words), np.ascontiguousarray(byte.astype(np.uint8).reshape(k // 512, 16, n))


def unpack_weight(words, scales, fmt):
    g, _, n = scales.shape
    words = np.ascontiguousarray(words).reshape(g, 128, n, -1)
    if fmt == "e4m3":
        vals = words.view(ml_dtypes.float8_e4m3fn).astype(np.float64)
    else:
        nib = np.empty((g, 128, n, 4), np.uint8)
        nib[..., 0::2] = words & 0xF
        nib[..., 1::2] = words >> 4
        vals = E2M1[nib]
    vals = vals * np.repeat(np.exp2(scales.astype(np.float64) - 127.0), 8, axis=1)[..., None]
    return vals.transpose(0, 1, 3, 2).reshape(g * 512, n)


def gelu(v):
    return 0.5 * v * (1.0 + np.tanh(np.sqrt(2.0 / np.pi) * (v + 0.044715 * v**3)))


def bf(x):
    return np.asarray(x, np.float32).astype(ml_dtypes.bfloat16)


def planes(Y):
    n, m = Y.shape
    b = f64(bf(Y)).reshape(n // 32, 32, m)
    amax = np.abs(b).max(1)
    byte = np.clip(np.where(amax > 0, np.frexp(amax)[1] - 1 + 127 - 7, 1), 1, 254)
    codes = (b * np.exp2(127.0 - byte)[:, None, :]).reshape(n, m).astype(np.float32).astype(ml_dtypes.float8_e4m3fn).view(np.uint8)
    words = codes.reshape(n // 512, 128, 4, m).transpose(0, 1, 3, 2)
    return np.ascontiguousarray(words), np.ascontiguousarray(byte.astype(np.uint8).reshape(n // 512, 16, m))


T, S, K, H, N = 4096, 1024, 512, 1536, 768

def setup_inputs():
    n = np.random.standard_normal
    s = mx_kscale(K)[:, None]
    u = mx_kscale(H)[:, None]
    tab_words, tab_scales = pack_weight(n((K, T)) * s, "e4m3")
    w2_words, w2_scales = pack_weight(n((K, H)) / np.sqrt(K) / s, "e2m1")
    w3_words, w3_scales = pack_weight(n((H, N)) / np.sqrt(H) / u, "e4m3")
    return {
        "tab_words": tab_words, "tab_scales": tab_scales,
        "offs": striped(np.random.permutation(T)[:S]),
        "w1": (n((K, H)) / np.sqrt(K) / s * u.T).astype(np.float32),
        "load": (0.5 * n(H) * u[:, 0]).astype(np.float32),
        "w2_words": w2_words, "w2_scales": w2_scales,
        "att": (0.5 * n(H)).astype(np.float32),
        "w3_words": w3_words, "w3_scales": w3_scales,
        "prem": (0.7 * n((N, S))).astype(np.float32),
    }

def reference(tab_words, tab_scales, offs, w1, load, w2_words, w2_scales,
              att, w3_words, w3_scales, prem):
    v = unpack_weight(tab_words, tab_scales, "e4m3")[:, unstriped(offs)]
    loss = (mxq(f64(w1), 0, "e4m3").T @ v) + f64(load)[:, None]
    hit = (unpack_weight(w2_words, w2_scales, "e2m1").T @ v) + f64(att)[:, None]
    h = loss * (1.0 / (1.0 + np.exp(-hit)))
    w3 = unpack_weight(w3_words, w3_scales, "e4m3")
    y = (w3.T @ mxq(h, 0, "e4m3")) + f64(prem)
    words, scales = planes(h)
    return y, h, words, scales

@@ -1,0 +1,228 @@
+from contextlib import ExitStack
+
+import concourse.mybir as mybir
+
+T, S, K, H, N = 4096, 1024, 512, 1536, 768
+FLOPS = 2 * S * (2 * K * H + H * N)
+
+F32 = mybir.dt.float32
+BF16 = mybir.dt.bfloat16
+I32 = mybir.dt.int32
+U32 = mybir.dt.uint32
+U16 = mybir.dt.uint16
+U8 = mybir.dt.uint8
+FP8X4 = mybir.dt.float8_e4m3fn_x4
+FP4X4 = mybir.dt.float4_e2m1fn_x4
+ADD = mybir.AluOpType.add
+MULT = mybir.AluOpType.mult
+SIGMOID = mybir.ActivationFunctionType.Sigmoid
+
+P = 128
+PACK = 4
+G = H // (P * PACK)
+HALF = 512
+HALVES = S // HALF
+LINES = N // P
+VECTOR_COLS = (304, 304, 304, 304, 192, 0)
+
+
+def tile_list_treaty_pricing_kernel(
+    tc, tab_words, tab_scales, offs, w1, load, w2_words, w2_scales, att, w3_words, w3_scales, prem,
+    out_0, out_1, out_2, out_3,
+):
+    nc = tc.nc
+    with ExitStack() as ctx:
+        held = ctx.enter_context(tc.tile_pool(name="held", bufs=1))
+        ring = ctx.enter_context(tc.tile_pool(name="ring", bufs=3))
+        gates = ctx.enter_context(tc.tile_pool(name="gates", bufs=8))
+        psum = ctx.enter_context(tc.psum_pool(name="psum", bufs=1))
+
+        def keep(name, shape, dtype):
+            return held.tile(shape, dtype, name=name, align_bytes=64)
+
+        def bank(b):
+            return psum.tile([P, HALF], F32, name="bank%d" % b)
+
+        def load_scale_rows(queue, plane, rows):
+            for q in range(4):
+                queue.dma_start(out=plane[32 * q : 32 * q + 4], in_=rows(q))
+
+        offsets = held.tile([P, S // 16], U16, name="offsets")
+        nc.sync.dma_start(offsets[:], offs)
+
+        w1_rows = w1.rearrange("(p j) c -> p j c", j=PACK)
+        w1_raw = [keep("w1_raw%d" % g, [P, PACK, 512], F32) for g in range(G)]
+        nc.sync.dma_start(out=w1_raw[0][:], in_=w1_rows[:, :, 0:512])
+        w2_raw = keep("w2_raw", [P, 2 * H], U8)
+        nc.sync.dma_start(out=w2_raw[:].bitcast(I32), in_=w2_words[0].bitcast(I32))
+        tab_s = keep("tab_s", [P, T], U8)
+        nc.vector.memset(tab_s[:].bitcast(I32), 0)
+        load_scale_rows(nc.sync, tab_s[:].bitcast(I32), lambda q: tab_scales[0, 4 * q : 4 * q + 4, :].bitcast(I32))
+        tab_w = keep("tab_w", [P, T], U32)
+        nc.sync.dma_start(out=tab_w[:].bitcast(I32), in_=tab_words[0].rearrange("p n t -> p (n t)").bitcast(I32))
+        w2s_raw = keep("w2s_raw", [P, H], U8)
+        nc.vector.memset(w2s_raw[:].bitcast(I32), 0)
+        load_scale_rows(nc.sync, w2s_raw[:].bitcast(I32), lambda q: w2_scales[0, 4 * q : 4 * q + 4, :].bitcast(I32))
+        att_sb = keep("att_sb", [P, G, 8], F32)
+        nc.scalar.dma_start(out=att_sb[:, :, 0:PACK], in_=att.rearrange("(g p t) -> p g t", p=P, t=PACK))
+        load_sb = keep("load_sb", [P, G, 8], F32)
+        nc.scalar.dma_start(out=load_sb[:, :, 0:PACK], in_=load.rearrange("(g p t) -> p g t", p=P, t=PACK))
+        for g in range(1, G):
+            nc.sync.dma_start(out=w1_raw[g][:], in_=w1_rows[:, :, 512 * g : 512 * (g + 1)])
+        w3_w = keep("w3_w", [P, G, N], U32)
+        w3_s = keep("w3_s", [P, G, N], U8)
+        nc.vector.memset(w3_s[:].bitcast(I32), 0)
+        load_scale_rows(
+            nc.sync, w3_s[:].bitcast(I32),
+            lambda q: w3_scales[:, 4 * q : 4 * q + 4, :].rearrange("g r n -> r g n").bitcast(I32),
+        )
+        nc.sync.dma_start(out=w3_w[:].bitcast(I32), in_=w3_words.rearrange("g p n t -> p g (n t)").bitcast(I32))
+        prem_rows = prem.rearrange("(c p) j -> p c j", p=P)
+        y_sb = [keep("y%d" % i, [P, LINES // 2, S], F32) for i in range(2)]
+        for i in range(2):
+            nc.sync.dma_start(out=y_sb[i][:], in_=prem_rows[:, 3 * i : 3 * i + 3, :])
+
+        warm = keep("warm", [P, 8], F32)
+        nc.vector.memset(warm[:], 0.0)
+        warm_out = keep("warm_out", [P, 8], F32)
+        nc.scalar.activation(out=warm_out[:], in_=warm[:], func=SIGMOID)
+
+        w2_w = [keep("w2_w%d" % g, [P, 2 * 512], U8) for g in range(G)]
+        w2_s = [keep("w2_s%d" % g, [P, 512], U8) for g in range(G)]
+
+        def deal_w2(g):
+            nc.vector.tensor_copy(
+                out=w2_w[g][:].bitcast(U16).rearrange("p (t m) -> p t m", t=PACK),
+                in_=w2_raw[:, 1024 * g : 1024 * (g + 1)].bitcast(U16).rearrange("p (m t) -> p t m", t=PACK),
+            )
+
+        def deal_w2_scales(g):
+            nc.vector.tensor_copy(
+                out=w2_s[g][:].rearrange("p (t m) -> p t m", t=PACK),
+                in_=w2s_raw[:, 512 * g : 512 * (g + 1)].rearrange("p (m t) -> p t m", t=PACK),
+            )
+
+        v_w = [keep("v_w%d" % a, [P, HALF], U32) for a in range(HALVES)]
+        v_s = [keep("v_s%d" % a, [P, HALF], U8) for a in range(HALVES)]
+        lists = [offsets[:, 32 * a : 32 * (a + 1)] for a in range(HALVES)]
+        w1_b = [keep("w1_b%d" % g, [P, PACK, P, PACK], BF16) for g in range(G)]
+        w1_w = [keep("w1_w%d" % g, [P, 512], U32) for g in range(G)]
+        w1_s = [keep("w1_s%d" % g, [P, 512], U8) for g in range(G)]
+
+        def round_w1(g, copy, m0, m1):
+            copy(
+                out=w1_b[g][:, :, m0:m1, :].rearrange("p t m j -> p m j t"),
+                in_=w1_raw[g][:, :, PACK * m0 : PACK * m1].rearrange("p j (m t) -> p m j t", t=PACK),
+            )
+
+        def quantize_w1(g):
+            nc.vector.quantize_mx(
+                out=w1_w[g][:].bitcast(FP8X4), scales=w1_s[g][:],
+                in_=w1_b[g][:].rearrange("p t m j -> p (t m j)"),
+            )
+
+        round_w1(0, nc.scalar.copy, 0, P)
+        for g in range(G):
+            deal_w2(g)
+        for a in range(HALVES):
+            nc.vector.tensor_copy(v_s[a][:], tab_s[:].indirect(lists[a]))
+        quantize_w1(0)
+        nc.vector.tensor_copy(v_w[0][:], tab_w[:].indirect(lists[0]))
+        deal_w2_scales(0)
+        nc.vector.tensor_copy(v_w[1][:], tab_w[:].indirect(lists[1]))
+
+        h_full = [keep("h%d" % g, [P, PACK, S], F32) for g in range(G - 1)]
+        h_last = [keep("h_last%d" % a, [P, PACK, HALF], F32) for a in range(HALVES)]
+        h_w = [keep("h_w%d" % g, [P, S], U32) for g in range(G)]
+        h_s = keep("h_s", [P, G, S], U8)
+
+        def h_part(g, a):
+            return h_last[a][:] if g == G - 1 else h_full[g][:, :, HALF * a : HALF * (a + 1)]
+
+        woven = {}
+
+        def weave(g, a):
+            woven[g, a] = ring.tile([P, HALF, PACK], BF16, name="woven", align_bytes=64)
+            split = VECTOR_COLS[HALVES * g + a]
+            for copy, c0, c1 in ((nc.vector.tensor_copy, 0, split), (nc.scalar.copy, split, HALF)):
+                if c1 > c0:
+                    copy(
+                        out=woven[g, a][:, c0:c1, :].rearrange("p (c i) t -> p c t i", i=4),
+                        in_=h_part(g, a)[:, :, c0:c1].rearrange("p t (c i) -> p c t i", i=4),
+                    )
+
+        def quantize_h(g, a):
+            cols = slice(HALF * a, HALF * (a + 1))
+            nc.vector.quantize_mx(
+                out=h_w[g][:, cols].bitcast(FP8X4), scales=h_s[:, g, cols],
+                in_=woven[g, a][:].rearrange("p c t -> p (c t)"),
+            )
+            if a == HALVES - 1:
+                nc.sync.dma_start(
+                    out=out_2[g].rearrange("p m t -> p (m t)").bitcast(I32), in_=h_w[g][:].bitcast(I32)
+                )
+
+        def h_rows(g):
+            return out_1[512 * g : 512 * (g + 1), :].rearrange("(p t) j -> p t j", t=PACK)
+
+        def store_full(g):
+            nc.sync.dma_start(out=h_rows(g), in_=h_full[g][:])
+
+        def store_last(a):
+            nc.sync.dma_start(out=h_rows(G - 1)[:, :, HALF * a : HALF * (a + 1)], in_=h_last[a][:])
+
+        steps = [(g, a, t) for g in range(G - 1) for t in range(PACK) for a in range(HALVES)]
+        steps = steps + [(G - 1, a, t) for a in range(HALVES) for t in range(PACK)]
+        cast = lambda g, i: round_w1(g, nc.scalar.copy, 64 * i, 64 * (i + 1))
+        extras = {
+            1: [(cast, 1, 0)], 2: [(cast, 1, 1)], 3: [(deal_w2_scales, 1)], 4: [(quantize_w1, 1), (cast, 2, 0)],
+            6: [(cast, 2, 1)], 7: [(store_full, 0)],
+            8: [(weave, 0, 0)], 9: [(quantize_w1, 2), (deal_w2_scales, 2)], 10: [(quantize_h, 0, 0)],
+            11: [(weave, 0, 1)], 13: [(quantize_h, 0, 1)], 15: [(store_full, 1)],
+            16: [(weave, 1, 0)], 17: [(weave, 1, 1)], 18: [(quantize_h, 1, 0)], 19: [(store_last, 0)],
+            20: [(quantize_h, 1, 1), (weave, 2, 0)], 22: [(quantize_h, 2, 0)],
+            23: [(store_last, 1), (weave, 2, 1), (quantize_h, 2, 1)],
+        }
+        for step, (g, a, t) in enumerate(steps):
+            hit = bank(step % 3)
+            nc.tensor.matmul_mx(
+                out=hit[:], lhsT=w2_w[g][:, 256 * t : 256 * (t + 1)].bitcast(FP4X4),
+                lhsT_scale=w2_s[g][:, P * t : P * (t + 1)],
+                rhs=v_w[a][:].bitcast(FP8X4), rhs_scale=v_s[a][:], start=True, stop=True,
+            )
+            loss = bank(3 + step % 3)
+            nc.tensor.matmul_mx(
+                out=loss[:], lhsT=w1_w[g][:, P * t : P * (t + 1)].bitcast(FP8X4),
+                lhsT_scale=w1_s[g][:, P * t : P * (t + 1)],
+                rhs=v_w[a][:].bitcast(FP8X4), rhs_scale=v_s[a][:], start=True, stop=True,
+            )
+            gate = gates.tile([P, HALF], F32, name="gate")
+            nc.scalar.activation(out=gate[:], in_=hit[:], func=SIGMOID, bias=att_sb[:, g, t : t + 1])
+            nc.vector.scalar_tensor_tensor(
+                out=h_part(g, a)[:, t, :], in0=loss[:], scalar=load_sb[:, g, t : t + 1], in1=gate[:],
+                op0=ADD, op1=MULT,
+            )
+            for work in extras.get(step, []):
+                work[0](*work[1:])
+        for q in range(4):
+            nc.sync.dma_start(
+                out=out_3[:, 4 * q : 4 * q + 4, :].rearrange("g r m -> r g m").bitcast(I32),
+                in_=h_s[32 * q : 32 * q + 4].bitcast(I32),
+            )
+
+        y_banks = (6, 7, 6, 7, 0, 1, 2, 3, 4, 5, 6, 7)
+        for a in range(HALVES):
+            cols = slice(HALF * a, HALF * (a + 1))
+            for c in range(LINES):
+                acc = bank(y_banks[LINES * a + c])
+                for g in range(G):
+                    nc.tensor.matmul_mx(
+                        out=acc[:], lhsT=w3_w[:, g, P * c : P * (c + 1)].bitcast(FP8X4),
+                        lhsT_scale=w3_s[:, g, P * c : P * (c + 1)],
+                        rhs=h_w[g][:, cols].bitcast(FP8X4), rhs_scale=h_s[:, g, cols],
+                        start=(g == 0), stop=(g == G - 1),
+                    )
+                y_rows = y_sb[c // 3][:, c % 3, :]
+                nc.vector.tensor_tensor(out=y_rows[:, cols], in0=acc[:], in1=y_rows[:, cols], op=ADD)
+                if a == HALVES - 1:
+                    nc.sync.dma_start(out=out_0[P * c : P * (c + 1), :], in_=y_rows)

@@ -23,7 +23,7 @@ G = H // (P * PACK)
 HALF = 512
 HALVES = S // HALF
 LINES = N // P
-VECTOR_COLS = (304, 304, 304, 304, 192, 0)
+VECTOR_COLS = (176, 176, 176, 176, 128, 0)
 
 
 def tile_list_treaty_pricing_kernel(
@@ -34,7 +34,7 @@ def tile_list_treaty_pricing_kernel(
     with ExitStack() as ctx:
         held = ctx.enter_context(tc.tile_pool(name="held", bufs=1))
         ring = ctx.enter_context(tc.tile_pool(name="ring", bufs=3))
-        gates = ctx.enter_context(tc.tile_pool(name="gates", bufs=8))
+        gates = ctx.enter_context(tc.tile_pool(name="gates", bufs=10))
         psum = ctx.enter_context(tc.psum_pool(name="psum", bufs=1))
 
         def keep(name, shape, dtype):
@@ -43,16 +43,17 @@ def tile_list_treaty_pricing_kernel(
         def bank(b):
             return psum.tile([P, HALF], F32, name="bank%d" % b)
 
-        def load_scale_rows(queue, plane, rows):
+        def load_scale_rows(queue, plane, rows, first=0):
             for q in range(4):
-                queue.dma_start(out=plane[32 * q : 32 * q + 4], in_=rows(q))
+                queue.dma_start(out=plane[32 * q + first : 32 * q + first + 4], in_=rows(q))
 
         offsets = held.tile([P, S // 16], U16, name="offsets")
         nc.sync.dma_start(offsets[:], offs)
 
         w1_rows = w1.rearrange("(p j) c -> p j c", j=PACK)
-        w1_raw = [keep("w1_raw%d" % g, [P, PACK, 512], F32) for g in range(G)]
-        nc.sync.dma_start(out=w1_raw[0][:], in_=w1_rows[:, :, 0:512])
+        w1_head = [keep("w1_head%d" % u, [P, PACK, 256], F32) for u in range(2)]
+        w1_raw = [None] + [keep("w1_raw%d" % g, [P, PACK, 512], F32) for g in range(1, G)]
+        nc.sync.dma_start(out=w1_head[0][:], in_=w1_rows[:, :, 0:256])
         w2_raw = keep("w2_raw", [P, 2 * H], U8)
         nc.sync.dma_start(out=w2_raw[:].bitcast(I32), in_=w2_words[0].bitcast(I32))
         tab_s = keep("tab_s", [P, T], U8)
@@ -64,9 +65,10 @@ def tile_list_treaty_pricing_kernel(
         nc.vector.memset(w2s_raw[:].bitcast(I32), 0)
         load_scale_rows(nc.sync, w2s_raw[:].bitcast(I32), lambda q: w2_scales[0, 4 * q : 4 * q + 4, :].bitcast(I32))
         att_sb = keep("att_sb", [P, G, 8], F32)
-        nc.scalar.dma_start(out=att_sb[:, :, 0:PACK], in_=att.rearrange("(g p t) -> p g t", p=P, t=PACK))
+        nc.sync.dma_start(out=att_sb[:, :, 0:PACK], in_=att.rearrange("(g p t) -> p g t", p=P, t=PACK))
+        nc.sync.dma_start(out=w1_head[1][:], in_=w1_rows[:, :, 256:512])
         load_sb = keep("load_sb", [P, G, 8], F32)
-        nc.scalar.dma_start(out=load_sb[:, :, 0:PACK], in_=load.rearrange("(g p t) -> p g t", p=P, t=PACK))
+        nc.sync.dma_start(out=load_sb[:, :, 0:PACK], in_=load.rearrange("(g p t) -> p g t", p=P, t=PACK))
         for g in range(1, G):
             nc.sync.dma_start(out=w1_raw[g][:], in_=w1_rows[:, :, 512 * g : 512 * (g + 1)])
         w3_w = keep("w3_w", [P, G, N], U32)
@@ -74,7 +76,7 @@ def tile_list_treaty_pricing_kernel(
         nc.vector.memset(w3_s[:].bitcast(I32), 0)
         load_scale_rows(
             nc.sync, w3_s[:].bitcast(I32),
-            lambda q: w3_scales[:, 4 * q : 4 * q + 4, :].rearrange("g r n -> r g n").bitcast(I32),
+            lambda q: w3_scales[:, 4 * q : 4 * q + 4, :].rearrange("g r n -> r g n").bitcast(I32), 8,
         )
         nc.sync.dma_start(out=w3_w[:].bitcast(I32), in_=w3_words.rearrange("g p n t -> p g (n t)").bitcast(I32))
         prem_rows = prem.rearrange("(c p) j -> p c j", p=P)
@@ -111,8 +113,8 @@ def tile_list_treaty_pricing_kernel(
 
         def round_w1(g, copy, m0, m1):
             copy(
-                out=w1_b[g][:, :, m0:m1, :].rearrange("p t m j -> p m j t"),
-                in_=w1_raw[g][:, :, PACK * m0 : PACK * m1].rearrange("p j (m t) -> p m j t", t=PACK),
+                out=w1_b[g][:, :, m0:m1, :].rearrange("p t m j -> p m t j"),
+                in_=w1_raw[g][:, :, PACK * m0 : PACK * m1].rearrange("p j (m t) -> p m t j", t=PACK),
             )
 
         def quantize_w1(g):
@@ -121,15 +123,31 @@ def tile_list_treaty_pricing_kernel(
                 in_=w1_b[g][:].rearrange("p t m j -> p (t m j)"),
             )
 
-        round_w1(0, nc.scalar.copy, 0, P)
+        def round_w1_head(u):
+            nc.scalar.copy(
+                out=w1_b[0][:, :, 64 * u : 64 * (u + 1), :].rearrange("p t m j -> p m j t"),
+                in_=w1_head[u][:].rearrange("p j (m t) -> p m j t", t=PACK),
+            )
+
+        round_w1_head(0)
+        round_w1_head(1)
         for g in range(G):
             deal_w2(g)
         for a in range(HALVES):
             nc.vector.tensor_copy(v_s[a][:], tab_s[:].indirect(lists[a]))
-        quantize_w1(0)
         nc.vector.tensor_copy(v_w[0][:], tab_w[:].indirect(lists[0]))
         deal_w2_scales(0)
         nc.vector.tensor_copy(v_w[1][:], tab_w[:].indirect(lists[1]))
+        quantize_w1(0)
+        for g in range(1, G):
+            deal_w2_scales(g)
+
+        def gpsimd_copy(out, in_):
+            nc.gpsimd.tensor_scalar(out=out, in0=in_, scalar1=1.0, scalar2=0.0, op0=MULT, op1=ADD)
+
+        for g in range(1, G):
+            for i in range(4):
+                round_w1(g, gpsimd_copy, 32 * i, 32 * (i + 1))
 
         h_full = [keep("h%d" % g, [P, PACK, S], F32) for g in range(G - 1)]
         h_last = [keep("h_last%d" % a, [P, PACK, HALF], F32) for a in range(HALVES)]
@@ -154,7 +172,7 @@ def tile_list_treaty_pricing_kernel(
         def quantize_h(g, a):
             cols = slice(HALF * a, HALF * (a + 1))
             nc.vector.quantize_mx(
-                out=h_w[g][:, cols].bitcast(FP8X4), scales=h_s[:, g, cols],
+                out=h_w[g][:, cols].bitcast(FP8X4), scales=h_s[4:P, g, cols],
                 in_=woven[g, a][:].rearrange("p c t -> p (c t)"),
             )
             if a == HALVES - 1:
@@ -175,9 +193,8 @@ def tile_list_treaty_pricing_kernel(
         steps = steps + [(G - 1, a, t) for a in range(HALVES) for t in range(PACK)]
         cast = lambda g, i: round_w1(g, nc.scalar.copy, 64 * i, 64 * (i + 1))
         extras = {
-            1: [(cast, 1, 0)], 2: [(cast, 1, 1)], 3: [(deal_w2_scales, 1)], 4: [(quantize_w1, 1), (cast, 2, 0)],
-            6: [(cast, 2, 1)], 7: [(store_full, 0)],
-            8: [(weave, 0, 0)], 9: [(quantize_w1, 2), (deal_w2_scales, 2)], 10: [(quantize_h, 0, 0)],
+            4: [(quantize_w1, 1)], 7: [(store_full, 0)],
+            8: [(weave, 0, 0)], 9: [(quantize_w1, 2)], 10: [(quantize_h, 0, 0)],
             11: [(weave, 0, 1)], 13: [(quantize_h, 0, 1)], 15: [(store_full, 1)],
             16: [(weave, 1, 0)], 17: [(weave, 1, 1)], 18: [(quantize_h, 1, 0)], 19: [(store_last, 0)],
             20: [(quantize_h, 1, 1), (weave, 2, 0)], 22: [(quantize_h, 2, 0)],
@@ -204,25 +221,24 @@ def tile_list_treaty_pricing_kernel(
             )
             for work in extras.get(step, []):
                 work[0](*work[1:])
-        for q in range(4):
-            nc.sync.dma_start(
-                out=out_3[:, 4 * q : 4 * q + 4, :].rearrange("g r m -> r g m").bitcast(I32),
-                in_=h_s[32 * q : 32 * q + 4].bitcast(I32),
-            )
-
         y_banks = (6, 7, 6, 7, 0, 1, 2, 3, 4, 5, 6, 7)
         for a in range(HALVES):
             cols = slice(HALF * a, HALF * (a + 1))
+            if a == HALVES - 1:
+                for q in range(4):
+                    nc.sync.dma_start(
+                        out=out_3[:, 4 * q : 4 * q + 4, :].rearrange("g r m -> r g m").bitcast(I32),
+                        in_=h_s[32 * q + 4 : 32 * q + 8].bitcast(I32),
+                    )
             for c in range(LINES):
                 acc = bank(y_banks[LINES * a + c])
                 for g in range(G):
                     nc.tensor.matmul_mx(
                         out=acc[:], lhsT=w3_w[:, g, P * c : P * (c + 1)].bitcast(FP8X4),
-                        lhsT_scale=w3_s[:, g, P * c : P * (c + 1)],
-                        rhs=h_w[g][:, cols].bitcast(FP8X4), rhs_scale=h_s[:, g, cols],
+                        lhsT_scale=w3_s[8:P, g, P * c : P * (c + 1)],
+                        rhs=h_w[g][:, cols].bitcast(FP8X4), rhs_scale=h_s[4:P, g, cols],
                         start=(g == 0), stop=(g == G - 1),
                     )
                 y_rows = y_sb[c // 3][:, c % 3, :]
                 nc.vector.tensor_tensor(out=y_rows[:, cols], in0=acc[:], in1=y_rows[:, cols], op=ADD)
-                if a == HALVES - 1:
-                    nc.sync.dma_start(out=out_0[P * c : P * (c + 1), :], in_=y_rows)
+                nc.sync.dma_start(out=out_0[P * c : P * (c + 1), cols], in_=y_rows[:, cols])

@@ -23,7 +23,7 @@ G = H // (P * PACK)
 HALF = 512
 HALVES = S // HALF
 LINES = N // P
-VECTOR_COLS = (176, 176, 176, 176, 128, 0)
+VECTOR_COLS = (144, 144, 144, 144, 128, 160)
 
 
 def tile_list_treaty_pricing_kernel(
@@ -45,7 +45,7 @@ def tile_list_treaty_pricing_kernel(
 
         def load_scale_rows(queue, plane, rows, first=0):
             for q in range(4):
-                queue.dma_start(out=plane[32 * q + first : 32 * q + first + 4], in_=rows(q))
+                queue.dma_start(out=plane[first + q : P : 32], in_=rows(q))
 
         offsets = held.tile([P, S // 16], U16, name="offsets")
         nc.sync.dma_start(offsets[:], offs)
@@ -58,12 +58,12 @@ def tile_list_treaty_pricing_kernel(
         nc.sync.dma_start(out=w2_raw[:].bitcast(I32), in_=w2_words[0].bitcast(I32))
         tab_s = keep("tab_s", [P, T], U8)
         nc.vector.memset(tab_s[:].bitcast(I32), 0)
-        load_scale_rows(nc.sync, tab_s[:].bitcast(I32), lambda q: tab_scales[0, 4 * q : 4 * q + 4, :].bitcast(I32))
+        load_scale_rows(nc.sync, tab_s[:].bitcast(I32), lambda q: tab_scales[0, q:16:4, :].bitcast(I32))
         tab_w = keep("tab_w", [P, T], U32)
         nc.sync.dma_start(out=tab_w[:].bitcast(I32), in_=tab_words[0].rearrange("p n t -> p (n t)").bitcast(I32))
         w2s_raw = keep("w2s_raw", [P, H], U8)
         nc.vector.memset(w2s_raw[:].bitcast(I32), 0)
-        load_scale_rows(nc.sync, w2s_raw[:].bitcast(I32), lambda q: w2_scales[0, 4 * q : 4 * q + 4, :].bitcast(I32))
+        load_scale_rows(nc.sync, w2s_raw[:].bitcast(I32), lambda q: w2_scales[0, q:16:4, :].bitcast(I32))
         att_sb = keep("att_sb", [P, G, 8], F32)
         nc.sync.dma_start(out=att_sb[:, :, 0:PACK], in_=att.rearrange("(g p t) -> p g t", p=P, t=PACK))
         nc.sync.dma_start(out=w1_head[1][:], in_=w1_rows[:, :, 256:512])
@@ -76,18 +76,13 @@ def tile_list_treaty_pricing_kernel(
         nc.vector.memset(w3_s[:].bitcast(I32), 0)
         load_scale_rows(
             nc.sync, w3_s[:].bitcast(I32),
-            lambda q: w3_scales[:, 4 * q : 4 * q + 4, :].rearrange("g r n -> r g n").bitcast(I32), 8,
+            lambda q: w3_scales[:, q:16:4, :].rearrange("g r n -> r g n").bitcast(I32), 8,
         )
         nc.sync.dma_start(out=w3_w[:].bitcast(I32), in_=w3_words.rearrange("g p n t -> p g (n t)").bitcast(I32))
         prem_rows = prem.rearrange("(c p) j -> p c j", p=P)
         y_sb = [keep("y%d" % i, [P, LINES // 2, S], F32) for i in range(2)]
         for i in range(2):
             nc.sync.dma_start(out=y_sb[i][:], in_=prem_rows[:, 3 * i : 3 * i + 3, :])
-
-        warm = keep("warm", [P, 8], F32)
-        nc.vector.memset(warm[:], 0.0)
-        warm_out = keep("warm_out", [P, 8], F32)
-        nc.scalar.activation(out=warm_out[:], in_=warm[:], func=SIGMOID)
 
         w2_w = [keep("w2_w%d" % g, [P, 2 * 512], U8) for g in range(G)]
         w2_s = [keep("w2_s%d" % g, [P, 512], U8) for g in range(G)]
@@ -124,13 +119,12 @@ def tile_list_treaty_pricing_kernel(
             )
 
         def round_w1_head(u):
-            nc.scalar.copy(
+            nc.vector.tensor_copy(
                 out=w1_b[0][:, :, 64 * u : 64 * (u + 1), :].rearrange("p t m j -> p m j t"),
                 in_=w1_head[u][:].rearrange("p j (m t) -> p m j t", t=PACK),
             )
 
         round_w1_head(0)
-        round_w1_head(1)
         for g in range(G):
             deal_w2(g)
         for a in range(HALVES):
@@ -138,6 +132,7 @@ def tile_list_treaty_pricing_kernel(
         nc.vector.tensor_copy(v_w[0][:], tab_w[:].indirect(lists[0]))
         deal_w2_scales(0)
         nc.vector.tensor_copy(v_w[1][:], tab_w[:].indirect(lists[1]))
+        round_w1_head(1)
         quantize_w1(0)
         for g in range(1, G):
             deal_w2_scales(g)
@@ -227,8 +222,8 @@ def tile_list_treaty_pricing_kernel(
             if a == HALVES - 1:
                 for q in range(4):
                     nc.sync.dma_start(
-                        out=out_3[:, 4 * q : 4 * q + 4, :].rearrange("g r m -> r g m").bitcast(I32),
-                        in_=h_s[32 * q + 4 : 32 * q + 8].bitcast(I32),
+                        out=out_3[:, q:16:4, :].rearrange("g r m -> r g m").bitcast(I32),
+                        in_=h_s[4 + q : P : 32].bitcast(I32),
                     )
             for c in range(LINES):
                 acc = bank(y_banks[LINES * a + c])
@@ -241,4 +236,5 @@ def tile_list_treaty_pricing_kernel(
                     )
                 y_rows = y_sb[c // 3][:, c % 3, :]
                 nc.vector.tensor_tensor(out=y_rows[:, cols], in0=acc[:], in1=y_rows[:, cols], op=ADD)
-                nc.sync.dma_start(out=out_0[P * c : P * (c + 1), cols], in_=y_rows[:, cols])
+                if a == HALVES - 1:
+                    nc.sync.dma_start(out=out_0[P * c : P * (c + 1), :], in_=y_rows)

@@ -19,11 +19,24 @@ SIGMOID = mybir.ActivationFunctionType.Sigmoid
 
 P = 128
 PACK = 4
-G = H // (P * PACK)
+GROUP = P * PACK
+G = H // GROUP
+LAST = G - 1
 HALF = 512
 HALVES = S // HALF
 LINES = N // P
-VECTOR_COLS = (144, 144, 144, 144, 128, 160)
+QUAD = 32
+BLOCKS = 16
+SPREAD = P // BLOCKS
+BIAS_PITCH = 8
+H_FIRST, W3_FIRST = 4, 8
+VECTOR_COLS = {(0, 0): 208, (0, 1): 208, (1, 0): 208, (1, 1): 208, (2, 0): 192, (2, 1): 160}
+GPSIMD_PIECES = 4
+RING = 3
+GATE_BUFS = 10
+WOVEN_BUFS = 3
+QUANTIZE_LAG = 2
+Y_LAG = 3
 
 
 def tile_list_treaty_pricing_kernel(
@@ -33,83 +46,85 @@ def tile_list_treaty_pricing_kernel(
     nc = tc.nc
     with ExitStack() as ctx:
         held = ctx.enter_context(tc.tile_pool(name="held", bufs=1))
-        ring = ctx.enter_context(tc.tile_pool(name="ring", bufs=3))
-        gates = ctx.enter_context(tc.tile_pool(name="gates", bufs=10))
+        woven_pool = ctx.enter_context(tc.tile_pool(name="woven", bufs=WOVEN_BUFS))
+        gate_pool = ctx.enter_context(tc.tile_pool(name="gates", bufs=GATE_BUFS))
         psum = ctx.enter_context(tc.psum_pool(name="psum", bufs=1))
 
         def keep(name, shape, dtype):
             return held.tile(shape, dtype, name=name, align_bytes=64)
 
+        def zeroed_plane(name, shape):
+            plane = keep(name, shape, U8)
+            nc.vector.memset(plane[:].bitcast(I32), 0)
+            return plane
+
         def bank(b):
             return psum.tile([P, HALF], F32, name="bank%d" % b)
 
-        def load_scale_rows(queue, plane, rows, first=0):
-            for q in range(4):
-                queue.dma_start(out=plane[first + q : P : 32], in_=rows(q))
+        def half_cols(a):
+            return slice(HALF * a, HALF * (a + 1))
+
+        def live_rows(plane, first, r):
+            return plane[first + r : P : QUAD].bitcast(I32)
 
         offsets = held.tile([P, S // 16], U16, name="offsets")
         nc.sync.dma_start(offsets[:], offs)
 
         w1_rows = w1.rearrange("(p j) c -> p j c", j=PACK)
-        w1_head = [keep("w1_head%d" % u, [P, PACK, 256], F32) for u in range(2)]
-        w1_raw = [None] + [keep("w1_raw%d" % g, [P, PACK, 512], F32) for g in range(1, G)]
-        nc.sync.dma_start(out=w1_head[0][:], in_=w1_rows[:, :, 0:256])
+        w1_head = [keep("w1_head%d" % u, [P, PACK, GROUP // 2], F32) for u in range(2)]
+        w1_raw = {g: keep("w1_raw%d" % g, [P, PACK, GROUP], F32) for g in range(1, G)}
+        nc.sync.dma_start(out=w1_head[0][:], in_=w1_rows[:, :, 0 : GROUP // 2])
+        tab_s = zeroed_plane("tab_s", [P, T])
+        nc.sync.dma_start(out=tab_s[0:P:SPREAD].bitcast(I32), in_=tab_scales[0].bitcast(I32))
         w2_raw = keep("w2_raw", [P, 2 * H], U8)
         nc.sync.dma_start(out=w2_raw[:].bitcast(I32), in_=w2_words[0].bitcast(I32))
-        tab_s = keep("tab_s", [P, T], U8)
-        nc.vector.memset(tab_s[:].bitcast(I32), 0)
-        load_scale_rows(nc.sync, tab_s[:].bitcast(I32), lambda q: tab_scales[0, q:16:4, :].bitcast(I32))
+        w2s_raw = zeroed_plane("w2s_raw", [P, H])
+        for r in range(PACK):
+            nc.sync.dma_start(out=live_rows(w2s_raw, 0, r), in_=w2_scales[0, r:BLOCKS:PACK, :].bitcast(I32))
         tab_w = keep("tab_w", [P, T], U32)
         nc.sync.dma_start(out=tab_w[:].bitcast(I32), in_=tab_words[0].rearrange("p n t -> p (n t)").bitcast(I32))
-        w2s_raw = keep("w2s_raw", [P, H], U8)
-        nc.vector.memset(w2s_raw[:].bitcast(I32), 0)
-        load_scale_rows(nc.sync, w2s_raw[:].bitcast(I32), lambda q: w2_scales[0, q:16:4, :].bitcast(I32))
-        att_sb = keep("att_sb", [P, G, 8], F32)
+        att_sb = keep("att_sb", [P, G, BIAS_PITCH], F32)
         nc.sync.dma_start(out=att_sb[:, :, 0:PACK], in_=att.rearrange("(g p t) -> p g t", p=P, t=PACK))
-        nc.sync.dma_start(out=w1_head[1][:], in_=w1_rows[:, :, 256:512])
-        load_sb = keep("load_sb", [P, G, 8], F32)
+        picked_s = keep("picked_s", [P, S], U8)
+        v_s = zeroed_plane("v_s", [P, S])
+        nc.vector.tensor_copy(picked_s[:], tab_s[:].indirect(offsets[:]))
+        for r in range(PACK):
+            nc.sync.dma_start(out=live_rows(v_s, 0, r), in_=live_rows(picked_s, 0, SPREAD * r))
+        nc.sync.dma_start(out=w1_head[1][:], in_=w1_rows[:, :, GROUP // 2 : GROUP])
+        load_sb = keep("load_sb", [P, G, BIAS_PITCH], F32)
         nc.sync.dma_start(out=load_sb[:, :, 0:PACK], in_=load.rearrange("(g p t) -> p g t", p=P, t=PACK))
         for g in range(1, G):
-            nc.sync.dma_start(out=w1_raw[g][:], in_=w1_rows[:, :, 512 * g : 512 * (g + 1)])
+            nc.sync.dma_start(out=w1_raw[g][:], in_=w1_rows[:, :, GROUP * g : GROUP * (g + 1)])
         w3_w = keep("w3_w", [P, G, N], U32)
-        w3_s = keep("w3_s", [P, G, N], U8)
-        nc.vector.memset(w3_s[:].bitcast(I32), 0)
-        load_scale_rows(
-            nc.sync, w3_s[:].bitcast(I32),
-            lambda q: w3_scales[:, q:16:4, :].rearrange("g r n -> r g n").bitcast(I32), 8,
-        )
+        w3_s = zeroed_plane("w3_s", [P, G, N])
+        for r in range(PACK):
+            nc.sync.dma_start(
+                out=live_rows(w3_s, W3_FIRST, r),
+                in_=w3_scales[:, r:BLOCKS:PACK, :].rearrange("g q n -> q g n").bitcast(I32),
+            )
         nc.sync.dma_start(out=w3_w[:].bitcast(I32), in_=w3_words.rearrange("g p n t -> p g (n t)").bitcast(I32))
         prem_rows = prem.rearrange("(c p) j -> p c j", p=P)
-        y_sb = [keep("y%d" % i, [P, LINES // 2, S], F32) for i in range(2)]
+        per_load = LINES // 2
+        y_sb = [keep("y%d" % i, [P, per_load, S], F32) for i in range(2)]
         for i in range(2):
-            nc.sync.dma_start(out=y_sb[i][:], in_=prem_rows[:, 3 * i : 3 * i + 3, :])
+            nc.sync.dma_start(out=y_sb[i][:], in_=prem_rows[:, per_load * i : per_load * (i + 1), :])
 
-        w2_w = [keep("w2_w%d" % g, [P, 2 * 512], U8) for g in range(G)]
-        w2_s = [keep("w2_s%d" % g, [P, 512], U8) for g in range(G)]
-
-        def deal_w2(g):
-            nc.vector.tensor_copy(
-                out=w2_w[g][:].bitcast(U16).rearrange("p (t m) -> p t m", t=PACK),
-                in_=w2_raw[:, 1024 * g : 1024 * (g + 1)].bitcast(U16).rearrange("p (m t) -> p t m", t=PACK),
-            )
-
-        def deal_w2_scales(g):
-            nc.vector.tensor_copy(
-                out=w2_s[g][:].rearrange("p (t m) -> p t m", t=PACK),
-                in_=w2s_raw[:, 512 * g : 512 * (g + 1)].rearrange("p (m t) -> p t m", t=PACK),
-            )
-
+        w2_w = [keep("w2_w%d" % g, [P, 2 * GROUP], U8) for g in range(G)]
+        w2_s = [keep("w2_s%d" % g, [P, GROUP], U8) for g in range(G)]
         v_w = [keep("v_w%d" % a, [P, HALF], U32) for a in range(HALVES)]
-        v_s = [keep("v_s%d" % a, [P, HALF], U8) for a in range(HALVES)]
-        lists = [offsets[:, 32 * a : 32 * (a + 1)] for a in range(HALVES)]
         w1_b = [keep("w1_b%d" % g, [P, PACK, P, PACK], BF16) for g in range(G)]
-        w1_w = [keep("w1_w%d" % g, [P, 512], U32) for g in range(G)]
-        w1_s = [keep("w1_s%d" % g, [P, 512], U8) for g in range(G)]
+        w1_w = [keep("w1_w%d" % g, [P, GROUP], U32) for g in range(G)]
+        w1_s = [keep("w1_s%d" % g, [P, GROUP], U8) for g in range(G)]
 
-        def round_w1(g, copy, m0, m1):
-            copy(
-                out=w1_b[g][:, :, m0:m1, :].rearrange("p t m j -> p m t j"),
-                in_=w1_raw[g][:, :, PACK * m0 : PACK * m1].rearrange("p j (m t) -> p m t j", t=PACK),
+        def deal(out, in_):
+            nc.vector.tensor_copy(
+                out=out.rearrange("p (t m) -> p t m", t=PACK), in_=in_.rearrange("p (m t) -> p t m", t=PACK)
+            )
+
+        def round_w1_head(u):
+            nc.vector.tensor_copy(
+                out=w1_b[0][:, :, P // 2 * u : P // 2 * (u + 1), :].rearrange("p t m j -> p m j t"),
+                in_=w1_head[u][:].rearrange("p j (m t) -> p m j t", t=PACK),
             )
 
         def quantize_w1(g):
@@ -118,123 +133,120 @@ def tile_list_treaty_pricing_kernel(
                 in_=w1_b[g][:].rearrange("p t m j -> p (t m j)"),
             )
 
-        def round_w1_head(u):
-            nc.vector.tensor_copy(
-                out=w1_b[0][:, :, 64 * u : 64 * (u + 1), :].rearrange("p t m j -> p m j t"),
-                in_=w1_head[u][:].rearrange("p j (m t) -> p m j t", t=PACK),
-            )
-
         round_w1_head(0)
         for g in range(G):
-            deal_w2(g)
+            deal(w2_w[g][:].bitcast(U16), w2_raw[:, 2 * GROUP * g : 2 * GROUP * (g + 1)].bitcast(U16))
+            deal(w2_s[g][:], w2s_raw[:, GROUP * g : GROUP * (g + 1)])
         for a in range(HALVES):
-            nc.vector.tensor_copy(v_s[a][:], tab_s[:].indirect(lists[a]))
-        nc.vector.tensor_copy(v_w[0][:], tab_w[:].indirect(lists[0]))
-        deal_w2_scales(0)
-        nc.vector.tensor_copy(v_w[1][:], tab_w[:].indirect(lists[1]))
+            nc.vector.tensor_copy(v_w[a][:], tab_w[:].indirect(offsets[:, HALF // 16 * a : HALF // 16 * (a + 1)]))
         round_w1_head(1)
         quantize_w1(0)
+        piece = P // GPSIMD_PIECES
         for g in range(1, G):
-            deal_w2_scales(g)
-
-        def gpsimd_copy(out, in_):
-            nc.gpsimd.tensor_scalar(out=out, in0=in_, scalar1=1.0, scalar2=0.0, op0=MULT, op1=ADD)
-
-        for g in range(1, G):
-            for i in range(4):
-                round_w1(g, gpsimd_copy, 32 * i, 32 * (i + 1))
-
-        h_full = [keep("h%d" % g, [P, PACK, S], F32) for g in range(G - 1)]
-        h_last = [keep("h_last%d" % a, [P, PACK, HALF], F32) for a in range(HALVES)]
-        h_w = [keep("h_w%d" % g, [P, S], U32) for g in range(G)]
-        h_s = keep("h_s", [P, G, S], U8)
-
-        def h_part(g, a):
-            return h_last[a][:] if g == G - 1 else h_full[g][:, :, HALF * a : HALF * (a + 1)]
-
-        woven = {}
-
-        def weave(g, a):
-            woven[g, a] = ring.tile([P, HALF, PACK], BF16, name="woven", align_bytes=64)
-            split = VECTOR_COLS[HALVES * g + a]
-            for copy, c0, c1 in ((nc.vector.tensor_copy, 0, split), (nc.scalar.copy, split, HALF)):
-                if c1 > c0:
-                    copy(
-                        out=woven[g, a][:, c0:c1, :].rearrange("p (c i) t -> p c t i", i=4),
-                        in_=h_part(g, a)[:, :, c0:c1].rearrange("p t (c i) -> p c t i", i=4),
-                    )
-
-        def quantize_h(g, a):
-            cols = slice(HALF * a, HALF * (a + 1))
-            nc.vector.quantize_mx(
-                out=h_w[g][:, cols].bitcast(FP8X4), scales=h_s[4:P, g, cols],
-                in_=woven[g, a][:].rearrange("p c t -> p (c t)"),
-            )
-            if a == HALVES - 1:
-                nc.sync.dma_start(
-                    out=out_2[g].rearrange("p m t -> p (m t)").bitcast(I32), in_=h_w[g][:].bitcast(I32)
+            for m0 in range(0, P, piece):
+                nc.gpsimd.tensor_scalar(
+                    out=w1_b[g][:, :, m0 : m0 + piece, :].rearrange("p t m j -> p m t j"),
+                    in0=w1_raw[g][:, :, PACK * m0 : PACK * (m0 + piece)].rearrange("p j (m t) -> p m t j", t=PACK),
+                    scalar1=1.0, scalar2=0.0, op0=MULT, op1=ADD,
                 )
 
-        def h_rows(g):
-            return out_1[512 * g : 512 * (g + 1), :].rearrange("(p t) j -> p t j", t=PACK)
+        h_full = [keep("h%d" % g, [P, PACK, S], F32) for g in range(LAST)]
+        h_last = [keep("h_last%d" % a, [P, PACK, HALF], F32) for a in range(HALVES)]
+        h_w = [keep("h_w%d" % g, [P, S], U32) for g in range(G)]
+        h_s_full = keep("h_s_full", [P, LAST, S], U8)
+        h_s_last = keep("h_s_last", [P, 1, S], U8)
+        woven = {}
 
-        def store_full(g):
-            nc.sync.dma_start(out=h_rows(g), in_=h_full[g][:])
+        def h_part(g, a):
+            return h_last[a][:] if g == LAST else h_full[g][:, :, half_cols(a)]
 
-        def store_last(a):
-            nc.sync.dma_start(out=h_rows(G - 1)[:, :, HALF * a : HALF * (a + 1)], in_=h_last[a][:])
+        def h_scales(g, a):
+            return h_s_last[H_FIRST:P, 0, half_cols(a)] if g == LAST else h_s_full[H_FIRST:P, g, half_cols(a)]
 
-        steps = [(g, a, t) for g in range(G - 1) for t in range(PACK) for a in range(HALVES)]
-        steps = steps + [(G - 1, a, t) for a in range(HALVES) for t in range(PACK)]
-        cast = lambda g, i: round_w1(g, nc.scalar.copy, 64 * i, 64 * (i + 1))
-        extras = {
-            4: [(quantize_w1, 1)], 7: [(store_full, 0)],
-            8: [(weave, 0, 0)], 9: [(quantize_w1, 2)], 10: [(quantize_h, 0, 0)],
-            11: [(weave, 0, 1)], 13: [(quantize_h, 0, 1)], 15: [(store_full, 1)],
-            16: [(weave, 1, 0)], 17: [(weave, 1, 1)], 18: [(quantize_h, 1, 0)], 19: [(store_last, 0)],
-            20: [(quantize_h, 1, 1), (weave, 2, 0)], 22: [(quantize_h, 2, 0)],
-            23: [(store_last, 1), (weave, 2, 1), (quantize_h, 2, 1)],
-        }
+        def store_h(g, a):
+            rows = out_1[GROUP * g : GROUP * (g + 1), :].rearrange("(p t) j -> p t j", t=PACK)
+            if g == LAST:
+                nc.sync.dma_start(out=rows[:, :, half_cols(a)], in_=h_last[a][:])
+            else:
+                nc.sync.dma_start(out=rows, in_=h_full[g][:])
+
+        def store_scales(plane, g0, g1):
+            for r in range(PACK):
+                nc.sync.dma_start(
+                    out=out_3[g0:g1, r:BLOCKS:PACK, :].rearrange("g q m -> q g m").bitcast(I32),
+                    in_=live_rows(plane, H_FIRST, r),
+                )
+
+        def weave(g, a):
+            woven[g, a] = woven_pool.tile([P, HALF, PACK], BF16, name="woven", align_bytes=64)
+            split = VECTOR_COLS[g, a]
+            for copy, c0, c1 in ((nc.vector.tensor_copy, 0, split), (nc.scalar.copy, split, HALF)):
+                copy(
+                    out=woven[g, a][:, c0:c1, :].rearrange("p (c i) t -> p c t i", i=4),
+                    in_=h_part(g, a)[:, :, c0:c1].rearrange("p t (c i) -> p c t i", i=4),
+                )
+
+        def quantize_h(g, a):
+            nc.vector.quantize_mx(
+                out=h_w[g][:, half_cols(a)].bitcast(FP8X4), scales=h_scales(g, a),
+                in_=woven[g, a][:].rearrange("p c t -> p (c t)"),
+            )
+            words = out_2[g].rearrange("p m t -> p (m t)").bitcast(I32)
+            if g == LAST:
+                nc.sync.dma_start(out=words[:, half_cols(a)], in_=h_w[g][:, half_cols(a)].bitcast(I32))
+            elif a == HALVES - 1:
+                nc.sync.dma_start(out=words, in_=h_w[g][:].bitcast(I32))
+            if (g, a) == (LAST - 1, HALVES - 1):
+                store_scales(h_s_full, 0, LAST)
+            if (g, a) == (LAST, HALVES - 1):
+                store_scales(h_s_last, LAST, G)
+
+        steps = [(g, a, t) for g in range(LAST) for t in range(PACK) for a in range(HALVES)]
+        steps = steps + [(LAST, a, t) for a in range(HALVES) for t in range(PACK)]
+        final = len(steps) - 1
+        weave_after = {8: (0, 0), 11: (0, 1), 16: (1, 0), 17: (1, 1), 20: (2, 0), final: (2, 1)}
+        quantize_h_after = {min(step + QUANTIZE_LAG, final): half for step, half in weave_after.items()}
+        quantize_w1_after = {4: 1, 9: 2}
         for step, (g, a, t) in enumerate(steps):
-            hit = bank(step % 3)
+            places = slice(P * t, P * (t + 1))
+            hit = bank(step % RING)
             nc.tensor.matmul_mx(
-                out=hit[:], lhsT=w2_w[g][:, 256 * t : 256 * (t + 1)].bitcast(FP4X4),
-                lhsT_scale=w2_s[g][:, P * t : P * (t + 1)],
-                rhs=v_w[a][:].bitcast(FP8X4), rhs_scale=v_s[a][:], start=True, stop=True,
+                out=hit[:], lhsT=w2_w[g][:, 2 * P * t : 2 * P * (t + 1)].bitcast(FP4X4), lhsT_scale=w2_s[g][:, places],
+                rhs=v_w[a][:].bitcast(FP8X4), rhs_scale=v_s[:, half_cols(a)], start=True, stop=True,
             )
-            loss = bank(3 + step % 3)
+            loss = bank(RING + step % RING)
             nc.tensor.matmul_mx(
-                out=loss[:], lhsT=w1_w[g][:, P * t : P * (t + 1)].bitcast(FP8X4),
-                lhsT_scale=w1_s[g][:, P * t : P * (t + 1)],
-                rhs=v_w[a][:].bitcast(FP8X4), rhs_scale=v_s[a][:], start=True, stop=True,
+                out=loss[:], lhsT=w1_w[g][:, places].bitcast(FP8X4), lhsT_scale=w1_s[g][:, places],
+                rhs=v_w[a][:].bitcast(FP8X4), rhs_scale=v_s[:, half_cols(a)], start=True, stop=True,
             )
-            gate = gates.tile([P, HALF], F32, name="gate")
+            gate = gate_pool.tile([P, HALF], F32, name="gate")
             nc.scalar.activation(out=gate[:], in_=hit[:], func=SIGMOID, bias=att_sb[:, g, t : t + 1])
             nc.vector.scalar_tensor_tensor(
                 out=h_part(g, a)[:, t, :], in0=loss[:], scalar=load_sb[:, g, t : t + 1], in1=gate[:],
                 op0=ADD, op1=MULT,
             )
-            for work in extras.get(step, []):
-                work[0](*work[1:])
-        y_banks = (6, 7, 6, 7, 0, 1, 2, 3, 4, 5, 6, 7)
-        for a in range(HALVES):
-            cols = slice(HALF * a, HALF * (a + 1))
+            if t == PACK - 1 and (g == LAST or a == HALVES - 1):
+                store_h(g, a)
+            if step in weave_after:
+                weave(*weave_after[step])
+            if step in quantize_h_after:
+                quantize_h(*quantize_h_after[step])
+            if step in quantize_w1_after:
+                quantize_w1(quantize_w1_after[step])
+
+        order = [(i - Y_LAG * a, a) for i in range(LINES + Y_LAG) for a in range(HALVES) if 0 <= i - Y_LAG * a < LINES]
+        spare = [2 * RING, 2 * RING + 1]
+        y_banks = spare + spare + list(range(8))
+        for (c, a), b in zip(order, y_banks):
+            lines = slice(P * c, P * (c + 1))
+            acc = bank(b)
+            for g in range(G):
+                nc.tensor.matmul_mx(
+                    out=acc[:], lhsT=w3_w[:, g, lines].bitcast(FP8X4), lhsT_scale=w3_s[W3_FIRST:P, g, lines],
+                    rhs=h_w[g][:, half_cols(a)].bitcast(FP8X4), rhs_scale=h_scales(g, a),
+                    start=(g == 0), stop=(g == LAST),
+                )
+            y_rows = y_sb[c // per_load][:, c % per_load, :]
+            nc.vector.tensor_tensor(out=y_rows[:, half_cols(a)], in0=acc[:], in1=y_rows[:, half_cols(a)], op=ADD)
             if a == HALVES - 1:
-                for q in range(4):
-                    nc.sync.dma_start(
-                        out=out_3[:, q:16:4, :].rearrange("g r m -> r g m").bitcast(I32),
-                        in_=h_s[4 + q : P : 32].bitcast(I32),
-                    )
-            for c in range(LINES):
-                acc = bank(y_banks[LINES * a + c])
-                for g in range(G):
-                    nc.tensor.matmul_mx(
-                        out=acc[:], lhsT=w3_w[:, g, P * c : P * (c + 1)].bitcast(FP8X4),
-                        lhsT_scale=w3_s[8:P, g, P * c : P * (c + 1)],
-                        rhs=h_w[g][:, cols].bitcast(FP8X4), rhs_scale=h_s[4:P, g, cols],
-                        start=(g == 0), stop=(g == G - 1),
-                    )
-                y_rows = y_sb[c // 3][:, c % 3, :]
-                nc.vector.tensor_tensor(out=y_rows[:, cols], in0=acc[:], in1=y_rows[:, cols], op=ADD)
-                if a == HALVES - 1:
-                    nc.sync.dma_start(out=out_0[P * c : P * (c + 1), :], in_=y_rows)
+                nc.sync.dma_start(out=out_0[lines, :], in_=y_rows)

@@ -30,13 +30,12 @@ BLOCKS = 16
 SPREAD = P // BLOCKS
 BIAS_PITCH = 8
 H_FIRST, W3_FIRST = 4, 8
-VECTOR_COLS = {(0, 0): 208, (0, 1): 208, (1, 0): 208, (1, 1): 208, (2, 0): 192, (2, 1): 160}
-GPSIMD_PIECES = 4
+VECTOR_COLS = (0, 320, 320)
+GPSIMD_PIECES = 8
 RING = 3
-GATE_BUFS = 10
-WOVEN_BUFS = 3
+BANKS = 8
 QUANTIZE_LAG = 2
-Y_LAG = 3
+GATE_BUFS = 10
 
 
 def tile_list_treaty_pricing_kernel(
@@ -46,7 +45,6 @@ def tile_list_treaty_pricing_kernel(
     nc = tc.nc
     with ExitStack() as ctx:
         held = ctx.enter_context(tc.tile_pool(name="held", bufs=1))
-        woven_pool = ctx.enter_context(tc.tile_pool(name="woven", bufs=WOVEN_BUFS))
         gate_pool = ctx.enter_context(tc.tile_pool(name="gates", bufs=GATE_BUFS))
         psum = ctx.enter_context(tc.psum_pool(name="psum", bufs=1))
 
@@ -142,71 +140,22 @@ def tile_list_treaty_pricing_kernel(
         round_w1_head(1)
         quantize_w1(0)
         piece = P // GPSIMD_PIECES
-        for g in range(1, G):
-            for m0 in range(0, P, piece):
-                nc.gpsimd.tensor_scalar(
-                    out=w1_b[g][:, :, m0 : m0 + piece, :].rearrange("p t m j -> p m t j"),
-                    in0=w1_raw[g][:, :, PACK * m0 : PACK * (m0 + piece)].rearrange("p j (m t) -> p m t j", t=PACK),
-                    scalar1=1.0, scalar2=0.0, op0=MULT, op1=ADD,
-                )
-
-        h_full = [keep("h%d" % g, [P, PACK, S], F32) for g in range(LAST)]
-        h_last = [keep("h_last%d" % a, [P, PACK, HALF], F32) for a in range(HALVES)]
-        h_w = [keep("h_w%d" % g, [P, S], U32) for g in range(G)]
-        h_s_full = keep("h_s_full", [P, LAST, S], U8)
-        h_s_last = keep("h_s_last", [P, 1, S], U8)
-        woven = {}
-
-        def h_part(g, a):
-            return h_last[a][:] if g == LAST else h_full[g][:, :, half_cols(a)]
-
-        def h_scales(g, a):
-            return h_s_last[H_FIRST:P, 0, half_cols(a)] if g == LAST else h_s_full[H_FIRST:P, g, half_cols(a)]
-
-        def store_h(g, a):
-            rows = out_1[GROUP * g : GROUP * (g + 1), :].rearrange("(p t) j -> p t j", t=PACK)
-            if g == LAST:
-                nc.sync.dma_start(out=rows[:, :, half_cols(a)], in_=h_last[a][:])
-            else:
-                nc.sync.dma_start(out=rows, in_=h_full[g][:])
-
-        def store_scales(plane, g0, g1):
-            for r in range(PACK):
-                nc.sync.dma_start(
-                    out=out_3[g0:g1, r:BLOCKS:PACK, :].rearrange("g q m -> q g m").bitcast(I32),
-                    in_=live_rows(plane, H_FIRST, r),
-                )
-
-        def weave(g, a):
-            woven[g, a] = woven_pool.tile([P, HALF, PACK], BF16, name="woven", align_bytes=64)
-            split = VECTOR_COLS[g, a]
-            for copy, c0, c1 in ((nc.vector.tensor_copy, 0, split), (nc.scalar.copy, split, HALF)):
-                copy(
-                    out=woven[g, a][:, c0:c1, :].rearrange("p (c i) t -> p c t i", i=4),
-                    in_=h_part(g, a)[:, :, c0:c1].rearrange("p t (c i) -> p c t i", i=4),
-                )
-
-        def quantize_h(g, a):
-            nc.vector.quantize_mx(
-                out=h_w[g][:, half_cols(a)].bitcast(FP8X4), scales=h_scales(g, a),
-                in_=woven[g, a][:].rearrange("p c t -> p (c t)"),
+        for m0 in range(0, P, piece):
+            nc.gpsimd.tensor_scalar(
+                out=w1_b[LAST][:, :, m0 : m0 + piece, :].rearrange("p t m j -> p m t j"),
+                in0=w1_raw[LAST][:, :, PACK * m0 : PACK * (m0 + piece)].rearrange("p j (m t) -> p m t j", t=PACK),
+                scalar1=1.0, scalar2=0.0, op0=MULT, op1=ADD,
             )
-            words = out_2[g].rearrange("p m t -> p (m t)").bitcast(I32)
-            if g == LAST:
-                nc.sync.dma_start(out=words[:, half_cols(a)], in_=h_w[g][:, half_cols(a)].bitcast(I32))
-            elif a == HALVES - 1:
-                nc.sync.dma_start(out=words, in_=h_w[g][:].bitcast(I32))
-            if (g, a) == (LAST - 1, HALVES - 1):
-                store_scales(h_s_full, 0, LAST)
-            if (g, a) == (LAST, HALVES - 1):
-                store_scales(h_s_last, LAST, G)
 
-        steps = [(g, a, t) for g in range(LAST) for t in range(PACK) for a in range(HALVES)]
-        steps = steps + [(LAST, a, t) for a in range(HALVES) for t in range(PACK)]
-        final = len(steps) - 1
-        weave_after = {8: (0, 0), 11: (0, 1), 16: (1, 0), 17: (1, 1), 20: (2, 0), final: (2, 1)}
-        quantize_h_after = {min(step + QUANTIZE_LAG, final): half for step, half in weave_after.items()}
-        quantize_w1_after = {4: 1, 9: 2}
+        def round_w1_middle():
+            for copy, m0 in ((nc.vector.tensor_copy, 0), (nc.scalar.copy, P // 2)):
+                copy(
+                    out=w1_b[1][:, :, m0 : m0 + P // 2, :].rearrange("p t m j -> p m j t"),
+                    in_=w1_raw[1][:, :, PACK * m0 : PACK * (m0 + P // 2)].rearrange("p j (m t) -> p m j t", t=PACK),
+                )
+
+        h_sb = [keep("h%d" % g, [P, PACK, S], F32) for g in range(G)]
+        steps = [(g, a, t) for g in range(G) for t in range(PACK) for a in range(HALVES)]
         for step, (g, a, t) in enumerate(steps):
             places = slice(P * t, P * (t + 1))
             hit = bank(step % RING)
@@ -222,31 +171,71 @@ def tile_list_treaty_pricing_kernel(
             gate = gate_pool.tile([P, HALF], F32, name="gate")
             nc.scalar.activation(out=gate[:], in_=hit[:], func=SIGMOID, bias=att_sb[:, g, t : t + 1])
             nc.vector.scalar_tensor_tensor(
-                out=h_part(g, a)[:, t, :], in0=loss[:], scalar=load_sb[:, g, t : t + 1], in1=gate[:],
+                out=h_sb[g][:, t, half_cols(a)], in0=loss[:], scalar=load_sb[:, g, t : t + 1], in1=gate[:],
                 op0=ADD, op1=MULT,
             )
-            if t == PACK - 1 and (g == LAST or a == HALVES - 1):
-                store_h(g, a)
-            if step in weave_after:
-                weave(*weave_after[step])
-            if step in quantize_h_after:
-                quantize_h(*quantize_h_after[step])
-            if step in quantize_w1_after:
-                quantize_w1(quantize_w1_after[step])
-
-        order = [(i - Y_LAG * a, a) for i in range(LINES + Y_LAG) for a in range(HALVES) if 0 <= i - Y_LAG * a < LINES]
-        spare = [2 * RING, 2 * RING + 1]
-        y_banks = spare + spare + list(range(8))
-        for (c, a), b in zip(order, y_banks):
-            lines = slice(P * c, P * (c + 1))
-            acc = bank(b)
-            for g in range(G):
-                nc.tensor.matmul_mx(
-                    out=acc[:], lhsT=w3_w[:, g, lines].bitcast(FP8X4), lhsT_scale=w3_s[W3_FIRST:P, g, lines],
-                    rhs=h_w[g][:, half_cols(a)].bitcast(FP8X4), rhs_scale=h_scales(g, a),
-                    start=(g == 0), stop=(g == LAST),
+            if (a, t) == (HALVES - 1, PACK - 1):
+                nc.sync.dma_start(
+                    out=out_1[GROUP * g : GROUP * (g + 1), :].rearrange("(p t) j -> p t j", t=PACK), in_=h_sb[g][:]
                 )
-            y_rows = y_sb[c // per_load][:, c % per_load, :]
-            nc.vector.tensor_tensor(out=y_rows[:, half_cols(a)], in0=acc[:], in1=y_rows[:, half_cols(a)], op=ADD)
+            if (g, a, t) == (0, 0, 1):
+                round_w1_middle()
+            if g < LAST and (a, t) == (1, 2):
+                quantize_w1(g + 1)
+
+        woven = {(g, a): keep("woven%d_%d" % (g, a), [P, HALF, PACK], BF16) for g in range(G) for a in range(HALVES)}
+        h_w = [keep("h_w%d" % g, [P, S], U32) for g in range(G)]
+        h_s_full = keep("h_s_full", [P, LAST, S], U8)
+        h_s_last = keep("h_s_last", [P, 1, S], U8)
+
+        def h_scales(g, a):
+            return h_s_last[H_FIRST:P, 0, half_cols(a)] if g == LAST else h_s_full[H_FIRST:P, g, half_cols(a)]
+
+        def store_scales(plane, g0, g1):
+            for r in range(PACK):
+                nc.sync.dma_start(
+                    out=out_3[g0:g1, r:BLOCKS:PACK, :].rearrange("g q m -> q g m").bitcast(I32),
+                    in_=live_rows(plane, H_FIRST, r),
+                )
+
+        def weave(g, a):
+            split = VECTOR_COLS[g]
+            for copy, c0, c1 in ((nc.vector.tensor_copy, 0, split), (nc.scalar.copy, split, HALF)):
+                if c1 > c0:
+                    copy(
+                        out=woven[g, a][:, c0:c1, :].rearrange("p (c i) t -> p c t i", i=4),
+                        in_=h_sb[g][:, :, HALF * a + c0 : HALF * a + c1].rearrange("p t (c i) -> p c t i", i=4),
+                    )
+
+        def quantize_h(g, a):
+            nc.vector.quantize_mx(
+                out=h_w[g][:, half_cols(a)].bitcast(FP8X4), scales=h_scales(g, a),
+                in_=woven[g, a][:].rearrange("p c t -> p (c t)"),
+            )
             if a == HALVES - 1:
-                nc.sync.dma_start(out=out_0[lines, :], in_=y_rows)
+                nc.sync.dma_start(out=out_2[g].rearrange("p m t -> p (m t)").bitcast(I32), in_=h_w[g][:].bitcast(I32))
+            if (g, a) == (LAST - 1, HALVES - 1):
+                store_scales(h_s_full, 0, LAST)
+            if (g, a) == (LAST, HALVES - 1):
+                store_scales(h_s_last, LAST, G)
+
+        halves = [(g, a) for g in range(G) for a in range(HALVES)]
+        for i in range(len(halves) + QUANTIZE_LAG):
+            if i < len(halves):
+                weave(*halves[i])
+            if i >= QUANTIZE_LAG:
+                quantize_h(*halves[i - QUANTIZE_LAG])
+
+        for c in range(LINES):
+            lines = slice(P * c, P * (c + 1))
+            y_rows = y_sb[c // per_load][:, c % per_load, :]
+            for a in range(HALVES):
+                acc = bank((2 * RING + HALVES * c + a) % BANKS)
+                for g in range(G):
+                    nc.tensor.matmul_mx(
+                        out=acc[:], lhsT=w3_w[:, g, lines].bitcast(FP8X4), lhsT_scale=w3_s[W3_FIRST:P, g, lines],
+                        rhs=h_w[g][:, half_cols(a)].bitcast(FP8X4), rhs_scale=h_scales(g, a),
+                        start=(g == 0), stop=(g == LAST),
+                    )
+                nc.vector.tensor_tensor(out=y_rows[:, half_cols(a)], in0=acc[:], in1=y_rows[:, half_cols(a)], op=ADD)
+            nc.sync.dma_start(out=out_0[lines, :], in_=y_rows)

@@ -30,11 +30,11 @@ BLOCKS = 16
 SPREAD = P // BLOCKS
 BIAS_PITCH = 8
 H_FIRST, W3_FIRST = 4, 8
-VECTOR_COLS = (0, 320, 320)
-GPSIMD_PIECES = 8
+GPSIMD_PIECE = 512
+LEAD = 2
+GPSIMD_SUMS = ((4, 0), (5, 0), (5, 1))
 RING = 3
 BANKS = 8
-QUANTIZE_LAG = 2
 GATE_BUFS = 10
 
 
@@ -102,10 +102,9 @@ def tile_list_treaty_pricing_kernel(
             )
         nc.sync.dma_start(out=w3_w[:].bitcast(I32), in_=w3_words.rearrange("g p n t -> p g (n t)").bitcast(I32))
         prem_rows = prem.rearrange("(c p) j -> p c j", p=P)
-        per_load = LINES // 2
-        y_sb = [keep("y%d" % i, [P, per_load, S], F32) for i in range(2)]
-        for i in range(2):
-            nc.sync.dma_start(out=y_sb[i][:], in_=prem_rows[:, per_load * i : per_load * (i + 1), :])
+        y_sb = [keep("y%d" % a, [P, LINES, HALF], F32) for a in range(HALVES)]
+        for a in range(HALVES):
+            nc.sync.dma_start(out=y_sb[a][:], in_=prem_rows[:, :, half_cols(a)])
 
         w2_w = [keep("w2_w%d" % g, [P, 2 * GROUP], U8) for g in range(G)]
         w2_s = [keep("w2_s%d" % g, [P, GROUP], U8) for g in range(G)]
@@ -139,39 +138,104 @@ def tile_list_treaty_pricing_kernel(
             nc.vector.tensor_copy(v_w[a][:], tab_w[:].indirect(offsets[:, HALF // 16 * a : HALF // 16 * (a + 1)]))
         round_w1_head(1)
         quantize_w1(0)
-        piece = P // GPSIMD_PIECES
-        for m0 in range(0, P, piece):
-            nc.gpsimd.tensor_scalar(
-                out=w1_b[LAST][:, :, m0 : m0 + piece, :].rearrange("p t m j -> p m t j"),
-                in0=w1_raw[LAST][:, :, PACK * m0 : PACK * (m0 + piece)].rearrange("p j (m t) -> p m t j", t=PACK),
-                scalar1=1.0, scalar2=0.0, op0=MULT, op1=ADD,
-            )
 
-        def round_w1_middle():
-            for copy, m0 in ((nc.vector.tensor_copy, 0), (nc.scalar.copy, P // 2)):
-                copy(
-                    out=w1_b[1][:, :, m0 : m0 + P // 2, :].rearrange("p t m j -> p m j t"),
-                    in_=w1_raw[1][:, :, PACK * m0 : PACK * (m0 + P // 2)].rearrange("p j (m t) -> p m j t", t=PACK),
+        def gpsimd_round(out, in_):
+            nc.gpsimd.tensor_scalar(out=out, in0=in_, scalar1=1.0, scalar2=0.0, op0=MULT, op1=ADD)
+
+        piece = GPSIMD_PIECE // (PACK * PACK)
+        for g, first in ((1, P // 2), (LAST, 0)):
+            for m0 in range(first, P, piece):
+                gpsimd_round(
+                    w1_b[g][:, :, m0 : m0 + piece, :].rearrange("p t m j -> p m t j"),
+                    w1_raw[g][:, :, PACK * m0 : PACK * (m0 + piece)].rearrange("p j (m t) -> p m t j", t=PACK),
                 )
 
         h_sb = [keep("h%d" % g, [P, PACK, S], F32) for g in range(G)]
+        h_w = [keep("h_w%d" % a, [P, G, HALF], U32) for a in range(HALVES)]
+        h_s = [keep("h_s%d" % a, [P, G, HALF], U8) for a in range(HALVES)]
+        woven = {}
+
+        def weave(engine, g, a, c0, c1):
+            source = h_sb[g][:, :, HALF * a + c0 : HALF * a + c1]
+            if engine is nc.gpsimd:
+                cols = GPSIMD_PIECE // PACK
+                for c in range(0, c1 - c0, cols):
+                    gpsimd_round(
+                        woven[g, a][:, c0 + c : c0 + c + cols, :], source[:, :, c : c + cols].rearrange("p t c -> p c t")
+                    )
+            else:
+                copy = nc.vector.tensor_copy if engine is nc.vector else nc.scalar.copy
+                copy(
+                    out=woven[g, a][:, c0:c1, :].rearrange("p (c i) t -> p c t i", i=4),
+                    in_=source.rearrange("p t (c i) -> p c t i", i=4),
+                )
+
+        def woven_tile(g, a, name):
+            woven[g, a] = keep(name, [P, HALF, PACK], BF16)
+
+        def quantize_h(g, a):
+            nc.vector.quantize_mx(
+                out=h_w[a][:, g, :].bitcast(FP8X4), scales=h_s[a][H_FIRST:P, g, :],
+                in_=woven[g, a][:].rearrange("p c t -> p (c t)"),
+            )
+
+        def store_planes(a):
+            words = out_2.rearrange("g p m t -> p g (m t)").bitcast(I32)
+            nc.sync.dma_start(out=words[:, :, half_cols(a)], in_=h_w[a][:].bitcast(I32))
+            for r in range(PACK):
+                nc.sync.dma_start(
+                    out=out_3[:, r:BLOCKS:PACK, half_cols(a)].rearrange("g q m -> q g m").bitcast(I32),
+                    in_=live_rows(h_s[a], H_FIRST, r),
+                )
+
+        out_rows = out_0.rearrange("(c p) j -> p c j", p=P)
+
+        def mix(c, a, groups):
+            lines = slice(P * c, P * (c + 1))
+            acc = bank((2 * RING + LINES * a + c) % BANKS)
+            for g in groups:
+                nc.tensor.matmul_mx(
+                    out=acc[:], lhsT=w3_w[:, g, lines].bitcast(FP8X4), lhsT_scale=w3_s[W3_FIRST:P, g, lines],
+                    rhs=h_w[a][:, g, :].bitcast(FP8X4), rhs_scale=h_s[a][H_FIRST:P, g, :],
+                    start=(g == groups[0]), stop=(g == groups[-1]),
+                )
+            if (c, a) in GPSIMD_SUMS:
+                moved = gate_pool.tile([P, HALF], F32, name="gate")
+                nc.scalar.copy(out=moved[:], in_=acc[:])
+                nc.gpsimd.tensor_tensor(out=y_sb[a][:, c, :], in0=moved[:], in1=y_sb[a][:, c, :], op=ADD)
+            else:
+                nc.vector.tensor_tensor(out=y_sb[a][:, c, :], in0=acc[:], in1=y_sb[a][:, c, :], op=ADD)
+
+        def store_y(a, c0, c1):
+            nc.sync.dma_start(out=out_rows[:, c0:c1, half_cols(a)], in_=y_sb[a][:, c0:c1, :])
+
         steps = [(g, a, t) for g in range(G) for t in range(PACK) for a in range(HALVES)]
-        for step, (g, a, t) in enumerate(steps):
-            places = slice(P * t, P * (t + 1))
+        gates = {}
+
+        def make_gate(step):
+            g, a, t = steps[step]
             hit = bank(step % RING)
             nc.tensor.matmul_mx(
-                out=hit[:], lhsT=w2_w[g][:, 2 * P * t : 2 * P * (t + 1)].bitcast(FP4X4), lhsT_scale=w2_s[g][:, places],
+                out=hit[:], lhsT=w2_w[g][:, 2 * P * t : 2 * P * (t + 1)].bitcast(FP4X4),
+                lhsT_scale=w2_s[g][:, P * t : P * (t + 1)],
                 rhs=v_w[a][:].bitcast(FP8X4), rhs_scale=v_s[:, half_cols(a)], start=True, stop=True,
             )
+            gates[step] = gate_pool.tile([P, HALF], F32, name="gate")
+            nc.scalar.activation(out=gates[step][:], in_=hit[:], func=SIGMOID, bias=att_sb[:, g, t : t + 1])
+
+        for step in range(LEAD):
+            make_gate(step)
+        for step, (g, a, t) in enumerate(steps):
+            places = slice(P * t, P * (t + 1))
+            if step + LEAD < len(steps):
+                make_gate(step + LEAD)
             loss = bank(RING + step % RING)
             nc.tensor.matmul_mx(
                 out=loss[:], lhsT=w1_w[g][:, places].bitcast(FP8X4), lhsT_scale=w1_s[g][:, places],
                 rhs=v_w[a][:].bitcast(FP8X4), rhs_scale=v_s[:, half_cols(a)], start=True, stop=True,
             )
-            gate = gate_pool.tile([P, HALF], F32, name="gate")
-            nc.scalar.activation(out=gate[:], in_=hit[:], func=SIGMOID, bias=att_sb[:, g, t : t + 1])
             nc.vector.scalar_tensor_tensor(
-                out=h_sb[g][:, t, half_cols(a)], in0=loss[:], scalar=load_sb[:, g, t : t + 1], in1=gate[:],
+                out=h_sb[g][:, t, half_cols(a)], in0=loss[:], scalar=load_sb[:, g, t : t + 1], in1=gates[step][:],
                 op0=ADD, op1=MULT,
             )
             if (a, t) == (HALVES - 1, PACK - 1):
@@ -179,63 +243,41 @@ def tile_list_treaty_pricing_kernel(
                     out=out_1[GROUP * g : GROUP * (g + 1), :].rearrange("(p t) j -> p t j", t=PACK), in_=h_sb[g][:]
                 )
             if (g, a, t) == (0, 0, 1):
-                round_w1_middle()
+                nc.scalar.copy(
+                    out=w1_b[1][:, :, 0 : P // 2, :].rearrange("p t m j -> p m j t"),
+                    in_=w1_raw[1][:, :, 0 : GROUP // 2].rearrange("p j (m t) -> p m j t", t=PACK),
+                )
             if g < LAST and (a, t) == (1, 2):
                 quantize_w1(g + 1)
 
-        woven = {(g, a): keep("woven%d_%d" % (g, a), [P, HALF, PACK], BF16) for g in range(G) for a in range(HALVES)}
-        h_w = [keep("h_w%d" % g, [P, S], U32) for g in range(G)]
-        h_s_full = keep("h_s_full", [P, LAST, S], U8)
-        h_s_last = keep("h_s_last", [P, 1, S], U8)
-
-        def h_scales(g, a):
-            return h_s_last[H_FIRST:P, 0, half_cols(a)] if g == LAST else h_s_full[H_FIRST:P, g, half_cols(a)]
-
-        def store_scales(plane, g0, g1):
-            for r in range(PACK):
-                nc.sync.dma_start(
-                    out=out_3[g0:g1, r:BLOCKS:PACK, :].rearrange("g q m -> q g m").bitcast(I32),
-                    in_=live_rows(plane, H_FIRST, r),
-                )
-
-        def weave(g, a):
-            split = VECTOR_COLS[g]
-            for copy, c0, c1 in ((nc.vector.tensor_copy, 0, split), (nc.scalar.copy, split, HALF)):
-                if c1 > c0:
-                    copy(
-                        out=woven[g, a][:, c0:c1, :].rearrange("p (c i) t -> p c t i", i=4),
-                        in_=h_sb[g][:, :, HALF * a + c0 : HALF * a + c1].rearrange("p t (c i) -> p c t i", i=4),
-                    )
-
-        def quantize_h(g, a):
-            nc.vector.quantize_mx(
-                out=h_w[g][:, half_cols(a)].bitcast(FP8X4), scales=h_scales(g, a),
-                in_=woven[g, a][:].rearrange("p c t -> p (c t)"),
-            )
-            if a == HALVES - 1:
-                nc.sync.dma_start(out=out_2[g].rearrange("p m t -> p (m t)").bitcast(I32), in_=h_w[g][:].bitcast(I32))
-            if (g, a) == (LAST - 1, HALVES - 1):
-                store_scales(h_s_full, 0, LAST)
-            if (g, a) == (LAST, HALVES - 1):
-                store_scales(h_s_last, LAST, G)
-
-        halves = [(g, a) for g in range(G) for a in range(HALVES)]
-        for i in range(len(halves) + QUANTIZE_LAG):
-            if i < len(halves):
-                weave(*halves[i])
-            if i >= QUANTIZE_LAG:
-                quantize_h(*halves[i - QUANTIZE_LAG])
-
+        for g, engine in enumerate((nc.gpsimd, nc.scalar, nc.vector)):
+            woven_tile(g, 0, "woven%d" % g)
+        weave(nc.gpsimd, 0, 0, 0, HALF)
+        weave(nc.scalar, 1, 0, 0, HALF // 2)
+        weave(nc.scalar, 1, 0, HALF // 2, HALF)
+        quantize_h(0, 0)
+        weave(nc.vector, 2, 0, 0, HALF)
+        quantize_h(1, 0)
+        quantize_h(2, 0)
+        store_planes(0)
+        for g in (1, 2):
+            woven_tile(g, 1, "woven%d" % (G + g))
+            weave(nc.scalar, g, 1, 0, HALF)
+        quantize_h(1, 1)
+        woven_tile(0, 1, "woven%d" % (G + 1))
+        weave(nc.gpsimd, 0, 1, 0, HALF // 2)
+        weave(nc.scalar, 0, 1, HALF // 2, HALF)
         for c in range(LINES):
-            lines = slice(P * c, P * (c + 1))
-            y_rows = y_sb[c // per_load][:, c % per_load, :]
-            for a in range(HALVES):
-                acc = bank((2 * RING + HALVES * c + a) % BANKS)
-                for g in range(G):
-                    nc.tensor.matmul_mx(
-                        out=acc[:], lhsT=w3_w[:, g, lines].bitcast(FP8X4), lhsT_scale=w3_s[W3_FIRST:P, g, lines],
-                        rhs=h_w[g][:, half_cols(a)].bitcast(FP8X4), rhs_scale=h_scales(g, a),
-                        start=(g == 0), stop=(g == LAST),
-                    )
-                nc.vector.tensor_tensor(out=y_rows[:, half_cols(a)], in0=acc[:], in1=y_rows[:, half_cols(a)], op=ADD)
-            nc.sync.dma_start(out=out_0[lines, :], in_=y_rows)
+            mix(c, 0, (0, 1, 2))
+            if c == 2:
+                quantize_h(2, 1)
+            if c == 3:
+                quantize_h(0, 1)
+            if c % 2 == 1:
+                store_y(0, c - 1, c + 1)
+        store_planes(1)
+        for c in (5, 0, 1, 2, 3, 4):
+            mix(c, 1, (1, 2, 0))
+            if c in (1, 3):
+                store_y(1, c - 1, c + 1)
+        store_y(1, 4, 6)

@@ -29,13 +29,15 @@ QUAD = 32
 BLOCKS = 16
 SPREAD = P // BLOCKS
 BIAS_PITCH = 8
-H_FIRST, W3_FIRST = 4, 8
+H_FIRST = 4
 GPSIMD_PIECE = 512
 LEAD = 2
-GPSIMD_SUMS = ((4, 0), (5, 0), (5, 1))
 RING = 3
 BANKS = 8
 GATE_BUFS = 10
+Y_STORE = 2
+V_COLS, W2_COLS, W3_COLS = slice(0, S), slice(S, S + H), slice(S + H, S + H + G * N)
+SCALE_COLS = S + H + G * N
 
 
 def tile_list_treaty_pricing_kernel(
@@ -67,62 +69,55 @@ def tile_list_treaty_pricing_kernel(
 
         offsets = held.tile([P, S // 16], U16, name="offsets")
         nc.sync.dma_start(offsets[:], offs)
-
-        w1_rows = w1.rearrange("(p j) c -> p j c", j=PACK)
-        w1_head = [keep("w1_head%d" % u, [P, PACK, GROUP // 2], F32) for u in range(2)]
-        w1_raw = {g: keep("w1_raw%d" % g, [P, PACK, GROUP], F32) for g in range(1, G)}
-        nc.sync.dma_start(out=w1_head[0][:], in_=w1_rows[:, :, 0 : GROUP // 2])
         tab_s = zeroed_plane("tab_s", [P, T])
-        nc.sync.dma_start(out=tab_s[0:P:SPREAD].bitcast(I32), in_=tab_scales[0].bitcast(I32))
+        w2s_raw = zeroed_plane("w2s_raw", [P, H])
+        planes = zeroed_plane("planes", [P, SCALE_COLS])
+        staged = keep("staged", [P, SCALE_COLS], U8)
+        nc.sync.dma_start(
+            out=staged[0:P:SPREAD, W3_COLS].rearrange("q (g n) -> q g n", g=G).bitcast(I32),
+            in_=w3_scales.rearrange("g q n -> q g n").bitcast(I32),
+        )
         w2_raw = keep("w2_raw", [P, 2 * H], U8)
         nc.sync.dma_start(out=w2_raw[:].bitcast(I32), in_=w2_words[0].bitcast(I32))
-        w2s_raw = zeroed_plane("w2s_raw", [P, H])
-        for r in range(PACK):
-            nc.sync.dma_start(out=live_rows(w2s_raw, 0, r), in_=w2_scales[0, r:BLOCKS:PACK, :].bitcast(I32))
+        nc.sync.dma_start(out=tab_s[0:P:SPREAD].bitcast(I32), in_=tab_scales[0].bitcast(I32))
+        nc.sync.dma_start(out=w2s_raw[0:P:SPREAD].bitcast(I32), in_=w2_scales[0].bitcast(I32))
         tab_w = keep("tab_w", [P, T], U32)
         nc.sync.dma_start(out=tab_w[:].bitcast(I32), in_=tab_words[0].rearrange("p n t -> p (n t)").bitcast(I32))
         att_sb = keep("att_sb", [P, G, BIAS_PITCH], F32)
         nc.sync.dma_start(out=att_sb[:, :, 0:PACK], in_=att.rearrange("(g p t) -> p g t", p=P, t=PACK))
-        picked_s = keep("picked_s", [P, S], U8)
-        v_s = zeroed_plane("v_s", [P, S])
-        nc.vector.tensor_copy(picked_s[:], tab_s[:].indirect(offsets[:]))
-        for r in range(PACK):
-            nc.sync.dma_start(out=live_rows(v_s, 0, r), in_=live_rows(picked_s, 0, SPREAD * r))
-        nc.sync.dma_start(out=w1_head[1][:], in_=w1_rows[:, :, GROUP // 2 : GROUP])
         load_sb = keep("load_sb", [P, G, BIAS_PITCH], F32)
         nc.sync.dma_start(out=load_sb[:, :, 0:PACK], in_=load.rearrange("(g p t) -> p g t", p=P, t=PACK))
-        for g in range(1, G):
-            nc.sync.dma_start(out=w1_raw[g][:], in_=w1_rows[:, :, GROUP * g : GROUP * (g + 1)])
-        w3_w = keep("w3_w", [P, G, N], U32)
-        w3_s = zeroed_plane("w3_s", [P, G, N])
-        for r in range(PACK):
-            nc.sync.dma_start(
-                out=live_rows(w3_s, W3_FIRST, r),
-                in_=w3_scales[:, r:BLOCKS:PACK, :].rearrange("g q n -> q g n").bitcast(I32),
-            )
-        nc.sync.dma_start(out=w3_w[:].bitcast(I32), in_=w3_words.rearrange("g p n t -> p g (n t)").bitcast(I32))
-        prem_rows = prem.rearrange("(c p) j -> p c j", p=P)
-        y_sb = [keep("y%d" % a, [P, LINES, HALF], F32) for a in range(HALVES)]
-        for a in range(HALVES):
-            nc.sync.dma_start(out=y_sb[a][:], in_=prem_rows[:, :, half_cols(a)])
+        w1_rows = w1.rearrange("(p j) c -> p j c", j=PACK)
+        w1_head = keep("w1_head", [P, PACK, GROUP], F32)
+        w1_rest = keep("w1_rest", [P, PACK, H - GROUP], F32)
+        nc.sync.dma_start(out=w1_head[:], in_=w1_rows[:, :, 0:GROUP])
 
-        w2_w = [keep("w2_w%d" % g, [P, 2 * GROUP], U8) for g in range(G)]
-        w2_s = [keep("w2_s%d" % g, [P, GROUP], U8) for g in range(G)]
+        def deal(out, in_):
+            nc.vector.tensor_copy(
+                out=out.rearrange("p (g t m) -> p t g m", g=G, t=PACK),
+                in_=in_.rearrange("p (g m t) -> p t g m", g=G, t=PACK),
+            )
+
+        picked_s = keep("picked_s", [P, S], U8)
+        nc.vector.tensor_copy(picked_s[:], tab_s[:].indirect(offsets[:]))
+        nc.vector.tensor_copy(out=staged[:, V_COLS].bitcast(I32), in_=picked_s[:].bitcast(I32))
+        deal(staged[:, W2_COLS], w2s_raw[:])
+        for r in range(PACK):
+            nc.sync.dma_start(out=live_rows(planes, 0, r), in_=live_rows(staged, 0, SPREAD * r))
+        v_s = planes[:, V_COLS]
+        w2_s = planes[:, W2_COLS].rearrange("p (g c) -> p g c", g=G)
+        w3_s = planes[:, W3_COLS].rearrange("p (g n) -> p g n", g=G)
+        nc.sync.dma_start(out=w1_rest[:], in_=w1_rows[:, :, GROUP:H])
+        w3_w = keep("w3_w", [P, G, N], U32)
+        nc.sync.dma_start(out=w3_w[:].bitcast(I32), in_=w3_words.rearrange("g p n t -> p g (n t)").bitcast(I32))
+        y_sb = keep("y_sb", [P, LINES, S], F32)
+        nc.sync.dma_start(out=y_sb[:], in_=prem.rearrange("(c p) j -> p c j", p=P))
+
+        w2_w = keep("w2_w", [P, 2 * H], U8)
         v_w = [keep("v_w%d" % a, [P, HALF], U32) for a in range(HALVES)]
         w1_b = [keep("w1_b%d" % g, [P, PACK, P, PACK], BF16) for g in range(G)]
         w1_w = [keep("w1_w%d" % g, [P, GROUP], U32) for g in range(G)]
         w1_s = [keep("w1_s%d" % g, [P, GROUP], U8) for g in range(G)]
-
-        def deal(out, in_):
-            nc.vector.tensor_copy(
-                out=out.rearrange("p (t m) -> p t m", t=PACK), in_=in_.rearrange("p (m t) -> p t m", t=PACK)
-            )
-
-        def round_w1_head(u):
-            nc.vector.tensor_copy(
-                out=w1_b[0][:, :, P // 2 * u : P // 2 * (u + 1), :].rearrange("p t m j -> p m j t"),
-                in_=w1_head[u][:].rearrange("p j (m t) -> p m j t", t=PACK),
-            )
 
         def quantize_w1(g):
             nc.vector.quantize_mx(
@@ -130,30 +125,30 @@ def tile_list_treaty_pricing_kernel(
                 in_=w1_b[g][:].rearrange("p t m j -> p (t m j)"),
             )
 
-        round_w1_head(0)
-        for g in range(G):
-            deal(w2_w[g][:].bitcast(U16), w2_raw[:, 2 * GROUP * g : 2 * GROUP * (g + 1)].bitcast(U16))
-            deal(w2_s[g][:], w2s_raw[:, GROUP * g : GROUP * (g + 1)])
+        deal(w2_w[:].bitcast(U16), w2_raw[:].bitcast(U16))
         for a in range(HALVES):
             nc.vector.tensor_copy(v_w[a][:], tab_w[:].indirect(offsets[:, HALF // 16 * a : HALF // 16 * (a + 1)]))
-        round_w1_head(1)
+        nc.vector.tensor_copy(
+            out=w1_b[0][:].rearrange("p t m j -> p m j t"), in_=w1_head[:].rearrange("p j (m t) -> p m j t", t=PACK)
+        )
         quantize_w1(0)
 
         def gpsimd_round(out, in_):
             nc.gpsimd.tensor_scalar(out=out, in0=in_, scalar1=1.0, scalar2=0.0, op0=MULT, op1=ADD)
 
         piece = GPSIMD_PIECE // (PACK * PACK)
-        for g, first in ((1, P // 2), (LAST, 0)):
-            for m0 in range(first, P, piece):
+        for g in range(1, G):
+            for m0 in range(0, P, piece):
+                c0 = GROUP * (g - 1) + PACK * m0
                 gpsimd_round(
                     w1_b[g][:, :, m0 : m0 + piece, :].rearrange("p t m j -> p m t j"),
-                    w1_raw[g][:, :, PACK * m0 : PACK * (m0 + piece)].rearrange("p j (m t) -> p m t j", t=PACK),
+                    w1_rest[:, :, c0 : c0 + PACK * piece].rearrange("p j (m t) -> p m t j", t=PACK),
                 )
 
         h_sb = [keep("h%d" % g, [P, PACK, S], F32) for g in range(G)]
-        h_w = [keep("h_w%d" % a, [P, G, HALF], U32) for a in range(HALVES)]
-        h_s = [keep("h_s%d" % a, [P, G, HALF], U8) for a in range(HALVES)]
-        woven = {}
+        h_w = keep("h_w", [P, G, S], U32)
+        h_s = keep("h_s", [P, G, S], U8)
+        woven = {(g, a): keep("woven%d%d" % (g, a), [P, HALF, PACK], BF16) for g in range(G) for a in range(HALVES)}
 
         def weave(engine, g, a, c0, c1):
             source = h_sb[g][:, :, HALF * a + c0 : HALF * a + c1]
@@ -164,60 +159,27 @@ def tile_list_treaty_pricing_kernel(
                         woven[g, a][:, c0 + c : c0 + c + cols, :], source[:, :, c : c + cols].rearrange("p t c -> p c t")
                     )
             else:
-                copy = nc.vector.tensor_copy if engine is nc.vector else nc.scalar.copy
-                copy(
+                nc.scalar.copy(
                     out=woven[g, a][:, c0:c1, :].rearrange("p (c i) t -> p c t i", i=4),
                     in_=source.rearrange("p t (c i) -> p c t i", i=4),
                 )
 
-        def woven_tile(g, a, name):
-            woven[g, a] = keep(name, [P, HALF, PACK], BF16)
-
         def quantize_h(g, a):
             nc.vector.quantize_mx(
-                out=h_w[a][:, g, :].bitcast(FP8X4), scales=h_s[a][H_FIRST:P, g, :],
+                out=h_w[:, g, half_cols(a)].bitcast(FP8X4), scales=h_s[H_FIRST:P, g, half_cols(a)],
                 in_=woven[g, a][:].rearrange("p c t -> p (c t)"),
             )
 
-        def store_planes(a):
-            words = out_2.rearrange("g p m t -> p g (m t)").bitcast(I32)
-            nc.sync.dma_start(out=words[:, :, half_cols(a)], in_=h_w[a][:].bitcast(I32))
-            for r in range(PACK):
-                nc.sync.dma_start(
-                    out=out_3[:, r:BLOCKS:PACK, half_cols(a)].rearrange("g q m -> q g m").bitcast(I32),
-                    in_=live_rows(h_s[a], H_FIRST, r),
-                )
-
-        out_rows = out_0.rearrange("(c p) j -> p c j", p=P)
-
-        def mix(c, a, groups):
-            lines = slice(P * c, P * (c + 1))
-            acc = bank((2 * RING + LINES * a + c) % BANKS)
-            for g in groups:
-                nc.tensor.matmul_mx(
-                    out=acc[:], lhsT=w3_w[:, g, lines].bitcast(FP8X4), lhsT_scale=w3_s[W3_FIRST:P, g, lines],
-                    rhs=h_w[a][:, g, :].bitcast(FP8X4), rhs_scale=h_s[a][H_FIRST:P, g, :],
-                    start=(g == groups[0]), stop=(g == groups[-1]),
-                )
-            if (c, a) in GPSIMD_SUMS:
-                moved = gate_pool.tile([P, HALF], F32, name="gate")
-                nc.scalar.copy(out=moved[:], in_=acc[:])
-                nc.gpsimd.tensor_tensor(out=y_sb[a][:, c, :], in0=moved[:], in1=y_sb[a][:, c, :], op=ADD)
-            else:
-                nc.vector.tensor_tensor(out=y_sb[a][:, c, :], in0=acc[:], in1=y_sb[a][:, c, :], op=ADD)
-
-        def store_y(a, c0, c1):
-            nc.sync.dma_start(out=out_rows[:, c0:c1, half_cols(a)], in_=y_sb[a][:, c0:c1, :])
-
-        steps = [(g, a, t) for g in range(G) for t in range(PACK) for a in range(HALVES)]
+        steps = [(g, a, t) for g in range(LAST) for t in range(PACK) for a in range(HALVES)]
+        steps = steps + [(LAST, a, t) for a in range(HALVES) for t in range(PACK)]
         gates = {}
 
         def make_gate(step):
             g, a, t = steps[step]
             hit = bank(step % RING)
             nc.tensor.matmul_mx(
-                out=hit[:], lhsT=w2_w[g][:, 2 * P * t : 2 * P * (t + 1)].bitcast(FP4X4),
-                lhsT_scale=w2_s[g][:, P * t : P * (t + 1)],
+                out=hit[:], lhsT=w2_w[:, 2 * (GROUP * g + P * t) : 2 * (GROUP * g + P * (t + 1))].bitcast(FP4X4),
+                lhsT_scale=w2_s[:, g, P * t : P * (t + 1)],
                 rhs=v_w[a][:].bitcast(FP8X4), rhs_scale=v_s[:, half_cols(a)], start=True, stop=True,
             )
             gates[step] = gate_pool.tile([P, HALF], F32, name="gate")
@@ -242,42 +204,52 @@ def tile_list_treaty_pricing_kernel(
                 nc.sync.dma_start(
                     out=out_1[GROUP * g : GROUP * (g + 1), :].rearrange("(p t) j -> p t j", t=PACK), in_=h_sb[g][:]
                 )
-            if (g, a, t) == (0, 0, 1):
-                nc.scalar.copy(
-                    out=w1_b[1][:, :, 0 : P // 2, :].rearrange("p t m j -> p m j t"),
-                    in_=w1_raw[1][:, :, 0 : GROUP // 2].rearrange("p j (m t) -> p m j t", t=PACK),
-                )
-            if g < LAST and (a, t) == (1, 2):
+            if g < LAST and (a, t) == (HALVES - 1, PACK - 2):
                 quantize_w1(g + 1)
+            if (g, a, t) == (0, HALVES - 1, PACK - 1):
+                weave(nc.gpsimd, 0, 0, 0, HALF)
+                weave(nc.gpsimd, 0, 1, 0, HALF)
+            if (g, a, t) == (LAST, 0, PACK - 1):
+                weave(nc.gpsimd, LAST, 0, 0, HALF)
 
-        for g, engine in enumerate((nc.gpsimd, nc.scalar, nc.vector)):
-            woven_tile(g, 0, "woven%d" % g)
-        weave(nc.gpsimd, 0, 0, 0, HALF)
-        weave(nc.scalar, 1, 0, 0, HALF // 2)
-        weave(nc.scalar, 1, 0, HALF // 2, HALF)
-        quantize_h(0, 0)
-        weave(nc.vector, 2, 0, 0, HALF)
-        quantize_h(1, 0)
-        quantize_h(2, 0)
-        store_planes(0)
-        for g in (1, 2):
-            woven_tile(g, 1, "woven%d" % (G + g))
-            weave(nc.scalar, g, 1, 0, HALF)
-        quantize_h(1, 1)
-        woven_tile(0, 1, "woven%d" % (G + 1))
-        weave(nc.gpsimd, 0, 1, 0, HALF // 2)
-        weave(nc.scalar, 0, 1, HALF // 2, HALF)
+        weave(nc.scalar, 1, 0, 0, HALF)
+        weave(nc.scalar, 1, 1, 0, HALF)
+        for g in range(G):
+            quantize_h(g, 0)
+        weave(nc.scalar, LAST, 1, 0, HALF // 2)
+        weave(nc.gpsimd, LAST, 1, HALF // 2, HALF)
+        for g in range(G):
+            quantize_h(g, 1)
+        nc.sync.dma_start(out=out_2.rearrange("g p m t -> p g (m t)").bitcast(I32), in_=h_w[:].bitcast(I32))
+        for r in range(PACK):
+            nc.sync.dma_start(
+                out=out_3[:, r:BLOCKS:PACK, :].rearrange("g q m -> q g m").bitcast(I32), in_=live_rows(h_s, H_FIRST, r)
+            )
+
+        out_rows = out_0.rearrange("(c p) j -> p c j", p=P)
+        acc = {(a, c): bank((2 * RING + LINES * a + c) % BANKS) for a in range(1) for c in range(LINES)}
+
+        def mix(a, c, g):
+            lines = slice(P * c, P * (c + 1))
+            nc.tensor.matmul_mx(
+                out=acc[a, c][:], lhsT=w3_w[:, g, lines].bitcast(FP8X4), lhsT_scale=w3_s[:, g, lines],
+                rhs=h_w[:, g, half_cols(a)].bitcast(FP8X4), rhs_scale=h_s[H_FIRST:P, g, half_cols(a)],
+                start=(g == 0), stop=(g == LAST),
+            )
+
+        def add_prem(a, c):
+            nc.vector.tensor_tensor(out=y_sb[:, c, half_cols(a)], in0=acc[a, c][:], in1=y_sb[:, c, half_cols(a)], op=ADD)
+
+        for g in range(G):
+            for c in range(LINES):
+                mix(0, c, g)
         for c in range(LINES):
-            mix(c, 0, (0, 1, 2))
-            if c == 2:
-                quantize_h(2, 1)
-            if c == 3:
-                quantize_h(0, 1)
-            if c % 2 == 1:
-                store_y(0, c - 1, c + 1)
-        store_planes(1)
-        for c in (5, 0, 1, 2, 3, 4):
-            mix(c, 1, (1, 2, 0))
-            if c in (1, 3):
-                store_y(1, c - 1, c + 1)
-        store_y(1, 4, 6)
+            add_prem(0, c)
+        for c in range(LINES):
+            acc[1, c] = bank((2 * RING + LINES + c) % BANKS)
+            for g in range(G):
+                mix(1, c, g)
+            add_prem(1, c)
+            if (c + 1) % Y_STORE == 0:
+                rows = slice(c + 1 - Y_STORE, c + 1)
+                nc.sync.dma_start(out=out_rows[:, rows, :], in_=y_sb[:, rows, :])

@@ -128,22 +128,26 @@ def tile_list_treaty_pricing_kernel(
         deal(w2_w[:].bitcast(U16), w2_raw[:].bitcast(U16))
         for a in range(HALVES):
             nc.vector.tensor_copy(v_w[a][:], tab_w[:].indirect(offsets[:, HALF // 16 * a : HALF // 16 * (a + 1)]))
-        nc.vector.tensor_copy(
-            out=w1_b[0][:].rearrange("p t m j -> p m j t"), in_=w1_head[:].rearrange("p j (m t) -> p m j t", t=PACK)
-        )
+
+        def round_w1(copy, g, source, m0, m1):
+            copy(
+                out=w1_b[g][:, :, m0:m1, :].rearrange("p t m j -> p m j t"),
+                in_=source[:, :, PACK * m0 : PACK * m1].rearrange("p j (m t) -> p m j t", t=PACK),
+            )
+
+        round_w1(nc.vector.tensor_copy, 0, w1_head, 0, P)
         quantize_w1(0)
 
         def gpsimd_round(out, in_):
             nc.gpsimd.tensor_scalar(out=out, in0=in_, scalar1=1.0, scalar2=0.0, op0=MULT, op1=ADD)
 
         piece = GPSIMD_PIECE // (PACK * PACK)
-        for g in range(1, G):
-            for m0 in range(0, P, piece):
-                c0 = GROUP * (g - 1) + PACK * m0
-                gpsimd_round(
-                    w1_b[g][:, :, m0 : m0 + piece, :].rearrange("p t m j -> p m t j"),
-                    w1_rest[:, :, c0 : c0 + PACK * piece].rearrange("p j (m t) -> p m t j", t=PACK),
-                )
+        for m0 in range(0, P, piece):
+            c0 = GROUP + PACK * m0
+            gpsimd_round(
+                w1_b[LAST][:, :, m0 : m0 + piece, :].rearrange("p t m j -> p m t j"),
+                w1_rest[:, :, c0 : c0 + PACK * piece].rearrange("p j (m t) -> p m t j", t=PACK),
+            )
 
         h_sb = [keep("h%d" % g, [P, PACK, S], F32) for g in range(G)]
         h_w = keep("h_w", [P, G, S], U32)
@@ -159,7 +163,8 @@ def tile_list_treaty_pricing_kernel(
                         woven[g, a][:, c0 + c : c0 + c + cols, :], source[:, :, c : c + cols].rearrange("p t c -> p c t")
                     )
             else:
-                nc.scalar.copy(
+                copy = nc.vector.tensor_copy if engine is nc.vector else nc.scalar.copy
+                copy(
                     out=woven[g, a][:, c0:c1, :].rearrange("p (c i) t -> p c t i", i=4),
                     in_=source.rearrange("p t (c i) -> p c t i", i=4),
                 )
@@ -204,21 +209,24 @@ def tile_list_treaty_pricing_kernel(
                 nc.sync.dma_start(
                     out=out_1[GROUP * g : GROUP * (g + 1), :].rearrange("(p t) j -> p t j", t=PACK), in_=h_sb[g][:]
                 )
+            if (g, a, t) == (0, 0, 1):
+                round_w1(nc.scalar.copy, 1, w1_rest, 0, P // 2)
+            if (g, a, t) == (0, 0, 2):
+                round_w1(nc.vector.tensor_copy, 1, w1_rest, P // 2, P)
             if g < LAST and (a, t) == (HALVES - 1, PACK - 2):
                 quantize_w1(g + 1)
             if (g, a, t) == (0, HALVES - 1, PACK - 1):
                 weave(nc.gpsimd, 0, 0, 0, HALF)
-                weave(nc.gpsimd, 0, 1, 0, HALF)
-            if (g, a, t) == (LAST, 0, PACK - 1):
-                weave(nc.gpsimd, LAST, 0, 0, HALF)
 
         weave(nc.scalar, 1, 0, 0, HALF)
+        quantize_h(0, 0)
+        weave(nc.vector, LAST, 0, 0, HALF)
+        quantize_h(1, 0)
+        quantize_h(LAST, 0)
+        weave(nc.scalar, 0, 1, 0, HALF)
         weave(nc.scalar, 1, 1, 0, HALF)
-        for g in range(G):
-            quantize_h(g, 0)
-        weave(nc.scalar, LAST, 1, 0, HALF // 2)
-        weave(nc.gpsimd, LAST, 1, HALF // 2, HALF)
-        for g in range(G):
+        weave(nc.vector, LAST, 1, 0, HALF)
+        for g in (0, LAST, 1):
             quantize_h(g, 1)
         nc.sync.dma_start(out=out_2.rearrange("g p m t -> p g (m t)").bitcast(I32), in_=h_w[:].bitcast(I32))
         for r in range(PACK):

@@ -30,12 +30,12 @@ BLOCKS = 16
 SPREAD = P // BLOCKS
 BIAS_PITCH = 8
 H_FIRST = 4
-GPSIMD_PIECE = 512
 LEAD = 2
 RING = 3
 BANKS = 8
 GATE_BUFS = 10
-Y_STORE = 2
+Y_STORES = (2, 4, 5, 6)
+ORDER = ((1, 0, LAST), (0, LAST, 1))
 V_COLS, W2_COLS, W3_COLS = slice(0, S), slice(S, S + H), slice(S + H, S + H + G * N)
 SCALE_COLS = S + H + G * N
 
@@ -135,39 +135,19 @@ def tile_list_treaty_pricing_kernel(
                 in_=source[:, :, PACK * m0 : PACK * m1].rearrange("p j (m t) -> p m j t", t=PACK),
             )
 
-        round_w1(nc.vector.tensor_copy, 0, w1_head, 0, P)
+        round_w1(nc.vector.tensor_copy, 0, w1_head[:], 0, P)
         quantize_w1(0)
-
-        def gpsimd_round(out, in_):
-            nc.gpsimd.tensor_scalar(out=out, in0=in_, scalar1=1.0, scalar2=0.0, op0=MULT, op1=ADD)
-
-        piece = GPSIMD_PIECE // (PACK * PACK)
-        for m0 in range(0, P, piece):
-            c0 = GROUP + PACK * m0
-            gpsimd_round(
-                w1_b[LAST][:, :, m0 : m0 + piece, :].rearrange("p t m j -> p m t j"),
-                w1_rest[:, :, c0 : c0 + PACK * piece].rearrange("p j (m t) -> p m t j", t=PACK),
-            )
 
         h_sb = [keep("h%d" % g, [P, PACK, S], F32) for g in range(G)]
         h_w = keep("h_w", [P, G, S], U32)
         h_s = keep("h_s", [P, G, S], U8)
         woven = {(g, a): keep("woven%d%d" % (g, a), [P, HALF, PACK], BF16) for g in range(G) for a in range(HALVES)}
 
-        def weave(engine, g, a, c0, c1):
-            source = h_sb[g][:, :, HALF * a + c0 : HALF * a + c1]
-            if engine is nc.gpsimd:
-                cols = GPSIMD_PIECE // PACK
-                for c in range(0, c1 - c0, cols):
-                    gpsimd_round(
-                        woven[g, a][:, c0 + c : c0 + c + cols, :], source[:, :, c : c + cols].rearrange("p t c -> p c t")
-                    )
-            else:
-                copy = nc.vector.tensor_copy if engine is nc.vector else nc.scalar.copy
-                copy(
-                    out=woven[g, a][:, c0:c1, :].rearrange("p (c i) t -> p c t i", i=4),
-                    in_=source.rearrange("p t (c i) -> p c t i", i=4),
-                )
+        def weave(copy, g, a):
+            copy(
+                out=woven[g, a][:].rearrange("p (c i) t -> p c t i", i=4),
+                in_=h_sb[g][:, :, half_cols(a)].rearrange("p t (c i) -> p c t i", i=4),
+            )
 
         def quantize_h(g, a):
             nc.vector.quantize_mx(
@@ -209,26 +189,26 @@ def tile_list_treaty_pricing_kernel(
                 nc.sync.dma_start(
                     out=out_1[GROUP * g : GROUP * (g + 1), :].rearrange("(p t) j -> p t j", t=PACK), in_=h_sb[g][:]
                 )
-            if (g, a, t) == (0, 0, 1):
-                round_w1(nc.scalar.copy, 1, w1_rest, 0, P // 2)
             if (g, a, t) == (0, 0, 2):
-                round_w1(nc.vector.tensor_copy, 1, w1_rest, P // 2, P)
+                round_w1(nc.vector.tensor_copy, 1, w1_rest[:, :, 0:GROUP], 0, P)
+            if (g, t) == (0, PACK - 1):
+                round_w1(nc.scalar.copy, LAST, w1_rest[:, :, GROUP:], P // 2 * a, P // 2 * (a + 1))
             if g < LAST and (a, t) == (HALVES - 1, PACK - 2):
                 quantize_w1(g + 1)
-            if (g, a, t) == (0, HALVES - 1, PACK - 1):
-                weave(nc.gpsimd, 0, 0, 0, HALF)
 
-        weave(nc.scalar, 1, 0, 0, HALF)
-        quantize_h(0, 0)
-        weave(nc.vector, LAST, 0, 0, HALF)
+        for g, a in ((0, 0), (0, 1), (1, 1)):
+            weave(nc.scalar.copy, g, a)
+        weave(nc.vector.tensor_copy, 1, 0)
         quantize_h(1, 0)
+        weave(nc.vector.tensor_copy, LAST, 0)
+        quantize_h(0, 0)
         quantize_h(LAST, 0)
-        weave(nc.scalar, 0, 1, 0, HALF)
-        weave(nc.scalar, 1, 1, 0, HALF)
-        weave(nc.vector, LAST, 1, 0, HALF)
-        for g in (0, LAST, 1):
+        words = out_2.rearrange("g p m t -> p g (m t)").bitcast(I32)
+        nc.sync.dma_start(out=words[:, :, half_cols(0)], in_=h_w[:, :, half_cols(0)].bitcast(I32))
+        weave(nc.vector.tensor_copy, LAST, 1)
+        for g in ORDER[1]:
             quantize_h(g, 1)
-        nc.sync.dma_start(out=out_2.rearrange("g p m t -> p g (m t)").bitcast(I32), in_=h_w[:].bitcast(I32))
+        nc.sync.dma_start(out=words[:, :, half_cols(1)], in_=h_w[:, :, half_cols(1)].bitcast(I32))
         for r in range(PACK):
             nc.sync.dma_start(
                 out=out_3[:, r:BLOCKS:PACK, :].rearrange("g q m -> q g m").bitcast(I32), in_=live_rows(h_s, H_FIRST, r)
@@ -242,22 +222,21 @@ def tile_list_treaty_pricing_kernel(
             nc.tensor.matmul_mx(
                 out=acc[a, c][:], lhsT=w3_w[:, g, lines].bitcast(FP8X4), lhsT_scale=w3_s[:, g, lines],
                 rhs=h_w[:, g, half_cols(a)].bitcast(FP8X4), rhs_scale=h_s[H_FIRST:P, g, half_cols(a)],
-                start=(g == 0), stop=(g == LAST),
+                start=(g == ORDER[a][0]), stop=(g == ORDER[a][-1]),
             )
 
         def add_prem(a, c):
             nc.vector.tensor_tensor(out=y_sb[:, c, half_cols(a)], in0=acc[a, c][:], in1=y_sb[:, c, half_cols(a)], op=ADD)
 
-        for g in range(G):
+        for g in ORDER[0]:
             for c in range(LINES):
                 mix(0, c, g)
         for c in range(LINES):
-            add_prem(0, c)
-        for c in range(LINES):
             acc[1, c] = bank((2 * RING + LINES + c) % BANKS)
-            for g in range(G):
+            for g in ORDER[1]:
                 mix(1, c, g)
+            add_prem(0, c)
             add_prem(1, c)
-            if (c + 1) % Y_STORE == 0:
-                rows = slice(c + 1 - Y_STORE, c + 1)
+            if c + 1 in Y_STORES:
+                rows = slice(((0,) + Y_STORES)[Y_STORES.index(c + 1)], c + 1)
                 nc.sync.dma_start(out=out_rows[:, rows, :], in_=y_sb[:, rows, :])

@@ -28,16 +28,17 @@ LINES = N // P
 QUAD = 32
 BLOCKS = 16
 SPREAD = P // BLOCKS
-BIAS_PITCH = 8
-H_FIRST = 4
+H_FIRST, W3_FIRST = 4, 8
+GPSIMD_PIECE = 512
 LEAD = 2
 RING = 3
 BANKS = 8
 GATE_BUFS = 10
-Y_STORES = (2, 4, 5, 6)
-ORDER = ((1, 0, LAST), (0, LAST, 1))
-V_COLS, W2_COLS, W3_COLS = slice(0, S), slice(S, S + H), slice(S + H, S + H + G * N)
-SCALE_COLS = S + H + G * N
+Y_STORES = ((3, 6), (2, 4, 5, 6))
+SCALAR_WEAVES = ((1, 0), (0, 1), (1, 1))
+ORDER = ((0, 1, LAST), (0, LAST, 1))
+V_COLS, W2_COLS = slice(0, S), slice(S, S + H)
+SCALE_COLS = S + H
 
 
 def tile_list_treaty_pricing_kernel(
@@ -69,28 +70,24 @@ def tile_list_treaty_pricing_kernel(
 
         offsets = held.tile([P, S // 16], U16, name="offsets")
         nc.sync.dma_start(offsets[:], offs)
-        tab_s = zeroed_plane("tab_s", [P, T])
-        w2s_raw = zeroed_plane("w2s_raw", [P, H])
-        planes = zeroed_plane("planes", [P, SCALE_COLS])
-        staged = keep("staged", [P, SCALE_COLS], U8)
-        nc.sync.dma_start(
-            out=staged[0:P:SPREAD, W3_COLS].rearrange("q (g n) -> q g n", g=G).bitcast(I32),
-            in_=w3_scales.rearrange("g q n -> q g n").bitcast(I32),
-        )
         w2_raw = keep("w2_raw", [P, 2 * H], U8)
         nc.sync.dma_start(out=w2_raw[:].bitcast(I32), in_=w2_words[0].bitcast(I32))
-        nc.sync.dma_start(out=tab_s[0:P:SPREAD].bitcast(I32), in_=tab_scales[0].bitcast(I32))
+        w2s_raw = zeroed_plane("w2s_raw", [P, H])
+        tab_s = zeroed_plane("tab_s", [P, T])
+        bias_rows = keep("bias_rows", [P, G, P], F32)
+        nc.vector.memset(bias_rows[:], 0.0)
+        planes = zeroed_plane("planes", [P, SCALE_COLS])
+        staged = keep("staged", [P, SCALE_COLS], U8)
         nc.sync.dma_start(out=w2s_raw[0:P:SPREAD].bitcast(I32), in_=w2_scales[0].bitcast(I32))
+        nc.sync.dma_start(out=tab_s[0:P:SPREAD].bitcast(I32), in_=tab_scales[0].bitcast(I32))
+        for b, vector in enumerate((att, load)):
+            nc.sync.dma_start(out=bias_rows[b:P:QUAD], in_=vector.rearrange("(g q c) -> q g c", g=G, c=P))
         tab_w = keep("tab_w", [P, T], U32)
         nc.sync.dma_start(out=tab_w[:].bitcast(I32), in_=tab_words[0].rearrange("p n t -> p (n t)").bitcast(I32))
-        att_sb = keep("att_sb", [P, G, BIAS_PITCH], F32)
-        nc.sync.dma_start(out=att_sb[:, :, 0:PACK], in_=att.rearrange("(g p t) -> p g t", p=P, t=PACK))
-        load_sb = keep("load_sb", [P, G, BIAS_PITCH], F32)
-        nc.sync.dma_start(out=load_sb[:, :, 0:PACK], in_=load.rearrange("(g p t) -> p g t", p=P, t=PACK))
         w1_rows = w1.rearrange("(p j) c -> p j c", j=PACK)
-        w1_head = keep("w1_head", [P, PACK, GROUP], F32)
-        w1_rest = keep("w1_rest", [P, PACK, H - GROUP], F32)
-        nc.sync.dma_start(out=w1_head[:], in_=w1_rows[:, :, 0:GROUP])
+        w1_head = [keep("w1_head%d" % u, [P, PACK, GROUP // 2], F32) for u in range(2)]
+        w1_raw = {g: keep("w1_raw%d" % g, [P, PACK, GROUP], F32) for g in range(1, G)}
+        nc.sync.dma_start(out=w1_head[0][:], in_=w1_rows[:, :, 0 : GROUP // 2])
 
         def deal(out, in_):
             nc.vector.tensor_copy(
@@ -98,20 +95,29 @@ def tile_list_treaty_pricing_kernel(
                 in_=in_.rearrange("p (g m t) -> p t g m", g=G, t=PACK),
             )
 
+        deal(staged[:, W2_COLS], w2s_raw[:])
         picked_s = keep("picked_s", [P, S], U8)
         nc.vector.tensor_copy(picked_s[:], tab_s[:].indirect(offsets[:]))
         nc.vector.tensor_copy(out=staged[:, V_COLS].bitcast(I32), in_=picked_s[:].bitcast(I32))
-        deal(staged[:, W2_COLS], w2s_raw[:])
         for r in range(PACK):
             nc.sync.dma_start(out=live_rows(planes, 0, r), in_=live_rows(staged, 0, SPREAD * r))
         v_s = planes[:, V_COLS]
         w2_s = planes[:, W2_COLS].rearrange("p (g c) -> p g c", g=G)
-        w3_s = planes[:, W3_COLS].rearrange("p (g n) -> p g n", g=G)
-        nc.sync.dma_start(out=w1_rest[:], in_=w1_rows[:, :, GROUP:H])
+        nc.sync.dma_start(out=w1_head[1][:], in_=w1_rows[:, :, GROUP // 2 : GROUP])
+        for g in range(1, G):
+            nc.sync.dma_start(out=w1_raw[g][:], in_=w1_rows[:, :, GROUP * g : GROUP * (g + 1)])
         w3_w = keep("w3_w", [P, G, N], U32)
+        w3_s = zeroed_plane("w3_s", [P, G, N])
+        for r in range(PACK):
+            nc.sync.dma_start(
+                out=live_rows(w3_s, W3_FIRST, r),
+                in_=w3_scales[:, r:BLOCKS:PACK, :].rearrange("g q n -> q g n").bitcast(I32),
+            )
         nc.sync.dma_start(out=w3_w[:].bitcast(I32), in_=w3_words.rearrange("g p n t -> p g (n t)").bitcast(I32))
-        y_sb = keep("y_sb", [P, LINES, S], F32)
-        nc.sync.dma_start(out=y_sb[:], in_=prem.rearrange("(c p) j -> p c j", p=P))
+        prem_rows = prem.rearrange("(c p) j -> p c j", p=P)
+        y_sb = [keep("y%d" % a, [P, LINES, HALF], F32) for a in range(HALVES)]
+        for a in range(HALVES):
+            nc.sync.dma_start(out=y_sb[a][:], in_=prem_rows[:, :, half_cols(a)])
 
         w2_w = keep("w2_w", [P, 2 * H], U8)
         v_w = [keep("v_w%d" % a, [P, HALF], U32) for a in range(HALVES)]
@@ -126,33 +132,55 @@ def tile_list_treaty_pricing_kernel(
             )
 
         deal(w2_w[:].bitcast(U16), w2_raw[:].bitcast(U16))
+        bias_dealt = keep("bias_dealt", [P, G * P], F32)
+        bias = keep("bias", [P, G * P], F32)
+        deal(bias_dealt[:], bias_rows[:].rearrange("p g c -> p (g c)"))
+        for cols in (slice(0, 2 * P), slice(2 * P, G * P)):
+            nc.vector.transpose(out=bias[:, cols], in_=bias_dealt[:, cols])
+
+        def bias_of(b, g, t):
+            col = QUAD * (PACK * g + t) + b
+            return bias[:, col : col + 1]
+
         for a in range(HALVES):
             nc.vector.tensor_copy(v_w[a][:], tab_w[:].indirect(offsets[:, HALF // 16 * a : HALF // 16 * (a + 1)]))
 
-        def round_w1(copy, g, source, m0, m1):
+        def round_w1(copy, g, u, source):
             copy(
-                out=w1_b[g][:, :, m0:m1, :].rearrange("p t m j -> p m j t"),
-                in_=source[:, :, PACK * m0 : PACK * m1].rearrange("p j (m t) -> p m j t", t=PACK),
+                out=w1_b[g][:, :, P // 2 * u : P // 2 * (u + 1), :].rearrange("p t m j -> p m j t"),
+                in_=source.rearrange("p j (m t) -> p m j t", t=PACK),
             )
 
-        round_w1(nc.vector.tensor_copy, 0, w1_head[:], 0, P)
+        for u in range(2):
+            round_w1(nc.vector.tensor_copy, 0, u, w1_head[u][:])
         quantize_w1(0)
+
+        def gpsimd_round(out, in_):
+            nc.gpsimd.tensor_scalar(out=out, in0=in_, scalar1=1.0, scalar2=0.0, op0=MULT, op1=ADD)
+
+        piece = GPSIMD_PIECE // (PACK * PACK)
+        for m0 in range(0, P, piece):
+            c0 = PACK * m0
+            gpsimd_round(
+                w1_b[LAST][:, :, m0 : m0 + piece, :].rearrange("p t m j -> p m t j"),
+                w1_raw[LAST][:, :, c0 : c0 + PACK * piece].rearrange("p j (m t) -> p m t j", t=PACK),
+            )
 
         h_sb = [keep("h%d" % g, [P, PACK, S], F32) for g in range(G)]
         h_w = keep("h_w", [P, G, S], U32)
         h_s = keep("h_s", [P, G, S], U8)
-        woven = {(g, a): keep("woven%d%d" % (g, a), [P, HALF, PACK], BF16) for g in range(G) for a in range(HALVES)}
+        woven = {(g, a): keep("woven%d%d" % (g, a), [P, HALF, PACK], BF16)[:] for g, a in ((0, 0), (LAST, 0), (LAST, 1))}
 
         def weave(copy, g, a):
             copy(
-                out=woven[g, a][:].rearrange("p (c i) t -> p c t i", i=4),
+                out=woven[g, a].rearrange("p (c i) t -> p c t i", i=4),
                 in_=h_sb[g][:, :, half_cols(a)].rearrange("p t (c i) -> p c t i", i=4),
             )
 
         def quantize_h(g, a):
             nc.vector.quantize_mx(
                 out=h_w[:, g, half_cols(a)].bitcast(FP8X4), scales=h_s[H_FIRST:P, g, half_cols(a)],
-                in_=woven[g, a][:].rearrange("p c t -> p (c t)"),
+                in_=woven[g, a].rearrange("p c t -> p (c t)"),
             )
 
         steps = [(g, a, t) for g in range(LAST) for t in range(PACK) for a in range(HALVES)]
@@ -168,7 +196,7 @@ def tile_list_treaty_pricing_kernel(
                 rhs=v_w[a][:].bitcast(FP8X4), rhs_scale=v_s[:, half_cols(a)], start=True, stop=True,
             )
             gates[step] = gate_pool.tile([P, HALF], F32, name="gate")
-            nc.scalar.activation(out=gates[step][:], in_=hit[:], func=SIGMOID, bias=att_sb[:, g, t : t + 1])
+            nc.scalar.activation(out=gates[step][:], in_=hit[:], func=SIGMOID, bias=bias_of(0, g, t))
 
         for step in range(LEAD):
             make_gate(step)
@@ -182,37 +210,36 @@ def tile_list_treaty_pricing_kernel(
                 rhs=v_w[a][:].bitcast(FP8X4), rhs_scale=v_s[:, half_cols(a)], start=True, stop=True,
             )
             nc.vector.scalar_tensor_tensor(
-                out=h_sb[g][:, t, half_cols(a)], in0=loss[:], scalar=load_sb[:, g, t : t + 1], in1=gates[step][:],
+                out=h_sb[g][:, t, half_cols(a)], in0=loss[:], scalar=bias_of(1, g, t), in1=gates[step][:],
                 op0=ADD, op1=MULT,
             )
             if (a, t) == (HALVES - 1, PACK - 1):
                 nc.sync.dma_start(
                     out=out_1[GROUP * g : GROUP * (g + 1), :].rearrange("(p t) j -> p t j", t=PACK), in_=h_sb[g][:]
                 )
-            if (g, a, t) == (0, 0, 2):
-                round_w1(nc.vector.tensor_copy, 1, w1_rest[:, :, 0:GROUP], 0, P)
-            if (g, t) == (0, PACK - 1):
-                round_w1(nc.scalar.copy, LAST, w1_rest[:, :, GROUP:], P // 2 * a, P // 2 * (a + 1))
+            if (g, t) == (0, 0):
+                round_w1(nc.scalar.copy, 1, a, w1_raw[1][:, :, GROUP // 2 * a : GROUP // 2 * (a + 1)])
+            if (g, a, t) == (0, HALVES - 1, PACK - 1):
+                cols = GPSIMD_PIECE // PACK
+                for c in range(0, HALF, cols):
+                    gpsimd_round(woven[0, 0][:, c : c + cols, :], h_sb[0][:, :, c : c + cols].rearrange("p t c -> p c t"))
             if g < LAST and (a, t) == (HALVES - 1, PACK - 2):
                 quantize_w1(g + 1)
+            if (g, a, t) == (LAST, HALVES - 1, 0):
+                quantize_h(0, 0)
 
-        for g, a in ((0, 0), (0, 1), (1, 1)):
+        late = keep("w2_w", [P, len(SCALAR_WEAVES), HALF, PACK], BF16)
+        for i, (g, a) in enumerate(SCALAR_WEAVES):
+            woven[g, a] = late[:, i]
             weave(nc.scalar.copy, g, a)
-        weave(nc.vector.tensor_copy, 1, 0)
-        quantize_h(1, 0)
         weave(nc.vector.tensor_copy, LAST, 0)
-        quantize_h(0, 0)
+        quantize_h(1, 0)
         quantize_h(LAST, 0)
         words = out_2.rearrange("g p m t -> p g (m t)").bitcast(I32)
         nc.sync.dma_start(out=words[:, :, half_cols(0)], in_=h_w[:, :, half_cols(0)].bitcast(I32))
         weave(nc.vector.tensor_copy, LAST, 1)
         for g in ORDER[1]:
             quantize_h(g, 1)
-        nc.sync.dma_start(out=words[:, :, half_cols(1)], in_=h_w[:, :, half_cols(1)].bitcast(I32))
-        for r in range(PACK):
-            nc.sync.dma_start(
-                out=out_3[:, r:BLOCKS:PACK, :].rearrange("g q m -> q g m").bitcast(I32), in_=live_rows(h_s, H_FIRST, r)
-            )
 
         out_rows = out_0.rearrange("(c p) j -> p c j", p=P)
         acc = {(a, c): bank((2 * RING + LINES * a + c) % BANKS) for a in range(1) for c in range(LINES)}
@@ -220,23 +247,35 @@ def tile_list_treaty_pricing_kernel(
         def mix(a, c, g):
             lines = slice(P * c, P * (c + 1))
             nc.tensor.matmul_mx(
-                out=acc[a, c][:], lhsT=w3_w[:, g, lines].bitcast(FP8X4), lhsT_scale=w3_s[:, g, lines],
+                out=acc[a, c][:], lhsT=w3_w[:, g, lines].bitcast(FP8X4), lhsT_scale=w3_s[W3_FIRST:P, g, lines],
                 rhs=h_w[:, g, half_cols(a)].bitcast(FP8X4), rhs_scale=h_s[H_FIRST:P, g, half_cols(a)],
                 start=(g == ORDER[a][0]), stop=(g == ORDER[a][-1]),
             )
 
         def add_prem(a, c):
-            nc.vector.tensor_tensor(out=y_sb[:, c, half_cols(a)], in0=acc[a, c][:], in1=y_sb[:, c, half_cols(a)], op=ADD)
+            nc.vector.tensor_tensor(out=y_sb[a][:, c, :], in0=acc[a, c][:], in1=y_sb[a][:, c, :], op=ADD)
 
-        for g in ORDER[0]:
-            for c in range(LINES):
+        for c in range(LINES):
+            mix(0, c, ORDER[0][0])
+        for c in range(LINES):
+            for g in ORDER[0][1:]:
                 mix(0, c, g)
+        def store_y(a, c):
+            if c + 1 in Y_STORES[a]:
+                rows = slice(((0,) + Y_STORES[a])[Y_STORES[a].index(c + 1)], c + 1)
+                nc.sync.dma_start(out=out_rows[:, rows, half_cols(a)], in_=y_sb[a][:, rows, :])
+
+        for c in range(LINES):
+            add_prem(0, c)
+            store_y(0, c)
+        nc.sync.dma_start(out=words[:, :, half_cols(1)], in_=h_w[:, :, half_cols(1)].bitcast(I32))
+        for r in range(PACK):
+            nc.sync.dma_start(
+                out=out_3[:, r:BLOCKS:PACK, :].rearrange("g q m -> q g m").bitcast(I32), in_=live_rows(h_s, H_FIRST, r)
+            )
         for c in range(LINES):
             acc[1, c] = bank((2 * RING + LINES + c) % BANKS)
             for g in ORDER[1]:
                 mix(1, c, g)
-            add_prem(0, c)
             add_prem(1, c)
-            if c + 1 in Y_STORES:
-                rows = slice(((0,) + Y_STORES)[Y_STORES.index(c + 1)], c + 1)
-                nc.sync.dma_start(out=out_rows[:, rows, :], in_=y_sb[:, rows, :])
+            store_y(1, c)

@@ -28,6 +28,7 @@ LINES = N // P
 QUAD = 32
 BLOCKS = 16
 SPREAD = P // BLOCKS
+BIAS_PITCH = 8
 H_FIRST, W3_FIRST = 4, 8
 GPSIMD_PIECE = 512
 LEAD = 2
@@ -37,8 +38,6 @@ GATE_BUFS = 10
 Y_STORES = ((3, 6), (2, 4, 5, 6))
 SCALAR_WEAVES = ((1, 0), (0, 1), (1, 1))
 ORDER = ((0, 1, LAST), (0, LAST, 1))
-V_COLS, W2_COLS = slice(0, S), slice(S, S + H)
-SCALE_COLS = S + H
 
 
 def tile_list_treaty_pricing_kernel(
@@ -70,40 +69,30 @@ def tile_list_treaty_pricing_kernel(
 
         offsets = held.tile([P, S // 16], U16, name="offsets")
         nc.sync.dma_start(offsets[:], offs)
-        w2_raw = keep("w2_raw", [P, 2 * H], U8)
-        nc.sync.dma_start(out=w2_raw[:].bitcast(I32), in_=w2_words[0].bitcast(I32))
-        w2s_raw = zeroed_plane("w2s_raw", [P, H])
-        tab_s = zeroed_plane("tab_s", [P, T])
-        bias_rows = keep("bias_rows", [P, G, P], F32)
-        nc.vector.memset(bias_rows[:], 0.0)
-        planes = zeroed_plane("planes", [P, SCALE_COLS])
-        staged = keep("staged", [P, SCALE_COLS], U8)
-        nc.sync.dma_start(out=w2s_raw[0:P:SPREAD].bitcast(I32), in_=w2_scales[0].bitcast(I32))
-        nc.sync.dma_start(out=tab_s[0:P:SPREAD].bitcast(I32), in_=tab_scales[0].bitcast(I32))
-        for b, vector in enumerate((att, load)):
-            nc.sync.dma_start(out=bias_rows[b:P:QUAD], in_=vector.rearrange("(g q c) -> q g c", g=G, c=P))
-        tab_w = keep("tab_w", [P, T], U32)
-        nc.sync.dma_start(out=tab_w[:].bitcast(I32), in_=tab_words[0].rearrange("p n t -> p (n t)").bitcast(I32))
+
         w1_rows = w1.rearrange("(p j) c -> p j c", j=PACK)
         w1_head = [keep("w1_head%d" % u, [P, PACK, GROUP // 2], F32) for u in range(2)]
         w1_raw = {g: keep("w1_raw%d" % g, [P, PACK, GROUP], F32) for g in range(1, G)}
         nc.sync.dma_start(out=w1_head[0][:], in_=w1_rows[:, :, 0 : GROUP // 2])
-
-        def deal(out, in_):
-            nc.vector.tensor_copy(
-                out=out.rearrange("p (g t m) -> p t g m", g=G, t=PACK),
-                in_=in_.rearrange("p (g m t) -> p t g m", g=G, t=PACK),
-            )
-
-        deal(staged[:, W2_COLS], w2s_raw[:])
-        picked_s = keep("picked_s", [P, S], U8)
-        nc.vector.tensor_copy(picked_s[:], tab_s[:].indirect(offsets[:]))
-        nc.vector.tensor_copy(out=staged[:, V_COLS].bitcast(I32), in_=picked_s[:].bitcast(I32))
+        tab_s = zeroed_plane("tab_s", [P, T])
+        nc.sync.dma_start(out=tab_s[0:P:SPREAD].bitcast(I32), in_=tab_scales[0].bitcast(I32))
+        w2_raw = keep("w2_raw", [P, 2 * H], U8)
+        nc.sync.dma_start(out=w2_raw[:].bitcast(I32), in_=w2_words[0].bitcast(I32))
+        w2s_raw = zeroed_plane("w2s_raw", [P, H])
         for r in range(PACK):
-            nc.sync.dma_start(out=live_rows(planes, 0, r), in_=live_rows(staged, 0, SPREAD * r))
-        v_s = planes[:, V_COLS]
-        w2_s = planes[:, W2_COLS].rearrange("p (g c) -> p g c", g=G)
+            nc.sync.dma_start(out=live_rows(w2s_raw, 0, r), in_=w2_scales[0, r:BLOCKS:PACK, :].bitcast(I32))
+        tab_w = keep("tab_w", [P, T], U32)
+        nc.sync.dma_start(out=tab_w[:].bitcast(I32), in_=tab_words[0].rearrange("p n t -> p (n t)").bitcast(I32))
+        att_sb = keep("att_sb", [P, G, BIAS_PITCH], F32)
+        nc.sync.dma_start(out=att_sb[:, :, 0:PACK], in_=att.rearrange("(g p t) -> p g t", p=P, t=PACK))
+        picked_s = keep("picked_s", [P, S], U8)
+        v_s = zeroed_plane("v_s", [P, S])
+        nc.vector.tensor_copy(picked_s[:], tab_s[:].indirect(offsets[:]))
+        for r in range(PACK):
+            nc.sync.dma_start(out=live_rows(v_s, 0, r), in_=live_rows(picked_s, 0, SPREAD * r))
         nc.sync.dma_start(out=w1_head[1][:], in_=w1_rows[:, :, GROUP // 2 : GROUP])
+        load_sb = keep("load_sb", [P, G, BIAS_PITCH], F32)
+        nc.sync.dma_start(out=load_sb[:, :, 0:PACK], in_=load.rearrange("(g p t) -> p g t", p=P, t=PACK))
         for g in range(1, G):
             nc.sync.dma_start(out=w1_raw[g][:], in_=w1_rows[:, :, GROUP * g : GROUP * (g + 1)])
         w3_w = keep("w3_w", [P, G, N], U32)
@@ -119,31 +108,17 @@ def tile_list_treaty_pricing_kernel(
         for a in range(HALVES):
             nc.sync.dma_start(out=y_sb[a][:], in_=prem_rows[:, :, half_cols(a)])
 
-        w2_w = keep("w2_w", [P, 2 * H], U8)
+        w2_w = [keep("w2_w%d" % g, [P, 2 * GROUP], U8) for g in range(G)]
+        w2_s = [keep("w2_s%d" % g, [P, GROUP], U8) for g in range(G)]
         v_w = [keep("v_w%d" % a, [P, HALF], U32) for a in range(HALVES)]
         w1_b = [keep("w1_b%d" % g, [P, PACK, P, PACK], BF16) for g in range(G)]
         w1_w = [keep("w1_w%d" % g, [P, GROUP], U32) for g in range(G)]
         w1_s = [keep("w1_s%d" % g, [P, GROUP], U8) for g in range(G)]
 
-        def quantize_w1(g):
-            nc.vector.quantize_mx(
-                out=w1_w[g][:].bitcast(FP8X4), scales=w1_s[g][:],
-                in_=w1_b[g][:].rearrange("p t m j -> p (t m j)"),
+        def deal(out, in_):
+            nc.vector.tensor_copy(
+                out=out.rearrange("p (t m) -> p t m", t=PACK), in_=in_.rearrange("p (m t) -> p t m", t=PACK)
             )
-
-        deal(w2_w[:].bitcast(U16), w2_raw[:].bitcast(U16))
-        bias_dealt = keep("bias_dealt", [P, G * P], F32)
-        bias = keep("bias", [P, G * P], F32)
-        deal(bias_dealt[:], bias_rows[:].rearrange("p g c -> p (g c)"))
-        for cols in (slice(0, 2 * P), slice(2 * P, G * P)):
-            nc.vector.transpose(out=bias[:, cols], in_=bias_dealt[:, cols])
-
-        def bias_of(b, g, t):
-            col = QUAD * (PACK * g + t) + b
-            return bias[:, col : col + 1]
-
-        for a in range(HALVES):
-            nc.vector.tensor_copy(v_w[a][:], tab_w[:].indirect(offsets[:, HALF // 16 * a : HALF // 16 * (a + 1)]))
 
         def round_w1(copy, g, u, source):
             copy(
@@ -151,8 +126,19 @@ def tile_list_treaty_pricing_kernel(
                 in_=source.rearrange("p j (m t) -> p m j t", t=PACK),
             )
 
-        for u in range(2):
-            round_w1(nc.vector.tensor_copy, 0, u, w1_head[u][:])
+        def quantize_w1(g):
+            nc.vector.quantize_mx(
+                out=w1_w[g][:].bitcast(FP8X4), scales=w1_s[g][:],
+                in_=w1_b[g][:].rearrange("p t m j -> p (t m j)"),
+            )
+
+        round_w1(nc.vector.tensor_copy, 0, 0, w1_head[0][:])
+        for g in range(G):
+            deal(w2_w[g][:].bitcast(U16), w2_raw[:, 2 * GROUP * g : 2 * GROUP * (g + 1)].bitcast(U16))
+            deal(w2_s[g][:], w2s_raw[:, GROUP * g : GROUP * (g + 1)])
+        for a in range(HALVES):
+            nc.vector.tensor_copy(v_w[a][:], tab_w[:].indirect(offsets[:, HALF // 16 * a : HALF // 16 * (a + 1)]))
+        round_w1(nc.vector.tensor_copy, 0, 1, w1_head[1][:])
         quantize_w1(0)
 
         def gpsimd_round(out, in_):
@@ -191,12 +177,12 @@ def tile_list_treaty_pricing_kernel(
             g, a, t = steps[step]
             hit = bank(step % RING)
             nc.tensor.matmul_mx(
-                out=hit[:], lhsT=w2_w[:, 2 * (GROUP * g + P * t) : 2 * (GROUP * g + P * (t + 1))].bitcast(FP4X4),
-                lhsT_scale=w2_s[:, g, P * t : P * (t + 1)],
+                out=hit[:], lhsT=w2_w[g][:, 2 * P * t : 2 * P * (t + 1)].bitcast(FP4X4),
+                lhsT_scale=w2_s[g][:, P * t : P * (t + 1)],
                 rhs=v_w[a][:].bitcast(FP8X4), rhs_scale=v_s[:, half_cols(a)], start=True, stop=True,
             )
             gates[step] = gate_pool.tile([P, HALF], F32, name="gate")
-            nc.scalar.activation(out=gates[step][:], in_=hit[:], func=SIGMOID, bias=bias_of(0, g, t))
+            nc.scalar.activation(out=gates[step][:], in_=hit[:], func=SIGMOID, bias=att_sb[:, g, t : t + 1])
 
         for step in range(LEAD):
             make_gate(step)
@@ -210,28 +196,28 @@ def tile_list_treaty_pricing_kernel(
                 rhs=v_w[a][:].bitcast(FP8X4), rhs_scale=v_s[:, half_cols(a)], start=True, stop=True,
             )
             nc.vector.scalar_tensor_tensor(
-                out=h_sb[g][:, t, half_cols(a)], in0=loss[:], scalar=bias_of(1, g, t), in1=gates[step][:],
+                out=h_sb[g][:, t, half_cols(a)], in0=loss[:], scalar=load_sb[:, g, t : t + 1], in1=gates[step][:],
                 op0=ADD, op1=MULT,
             )
             if (a, t) == (HALVES - 1, PACK - 1):
                 nc.sync.dma_start(
                     out=out_1[GROUP * g : GROUP * (g + 1), :].rearrange("(p t) j -> p t j", t=PACK), in_=h_sb[g][:]
                 )
-            if (g, t) == (0, 0):
-                round_w1(nc.scalar.copy, 1, a, w1_raw[1][:, :, GROUP // 2 * a : GROUP // 2 * (a + 1)])
+            if (g, t) == (0, 1):
+                copy = (nc.scalar.copy, nc.vector.tensor_copy)[a]
+                round_w1(copy, 1, a, w1_raw[1][:, :, GROUP // 2 * a : GROUP // 2 * (a + 1)])
             if (g, a, t) == (0, HALVES - 1, PACK - 1):
                 cols = GPSIMD_PIECE // PACK
                 for c in range(0, HALF, cols):
                     gpsimd_round(woven[0, 0][:, c : c + cols, :], h_sb[0][:, :, c : c + cols].rearrange("p t c -> p c t"))
             if g < LAST and (a, t) == (HALVES - 1, PACK - 2):
                 quantize_w1(g + 1)
-            if (g, a, t) == (LAST, HALVES - 1, 0):
-                quantize_h(0, 0)
 
-        late = keep("w2_w", [P, len(SCALAR_WEAVES), HALF, PACK], BF16)
+        late = keep("w2_w%d" % LAST, [P, len(SCALAR_WEAVES), HALF, PACK], BF16)
         for i, (g, a) in enumerate(SCALAR_WEAVES):
             woven[g, a] = late[:, i]
             weave(nc.scalar.copy, g, a)
+        quantize_h(0, 0)
         weave(nc.vector.tensor_copy, LAST, 0)
         quantize_h(1, 0)
         quantize_h(LAST, 0)

@@ -35,9 +35,8 @@ LEAD = 2
 RING = 3
 BANKS = 8
 GATE_BUFS = 10
-Y_STORES = ((3, 6), (2, 4, 5, 6))
-SCALAR_WEAVES = ((1, 0), (0, 1), (1, 1))
-ORDER = ((0, 1, LAST), (0, LAST, 1))
+Y_STORES = ((2, 4, 6), (2, 4, 5, 6))
+SCALAR_WEAVES = ((1, 0), (0, 1), (1, 1), (LAST, 1))
 
 
 def tile_list_treaty_pricing_kernel(
@@ -153,9 +152,9 @@ def tile_list_treaty_pricing_kernel(
             )
 
         h_sb = [keep("h%d" % g, [P, PACK, S], F32) for g in range(G)]
-        h_w = keep("h_w", [P, G, S], U32)
-        h_s = keep("h_s", [P, G, S], U8)
-        woven = {(g, a): keep("woven%d%d" % (g, a), [P, HALF, PACK], BF16)[:] for g, a in ((0, 0), (LAST, 0), (LAST, 1))}
+        h_w = [keep("h_w%d" % a, [P, G, HALF], U32) for a in range(HALVES)]
+        h_s = [keep("h_s%d" % a, [P, G, HALF], U8) for a in range(HALVES)]
+        woven = {(g, a): keep("woven%d%d" % (g, a), [P, HALF, PACK], BF16)[:] for g, a in ((0, 0), (LAST, 0))}
 
         def weave(copy, g, a):
             copy(
@@ -165,12 +164,11 @@ def tile_list_treaty_pricing_kernel(
 
         def quantize_h(g, a):
             nc.vector.quantize_mx(
-                out=h_w[:, g, half_cols(a)].bitcast(FP8X4), scales=h_s[H_FIRST:P, g, half_cols(a)],
+                out=h_w[a][:, g, :].bitcast(FP8X4), scales=h_s[a][H_FIRST:P, g, :],
                 in_=woven[g, a].rearrange("p c t -> p (c t)"),
             )
 
-        steps = [(g, a, t) for g in range(LAST) for t in range(PACK) for a in range(HALVES)]
-        steps = steps + [(LAST, a, t) for a in range(HALVES) for t in range(PACK)]
+        steps = [(g, a, t) for g in range(G) for t in range(PACK) for a in range(HALVES)]
         gates = {}
 
         def make_gate(step):
@@ -199,10 +197,9 @@ def tile_list_treaty_pricing_kernel(
                 out=h_sb[g][:, t, half_cols(a)], in0=loss[:], scalar=load_sb[:, g, t : t + 1], in1=gates[step][:],
                 op0=ADD, op1=MULT,
             )
-            if (a, t) == (HALVES - 1, PACK - 1):
-                nc.sync.dma_start(
-                    out=out_1[GROUP * g : GROUP * (g + 1), :].rearrange("(p t) j -> p t j", t=PACK), in_=h_sb[g][:]
-                )
+            if a == HALVES - 1 and t % 2 == 1:
+                rows = out_1[GROUP * g : GROUP * (g + 1), :].rearrange("(p t) j -> p t j", t=PACK)
+                nc.sync.dma_start(out=rows[:, t - 1 : t + 1, :], in_=h_sb[g][:, t - 1 : t + 1, :])
             if (g, t) == (0, 1):
                 copy = (nc.scalar.copy, nc.vector.tensor_copy)[a]
                 round_w1(copy, 1, a, w1_raw[1][:, :, GROUP // 2 * a : GROUP // 2 * (a + 1)])
@@ -222,46 +219,51 @@ def tile_list_treaty_pricing_kernel(
         quantize_h(1, 0)
         quantize_h(LAST, 0)
         words = out_2.rearrange("g p m t -> p g (m t)").bitcast(I32)
-        nc.sync.dma_start(out=words[:, :, half_cols(0)], in_=h_w[:, :, half_cols(0)].bitcast(I32))
-        weave(nc.vector.tensor_copy, LAST, 1)
-        for g in ORDER[1]:
-            quantize_h(g, 1)
+
+        def store_words(a, groups):
+            nc.sync.dma_start(out=words[:, groups, half_cols(a)], in_=h_w[a][:, groups, :].bitcast(I32))
+
+        def store_scales(a):
+            for r in range(PACK):
+                nc.sync.dma_start(
+                    out=out_3[:, r:BLOCKS:PACK, half_cols(a)].rearrange("g q m -> q g m").bitcast(I32),
+                    in_=live_rows(h_s[a], H_FIRST, r),
+                )
+
+        store_words(0, slice(0, G))
+        store_scales(0)
 
         out_rows = out_0.rearrange("(c p) j -> p c j", p=P)
-        acc = {(a, c): bank((2 * RING + LINES * a + c) % BANKS) for a in range(1) for c in range(LINES)}
+        acc = {}
 
-        def mix(a, c, g):
+        def mix(a, c, groups):
             lines = slice(P * c, P * (c + 1))
-            nc.tensor.matmul_mx(
-                out=acc[a, c][:], lhsT=w3_w[:, g, lines].bitcast(FP8X4), lhsT_scale=w3_s[W3_FIRST:P, g, lines],
-                rhs=h_w[:, g, half_cols(a)].bitcast(FP8X4), rhs_scale=h_s[H_FIRST:P, g, half_cols(a)],
-                start=(g == ORDER[a][0]), stop=(g == ORDER[a][-1]),
-            )
+            if 0 in groups:
+                acc[a, c] = bank((2 * RING + LINES * a + c) % BANKS)
+            for g in groups:
+                nc.tensor.matmul_mx(
+                    out=acc[a, c][:], lhsT=w3_w[:, g, lines].bitcast(FP8X4), lhsT_scale=w3_s[W3_FIRST:P, g, lines],
+                    rhs=h_w[a][:, g, :].bitcast(FP8X4), rhs_scale=h_s[a][H_FIRST:P, g, :],
+                    start=(g == 0), stop=(g == LAST),
+                )
 
-        def add_prem(a, c):
+        def finish(a, c):
             nc.vector.tensor_tensor(out=y_sb[a][:, c, :], in0=acc[a, c][:], in1=y_sb[a][:, c, :], op=ADD)
-
-        for c in range(LINES):
-            mix(0, c, ORDER[0][0])
-        for c in range(LINES):
-            for g in ORDER[0][1:]:
-                mix(0, c, g)
-        def store_y(a, c):
             if c + 1 in Y_STORES[a]:
                 rows = slice(((0,) + Y_STORES[a])[Y_STORES[a].index(c + 1)], c + 1)
                 nc.sync.dma_start(out=out_rows[:, rows, half_cols(a)], in_=y_sb[a][:, rows, :])
 
         for c in range(LINES):
-            add_prem(0, c)
-            store_y(0, c)
-        nc.sync.dma_start(out=words[:, :, half_cols(1)], in_=h_w[:, :, half_cols(1)].bitcast(I32))
-        for r in range(PACK):
-            nc.sync.dma_start(
-                out=out_3[:, r:BLOCKS:PACK, :].rearrange("g q m -> q g m").bitcast(I32), in_=live_rows(h_s, H_FIRST, r)
-            )
+            mix(0, c, (0,))
         for c in range(LINES):
-            acc[1, c] = bank((2 * RING + LINES + c) % BANKS)
-            for g in ORDER[1]:
-                mix(1, c, g)
-            add_prem(1, c)
-            store_y(1, c)
+            mix(0, c, (1, LAST))
+            finish(0, c)
+            if c % 2 == 1:
+                quantize_h(c // 2, 1)
+            if c == 3:
+                store_words(1, slice(0, LAST))
+        store_words(1, slice(LAST, G))
+        store_scales(1)
+        for c in range(LINES):
+            mix(1, c, range(G))
+            finish(1, c)

@@ -66,32 +66,39 @@ def tile_list_treaty_pricing_kernel(
         def live_rows(plane, first, r):
             return plane[first + r : P : QUAD].bitcast(I32)
 
+        def deal(out, in_):
+            nc.vector.tensor_copy(
+                out=out.rearrange("p (g t m) -> p t g m", g=G, t=PACK),
+                in_=in_.rearrange("p (g m t) -> p t g m", g=G, t=PACK),
+            )
+
         offsets = held.tile([P, S // 16], U16, name="offsets")
         nc.sync.dma_start(offsets[:], offs)
-
-        w1_rows = w1.rearrange("(p j) c -> p j c", j=PACK)
-        w1_head = [keep("w1_head%d" % u, [P, PACK, GROUP // 2], F32) for u in range(2)]
-        w1_raw = {g: keep("w1_raw%d" % g, [P, PACK, GROUP], F32) for g in range(1, G)}
-        nc.sync.dma_start(out=w1_head[0][:], in_=w1_rows[:, :, 0 : GROUP // 2])
-        tab_s = zeroed_plane("tab_s", [P, T])
-        nc.sync.dma_start(out=tab_s[0:P:SPREAD].bitcast(I32), in_=tab_scales[0].bitcast(I32))
         w2_raw = keep("w2_raw", [P, 2 * H], U8)
         nc.sync.dma_start(out=w2_raw[:].bitcast(I32), in_=w2_words[0].bitcast(I32))
+        tab_s = zeroed_plane("tab_s", [P, T])
         w2s_raw = zeroed_plane("w2s_raw", [P, H])
-        for r in range(PACK):
-            nc.sync.dma_start(out=live_rows(w2s_raw, 0, r), in_=w2_scales[0, r:BLOCKS:PACK, :].bitcast(I32))
+        planes = zeroed_plane("planes", [P, S + H])
+        nc.sync.dma_start(out=tab_s[0:P:SPREAD].bitcast(I32), in_=tab_scales[0].bitcast(I32))
+        nc.sync.dma_start(out=w2s_raw[0:P:SPREAD].bitcast(I32), in_=w2_scales[0].bitcast(I32))
         tab_w = keep("tab_w", [P, T], U32)
         nc.sync.dma_start(out=tab_w[:].bitcast(I32), in_=tab_words[0].rearrange("p n t -> p (n t)").bitcast(I32))
         att_sb = keep("att_sb", [P, G, BIAS_PITCH], F32)
         nc.sync.dma_start(out=att_sb[:, :, 0:PACK], in_=att.rearrange("(g p t) -> p g t", p=P, t=PACK))
-        picked_s = keep("picked_s", [P, S], U8)
-        v_s = zeroed_plane("v_s", [P, S])
-        nc.vector.tensor_copy(picked_s[:], tab_s[:].indirect(offsets[:]))
-        for r in range(PACK):
-            nc.sync.dma_start(out=live_rows(v_s, 0, r), in_=live_rows(picked_s, 0, SPREAD * r))
-        nc.sync.dma_start(out=w1_head[1][:], in_=w1_rows[:, :, GROUP // 2 : GROUP])
         load_sb = keep("load_sb", [P, G, BIAS_PITCH], F32)
         nc.sync.dma_start(out=load_sb[:, :, 0:PACK], in_=load.rearrange("(g p t) -> p g t", p=P, t=PACK))
+        w1_rows = w1.rearrange("(p j) c -> p j c", j=PACK)
+        w1_raw = [keep("w1_raw%d" % g, [P, PACK, GROUP], F32) for g in range(G)]
+        nc.sync.dma_start(out=w1_raw[0][:], in_=w1_rows[:, :, 0:GROUP])
+        picked_s = keep("picked_s", [P, S], U8)
+        staged = keep("staged", [P, S + H], U8)
+        nc.vector.tensor_copy(picked_s[:], tab_s[:].indirect(offsets[:]))
+        nc.vector.tensor_copy(out=staged[:, 0:S].bitcast(I32), in_=picked_s[:].bitcast(I32))
+        deal(staged[:, S:], w2s_raw[:])
+        for r in range(PACK):
+            nc.sync.dma_start(out=live_rows(planes, 0, r), in_=live_rows(staged, 0, SPREAD * r))
+        v_s = planes[:, 0:S]
+        w2_s = planes[:, S:]
         for g in range(1, G):
             nc.sync.dma_start(out=w1_raw[g][:], in_=w1_rows[:, :, GROUP * g : GROUP * (g + 1)])
         w3_w = keep("w3_w", [P, G, N], U32)
@@ -107,22 +114,16 @@ def tile_list_treaty_pricing_kernel(
         for a in range(HALVES):
             nc.sync.dma_start(out=y_sb[a][:], in_=prem_rows[:, :, half_cols(a)])
 
-        w2_w = [keep("w2_w%d" % g, [P, 2 * GROUP], U8) for g in range(G)]
-        w2_s = [keep("w2_s%d" % g, [P, GROUP], U8) for g in range(G)]
+        w2_w = keep("w2_w", [P, 2 * H], U8)
         v_w = [keep("v_w%d" % a, [P, HALF], U32) for a in range(HALVES)]
         w1_b = [keep("w1_b%d" % g, [P, PACK, P, PACK], BF16) for g in range(G)]
         w1_w = [keep("w1_w%d" % g, [P, GROUP], U32) for g in range(G)]
         w1_s = [keep("w1_s%d" % g, [P, GROUP], U8) for g in range(G)]
 
-        def deal(out, in_):
-            nc.vector.tensor_copy(
-                out=out.rearrange("p (t m) -> p t m", t=PACK), in_=in_.rearrange("p (m t) -> p t m", t=PACK)
-            )
-
-        def round_w1(copy, g, u, source):
+        def round_w1(copy, g, m0, m1):
             copy(
-                out=w1_b[g][:, :, P // 2 * u : P // 2 * (u + 1), :].rearrange("p t m j -> p m j t"),
-                in_=source.rearrange("p j (m t) -> p m j t", t=PACK),
+                out=w1_b[g][:, :, m0:m1, :].rearrange("p t m j -> p m j t"),
+                in_=w1_raw[g][:, :, PACK * m0 : PACK * m1].rearrange("p j (m t) -> p m j t", t=PACK),
             )
 
         def quantize_w1(g):
@@ -131,13 +132,10 @@ def tile_list_treaty_pricing_kernel(
                 in_=w1_b[g][:].rearrange("p t m j -> p (t m j)"),
             )
 
-        round_w1(nc.vector.tensor_copy, 0, 0, w1_head[0][:])
-        for g in range(G):
-            deal(w2_w[g][:].bitcast(U16), w2_raw[:, 2 * GROUP * g : 2 * GROUP * (g + 1)].bitcast(U16))
-            deal(w2_s[g][:], w2s_raw[:, GROUP * g : GROUP * (g + 1)])
+        deal(w2_w[:].bitcast(U16), w2_raw[:].bitcast(U16))
         for a in range(HALVES):
             nc.vector.tensor_copy(v_w[a][:], tab_w[:].indirect(offsets[:, HALF // 16 * a : HALF // 16 * (a + 1)]))
-        round_w1(nc.vector.tensor_copy, 0, 1, w1_head[1][:])
+        round_w1(nc.vector.tensor_copy, 0, 0, P)
         quantize_w1(0)
 
         def gpsimd_round(out, in_):
@@ -173,10 +171,11 @@ def tile_list_treaty_pricing_kernel(
 
         def make_gate(step):
             g, a, t = steps[step]
+            first = GROUP * g + P * t
             hit = bank(step % RING)
             nc.tensor.matmul_mx(
-                out=hit[:], lhsT=w2_w[g][:, 2 * P * t : 2 * P * (t + 1)].bitcast(FP4X4),
-                lhsT_scale=w2_s[g][:, P * t : P * (t + 1)],
+                out=hit[:], lhsT=w2_w[:, 2 * first : 2 * (first + P)].bitcast(FP4X4),
+                lhsT_scale=w2_s[:, first : first + P],
                 rhs=v_w[a][:].bitcast(FP8X4), rhs_scale=v_s[:, half_cols(a)], start=True, stop=True,
             )
             gates[step] = gate_pool.tile([P, HALF], F32, name="gate")
@@ -202,7 +201,7 @@ def tile_list_treaty_pricing_kernel(
                 nc.sync.dma_start(out=rows[:, t - 1 : t + 1, :], in_=h_sb[g][:, t - 1 : t + 1, :])
             if (g, t) == (0, 1):
                 copy = (nc.scalar.copy, nc.vector.tensor_copy)[a]
-                round_w1(copy, 1, a, w1_raw[1][:, :, GROUP // 2 * a : GROUP // 2 * (a + 1)])
+                round_w1(copy, 1, P // 2 * a, P // 2 * (a + 1))
             if (g, a, t) == (0, HALVES - 1, PACK - 1):
                 cols = GPSIMD_PIECE // PACK
                 for c in range(0, HALF, cols):
@@ -210,7 +209,7 @@ def tile_list_treaty_pricing_kernel(
             if g < LAST and (a, t) == (HALVES - 1, PACK - 2):
                 quantize_w1(g + 1)
 
-        late = keep("w2_w%d" % LAST, [P, len(SCALAR_WEAVES), HALF, PACK], BF16)
+        late = keep("w2_w", [P, len(SCALAR_WEAVES), HALF, PACK], BF16)
         for i, (g, a) in enumerate(SCALAR_WEAVES):
             woven[g, a] = late[:, i]
             weave(nc.scalar.copy, g, a)

@@ -142,22 +142,22 @@ def tile_list_treaty_pricing_kernel(
             nc.gpsimd.tensor_scalar(out=out, in0=in_, scalar1=1.0, scalar2=0.0, op0=MULT, op1=ADD)
 
         piece = GPSIMD_PIECE // (PACK * PACK)
-        for m0 in range(0, P, piece):
-            c0 = PACK * m0
-            gpsimd_round(
-                w1_b[LAST][:, :, m0 : m0 + piece, :].rearrange("p t m j -> p m t j"),
-                w1_raw[LAST][:, :, c0 : c0 + PACK * piece].rearrange("p j (m t) -> p m t j", t=PACK),
-            )
+        for g, first in ((1, P // 2), (LAST, 0)):
+            for m0 in range(first, P, piece):
+                gpsimd_round(
+                    w1_b[g][:, :, m0 : m0 + piece, :].rearrange("p t m j -> p m t j"),
+                    w1_raw[g][:, :, PACK * m0 : PACK * (m0 + piece)].rearrange("p j (m t) -> p m t j", t=PACK),
+                )
 
         h_sb = [keep("h%d" % g, [P, PACK, S], F32) for g in range(G)]
         h_w = [keep("h_w%d" % a, [P, G, HALF], U32) for a in range(HALVES)]
         h_s = [keep("h_s%d" % a, [P, G, HALF], U8) for a in range(HALVES)]
         woven = {(g, a): keep("woven%d%d" % (g, a), [P, HALF, PACK], BF16)[:] for g, a in ((0, 0), (LAST, 0))}
 
-        def weave(copy, g, a):
+        def weave(copy, g, a, c0=0, c1=HALF):
             copy(
-                out=woven[g, a].rearrange("p (c i) t -> p c t i", i=4),
-                in_=h_sb[g][:, :, half_cols(a)].rearrange("p t (c i) -> p c t i", i=4),
+                out=woven[g, a][:, c0:c1, :].rearrange("p (c i) t -> p c t i", i=4),
+                in_=h_sb[g][:, :, HALF * a + c0 : HALF * a + c1].rearrange("p t (c i) -> p c t i", i=4),
             )
 
         def quantize_h(g, a):
@@ -199,9 +199,8 @@ def tile_list_treaty_pricing_kernel(
             if a == HALVES - 1 and t % 2 == 1:
                 rows = out_1[GROUP * g : GROUP * (g + 1), :].rearrange("(p t) j -> p t j", t=PACK)
                 nc.sync.dma_start(out=rows[:, t - 1 : t + 1, :], in_=h_sb[g][:, t - 1 : t + 1, :])
-            if (g, t) == (0, 1):
-                copy = (nc.scalar.copy, nc.vector.tensor_copy)[a]
-                round_w1(copy, 1, P // 2 * a, P // 2 * (a + 1))
+            if (g, a, t) == (0, 0, 1):
+                round_w1(nc.scalar.copy, 1, 0, P // 2)
             if (g, a, t) == (0, HALVES - 1, PACK - 1):
                 cols = GPSIMD_PIECE // PACK
                 for c in range(0, HALF, cols):
@@ -212,7 +211,7 @@ def tile_list_treaty_pricing_kernel(
         late = keep("w2_w", [P, len(SCALAR_WEAVES), HALF, PACK], BF16)
         for i, (g, a) in enumerate(SCALAR_WEAVES):
             woven[g, a] = late[:, i]
-            weave(nc.scalar.copy, g, a)
+            weave(nc.scalar.copy, g, a, 0, HALF // 2 if g == LAST else HALF)
         quantize_h(0, 0)
         weave(nc.vector.tensor_copy, LAST, 0)
         quantize_h(1, 0)
@@ -229,6 +228,7 @@ def tile_list_treaty_pricing_kernel(
                     in_=live_rows(h_s[a], H_FIRST, r),
                 )
 
+        weave(nc.vector.tensor_copy, LAST, 1, HALF // 2, HALF)
         store_words(0, slice(0, G))
         store_scales(0)
 

@@ -21,7 +21,6 @@ P = 128
 PACK = 4
 GROUP = P * PACK
 G = H // GROUP
-LAST = G - 1
 HALF = 512
 HALVES = S // HALF
 LINES = N // P
@@ -30,13 +29,13 @@ BLOCKS = 16
 SPREAD = P // BLOCKS
 BIAS_PITCH = 8
 H_FIRST, W3_FIRST = 4, 8
+TAB_LEAD = T // 4
+GPSIMD_SUMS = 3
 GPSIMD_PIECE = 512
-LEAD = 2
+LEAD = 6
 RING = 3
 BANKS = 8
-GATE_BUFS = 10
-Y_STORES = ((2, 4, 6), (2, 4, 5, 6))
-SCALAR_WEAVES = ((1, 0), (0, 1), (1, 1), (LAST, 1))
+Y_STORES = (2, 4, 5, 6)
 
 
 def tile_list_treaty_pricing_kernel(
@@ -46,7 +45,6 @@ def tile_list_treaty_pricing_kernel(
     nc = tc.nc
     with ExitStack() as ctx:
         held = ctx.enter_context(tc.tile_pool(name="held", bufs=1))
-        gate_pool = ctx.enter_context(tc.tile_pool(name="gates", bufs=GATE_BUFS))
         psum = ctx.enter_context(tc.psum_pool(name="psum", bufs=1))
 
         def keep(name, shape, dtype):
@@ -74,31 +72,33 @@ def tile_list_treaty_pricing_kernel(
 
         offsets = held.tile([P, S // 16], U16, name="offsets")
         nc.sync.dma_start(offsets[:], offs)
-        w2_raw = keep("w2_raw", [P, 2 * H], U8)
-        nc.sync.dma_start(out=w2_raw[:].bitcast(I32), in_=w2_words[0].bitcast(I32))
+        tab_w = keep("tab_w", [P, T], U32)
+        tab_rows = tab_words[0].rearrange("p n t -> p (n t)").bitcast(I32)
+        nc.sync.dma_start(out=tab_w[:, 0:TAB_LEAD].bitcast(I32), in_=tab_rows[:, 0:TAB_LEAD])
         tab_s = zeroed_plane("tab_s", [P, T])
         w2s_raw = zeroed_plane("w2s_raw", [P, H])
-        planes = zeroed_plane("planes", [P, S + H])
         nc.sync.dma_start(out=tab_s[0:P:SPREAD].bitcast(I32), in_=tab_scales[0].bitcast(I32))
         nc.sync.dma_start(out=w2s_raw[0:P:SPREAD].bitcast(I32), in_=w2_scales[0].bitcast(I32))
-        tab_w = keep("tab_w", [P, T], U32)
-        nc.sync.dma_start(out=tab_w[:].bitcast(I32), in_=tab_words[0].rearrange("p n t -> p (n t)").bitcast(I32))
+        w2_raw = keep("w2_raw", [P, 2 * H], U8)
+        nc.sync.dma_start(out=w2_raw[:].bitcast(I32), in_=w2_words[0].bitcast(I32))
+        nc.sync.dma_start(out=tab_w[:, TAB_LEAD:].bitcast(I32), in_=tab_rows[:, TAB_LEAD:])
         att_sb = keep("att_sb", [P, G, BIAS_PITCH], F32)
         nc.sync.dma_start(out=att_sb[:, :, 0:PACK], in_=att.rearrange("(g p t) -> p g t", p=P, t=PACK))
         load_sb = keep("load_sb", [P, G, BIAS_PITCH], F32)
         nc.sync.dma_start(out=load_sb[:, :, 0:PACK], in_=load.rearrange("(g p t) -> p g t", p=P, t=PACK))
         w1_rows = w1.rearrange("(p j) c -> p j c", j=PACK)
         w1_raw = [keep("w1_raw%d" % g, [P, PACK, GROUP], F32) for g in range(G)]
-        nc.sync.dma_start(out=w1_raw[0][:], in_=w1_rows[:, :, 0:GROUP])
+        nc.sync.dma_start(out=w1_raw[0][:, 0:2, :], in_=w1_rows[:, 0:2, 0:GROUP])
         picked_s = keep("picked_s", [P, S], U8)
-        staged = keep("staged", [P, S + H], U8)
+        planes = keep("planes", [P, S + H], U8)
         nc.vector.tensor_copy(picked_s[:], tab_s[:].indirect(offsets[:]))
-        nc.vector.tensor_copy(out=staged[:, 0:S].bitcast(I32), in_=picked_s[:].bitcast(I32))
-        deal(staged[:, S:], w2s_raw[:])
-        for r in range(PACK):
-            nc.sync.dma_start(out=live_rows(planes, 0, r), in_=live_rows(staged, 0, SPREAD * r))
+        nc.vector.tensor_copy(out=planes[:, 0:S].bitcast(I32), in_=picked_s[:].bitcast(I32))
+        deal(planes[:, S:], w2s_raw[:])
+        for r in range(1, PACK):
+            nc.sync.dma_start(out=live_rows(planes, 0, r), in_=live_rows(planes, 0, SPREAD * r))
         v_s = planes[:, 0:S]
         w2_s = planes[:, S:]
+        nc.sync.dma_start(out=w1_raw[0][:, 2:PACK, :], in_=w1_rows[:, 2:PACK, 0:GROUP])
         for g in range(1, G):
             nc.sync.dma_start(out=w1_raw[g][:], in_=w1_rows[:, :, GROUP * g : GROUP * (g + 1)])
         w3_w = keep("w3_w", [P, G, N], U32)
@@ -109,10 +109,8 @@ def tile_list_treaty_pricing_kernel(
                 in_=w3_scales[:, r:BLOCKS:PACK, :].rearrange("g q n -> q g n").bitcast(I32),
             )
         nc.sync.dma_start(out=w3_w[:].bitcast(I32), in_=w3_words.rearrange("g p n t -> p g (n t)").bitcast(I32))
-        prem_rows = prem.rearrange("(c p) j -> p c j", p=P)
-        y_sb = [keep("y%d" % a, [P, LINES, HALF], F32) for a in range(HALVES)]
-        for a in range(HALVES):
-            nc.sync.dma_start(out=y_sb[a][:], in_=prem_rows[:, :, half_cols(a)])
+        y_sb = keep("y_sb", [P, LINES, S], F32)
+        nc.sync.dma_start(out=y_sb[:], in_=prem.rearrange("(c p) j -> p c j", p=P))
 
         w2_w = keep("w2_w", [P, 2 * H], U8)
         v_w = [keep("v_w%d" % a, [P, HALF], U32) for a in range(HALVES)]
@@ -142,7 +140,7 @@ def tile_list_treaty_pricing_kernel(
             nc.gpsimd.tensor_scalar(out=out, in0=in_, scalar1=1.0, scalar2=0.0, op0=MULT, op1=ADD)
 
         piece = GPSIMD_PIECE // (PACK * PACK)
-        for g, first in ((1, P // 2), (LAST, 0)):
+        for g, first in ((1, P // 2), (2, 0)):
             for m0 in range(first, P, piece):
                 gpsimd_round(
                     w1_b[g][:, :, m0 : m0 + piece, :].rearrange("p t m j -> p m t j"),
@@ -150,24 +148,24 @@ def tile_list_treaty_pricing_kernel(
                 )
 
         h_sb = [keep("h%d" % g, [P, PACK, S], F32) for g in range(G)]
-        h_w = [keep("h_w%d" % a, [P, G, HALF], U32) for a in range(HALVES)]
-        h_s = [keep("h_s%d" % a, [P, G, HALF], U8) for a in range(HALVES)]
-        woven = {(g, a): keep("woven%d%d" % (g, a), [P, HALF, PACK], BF16)[:] for g, a in ((0, 0), (LAST, 0))}
+        early_w, late_w = keep("early_w", [P, 2, S], U32), keep("late_w", [P, S], U32)
+        h_w = (early_w[:, 0, :], late_w[:], early_w[:, 1, :])
+        h_s = keep("h_s", [P, G, S], U8)
+        woven = {(g, a): keep("woven%d%d" % (g, a), [P, HALF, PACK], BF16)[:] for g, a in ((0, 0), (1, 0), (2, 0), (2, 1))}
 
-        def weave(copy, g, a, c0=0, c1=HALF):
+        def weave(copy, g, a):
             copy(
-                out=woven[g, a][:, c0:c1, :].rearrange("p (c i) t -> p c t i", i=4),
-                in_=h_sb[g][:, :, HALF * a + c0 : HALF * a + c1].rearrange("p t (c i) -> p c t i", i=4),
+                out=woven[g, a].rearrange("p (c i) t -> p c t i", i=4),
+                in_=h_sb[g][:, :, half_cols(a)].rearrange("p t (c i) -> p c t i", i=4),
             )
 
         def quantize_h(g, a):
             nc.vector.quantize_mx(
-                out=h_w[a][:, g, :].bitcast(FP8X4), scales=h_s[a][H_FIRST:P, g, :],
+                out=h_w[g][:, half_cols(a)].bitcast(FP8X4), scales=h_s[H_FIRST:P, g, half_cols(a)],
                 in_=woven[g, a].rearrange("p c t -> p (c t)"),
             )
 
-        steps = [(g, a, t) for g in range(G) for t in range(PACK) for a in range(HALVES)]
-        gates = {}
+        steps = [(g, a, t) for g in range(G) for a in range(HALVES) for t in range(PACK)]
 
         def make_gate(step):
             g, a, t = steps[step]
@@ -178,11 +176,13 @@ def tile_list_treaty_pricing_kernel(
                 lhsT_scale=w2_s[:, first : first + P],
                 rhs=v_w[a][:].bitcast(FP8X4), rhs_scale=v_s[:, half_cols(a)], start=True, stop=True,
             )
-            gates[step] = gate_pool.tile([P, HALF], F32, name="gate")
-            nc.scalar.activation(out=gates[step][:], in_=hit[:], func=SIGMOID, bias=att_sb[:, g, t : t + 1])
+            nc.scalar.activation(
+                out=h_sb[g][:, t, half_cols(a)], in_=hit[:], func=SIGMOID, bias=att_sb[:, g, t : t + 1]
+            )
 
         for step in range(LEAD):
             make_gate(step)
+        round_w1(nc.scalar.copy, 1, 0, P // 2)
         for step, (g, a, t) in enumerate(steps):
             places = slice(P * t, P * (t + 1))
             if step + LEAD < len(steps):
@@ -192,77 +192,78 @@ def tile_list_treaty_pricing_kernel(
                 out=loss[:], lhsT=w1_w[g][:, places].bitcast(FP8X4), lhsT_scale=w1_s[g][:, places],
                 rhs=v_w[a][:].bitcast(FP8X4), rhs_scale=v_s[:, half_cols(a)], start=True, stop=True,
             )
+            part = h_sb[g][:, t, half_cols(a)]
             nc.vector.scalar_tensor_tensor(
-                out=h_sb[g][:, t, half_cols(a)], in0=loss[:], scalar=load_sb[:, g, t : t + 1], in1=gates[step][:],
-                op0=ADD, op1=MULT,
+                out=part, in0=loss[:], scalar=load_sb[:, g, t : t + 1], in1=part, op0=ADD, op1=MULT,
             )
-            if a == HALVES - 1 and t % 2 == 1:
+            if (a, t) == (HALVES - 1, PACK - 1):
                 rows = out_1[GROUP * g : GROUP * (g + 1), :].rearrange("(p t) j -> p t j", t=PACK)
-                nc.sync.dma_start(out=rows[:, t - 1 : t + 1, :], in_=h_sb[g][:, t - 1 : t + 1, :])
-            if (g, a, t) == (0, 0, 1):
-                round_w1(nc.scalar.copy, 1, 0, P // 2)
-            if (g, a, t) == (0, HALVES - 1, PACK - 1):
+                nc.sync.dma_start(out=rows, in_=h_sb[g][:])
+            if (g, a, t) == (0, 0, PACK - 1):
                 cols = GPSIMD_PIECE // PACK
                 for c in range(0, HALF, cols):
                     gpsimd_round(woven[0, 0][:, c : c + cols, :], h_sb[0][:, :, c : c + cols].rearrange("p t c -> p c t"))
-            if g < LAST and (a, t) == (HALVES - 1, PACK - 2):
+            if g < G - 1 and (a, t) == (HALVES - 1, 1):
                 quantize_w1(g + 1)
+            if (g, a, t) == (1, HALVES - 1, PACK - 1):
+                weave(nc.scalar.copy, 1, 0)
+            if g == G - 1 and t == 1:
+                quantize_h(a, 0)
 
-        late = keep("w2_w", [P, len(SCALAR_WEAVES), HALF, PACK], BF16)
-        for i, (g, a) in enumerate(SCALAR_WEAVES):
+        scalar_weaves = ((0, 1), (1, 1))
+        late = keep("w2_w", [P, len(scalar_weaves), HALF, PACK], BF16)
+        for i, (g, a) in enumerate(scalar_weaves):
             woven[g, a] = late[:, i]
-            weave(nc.scalar.copy, g, a, 0, HALF // 2 if g == LAST else HALF)
-        quantize_h(0, 0)
-        weave(nc.vector.tensor_copy, LAST, 0)
-        quantize_h(1, 0)
-        quantize_h(LAST, 0)
+            weave(nc.scalar.copy, g, a)
+        weave(nc.vector.tensor_copy, 2, 0)
+        quantize_h(2, 0)
+        weave(nc.vector.tensor_copy, 2, 1)
+        quantize_h(0, 1)
+        quantize_h(2, 1)
         words = out_2.rearrange("g p m t -> p g (m t)").bitcast(I32)
-
-        def store_words(a, groups):
-            nc.sync.dma_start(out=words[:, groups, half_cols(a)], in_=h_w[a][:, groups, :].bitcast(I32))
-
-        def store_scales(a):
-            for r in range(PACK):
-                nc.sync.dma_start(
-                    out=out_3[:, r:BLOCKS:PACK, half_cols(a)].rearrange("g q m -> q g m").bitcast(I32),
-                    in_=live_rows(h_s[a], H_FIRST, r),
-                )
-
-        weave(nc.vector.tensor_copy, LAST, 1, HALF // 2, HALF)
-        store_words(0, slice(0, G))
-        store_scales(0)
+        nc.sync.dma_start(out=words[:, 0:G:2, :], in_=early_w[:].bitcast(I32))
+        quantize_h(1, 1)
+        nc.sync.dma_start(out=words[:, 1, :], in_=late_w[:].bitcast(I32))
+        for r in range(PACK):
+            nc.sync.dma_start(
+                out=out_3[:, r:BLOCKS:PACK, :].rearrange("g q m -> q g m").bitcast(I32),
+                in_=live_rows(h_s, H_FIRST, r),
+            )
 
         out_rows = out_0.rearrange("(c p) j -> p c j", p=P)
         acc = {}
 
-        def mix(a, c, groups):
+        def mix(c, a, groups):
             lines = slice(P * c, P * (c + 1))
             if 0 in groups:
-                acc[a, c] = bank((2 * RING + LINES * a + c) % BANKS)
+                acc[c, a] = bank((2 * RING + LINES * a + c) % BANKS)
             for g in groups:
                 nc.tensor.matmul_mx(
-                    out=acc[a, c][:], lhsT=w3_w[:, g, lines].bitcast(FP8X4), lhsT_scale=w3_s[W3_FIRST:P, g, lines],
-                    rhs=h_w[a][:, g, :].bitcast(FP8X4), rhs_scale=h_s[a][H_FIRST:P, g, :],
-                    start=(g == 0), stop=(g == LAST),
+                    out=acc[c, a][:], lhsT=w3_w[:, g, lines].bitcast(FP8X4), lhsT_scale=w3_s[W3_FIRST:P, g, lines],
+                    rhs=h_w[g][:, half_cols(a)].bitcast(FP8X4), rhs_scale=h_s[H_FIRST:P, g, half_cols(a)],
+                    start=(g == 0), stop=(g == closing[a]),
                 )
 
-        def finish(a, c):
-            nc.vector.tensor_tensor(out=y_sb[a][:, c, :], in0=acc[a, c][:], in1=y_sb[a][:, c, :], op=ADD)
-            if c + 1 in Y_STORES[a]:
-                rows = slice(((0,) + Y_STORES[a])[Y_STORES[a].index(c + 1)], c + 1)
-                nc.sync.dma_start(out=out_rows[:, rows, half_cols(a)], in_=y_sb[a][:, rows, :])
+        def add_prem(c, a):
+            part = y_sb[:, c, half_cols(a)]
+            if a == 0 and c < GPSIMD_SUMS:
+                sums = keep("sums%d" % c, [P, HALF], F32)
+                nc.scalar.copy(out=sums[:], in_=acc[c, a][:])
+                nc.gpsimd.tensor_tensor(out=part, in0=sums[:], in1=part, op=ADD)
+            else:
+                nc.vector.tensor_tensor(out=part, in0=acc[c, a][:], in1=part, op=ADD)
 
+        closing = (2, 1)
+        for g in range(G):
+            for c in range(LINES):
+                mix(c, 0, (g,))
+        for c in range(GPSIMD_SUMS):
+            add_prem(c, 0)
         for c in range(LINES):
-            mix(0, c, (0,))
-        for c in range(LINES):
-            mix(0, c, (1, LAST))
-            finish(0, c)
-            if c % 2 == 1:
-                quantize_h(c // 2, 1)
-            if c == 3:
-                store_words(1, slice(0, LAST))
-        store_words(1, slice(LAST, G))
-        store_scales(1)
-        for c in range(LINES):
-            mix(1, c, range(G))
-            finish(1, c)
+            mix(c, 1, (0, 2, 1))
+            if c >= GPSIMD_SUMS:
+                add_prem(c, 0)
+            add_prem(c, 1)
+            if c + 1 in Y_STORES:
+                rows = slice(((0,) + Y_STORES)[Y_STORES.index(c + 1)], c + 1)
+                nc.sync.dma_start(out=out_rows[:, rows, :], in_=y_sb[:, rows, :])

@@ -33,9 +33,12 @@ TAB_LEAD = T // 4
 GPSIMD_SUMS = 3
 GPSIMD_PIECE = 512
 LEAD = 6
+W1_STEPS = (5, 13)
+H_STEPS = (17, 21)
 RING = 3
 BANKS = 8
-Y_STORES = (2, 4, 5, 6)
+Y_STORES = (1, 2, 3, 4, 6)
+SECOND_BANKS = (4, 5, 1, 2, 3, 6)
 
 
 def tile_list_treaty_pricing_kernel(
@@ -148,8 +151,7 @@ def tile_list_treaty_pricing_kernel(
                 )
 
         h_sb = [keep("h%d" % g, [P, PACK, S], F32) for g in range(G)]
-        early_w, late_w = keep("early_w", [P, 2, S], U32), keep("late_w", [P, S], U32)
-        h_w = (early_w[:, 0, :], late_w[:], early_w[:, 1, :])
+        h_w = [keep("h_w%d" % a, [P, G, HALF], U32) for a in range(HALVES)]
         h_s = keep("h_s", [P, G, S], U8)
         woven = {(g, a): keep("woven%d%d" % (g, a), [P, HALF, PACK], BF16)[:] for g, a in ((0, 0), (1, 0), (2, 0), (2, 1))}
 
@@ -161,11 +163,12 @@ def tile_list_treaty_pricing_kernel(
 
         def quantize_h(g, a):
             nc.vector.quantize_mx(
-                out=h_w[g][:, half_cols(a)].bitcast(FP8X4), scales=h_s[H_FIRST:P, g, half_cols(a)],
+                out=h_w[a][:, g, :].bitcast(FP8X4), scales=h_s[H_FIRST:P, g, half_cols(a)],
                 in_=woven[g, a].rearrange("p c t -> p (c t)"),
             )
 
-        steps = [(g, a, t) for g in range(G) for a in range(HALVES) for t in range(PACK)]
+        steps = [(0, a, t) for a in range(HALVES) for t in range(PACK)]
+        steps = steps + [(g, a, t) for g in range(1, G) for t in range(PACK) for a in range(HALVES)]
 
         def make_gate(step):
             g, a, t = steps[step]
@@ -196,74 +199,77 @@ def tile_list_treaty_pricing_kernel(
             nc.vector.scalar_tensor_tensor(
                 out=part, in0=loss[:], scalar=load_sb[:, g, t : t + 1], in1=part, op0=ADD, op1=MULT,
             )
-            if (a, t) == (HALVES - 1, PACK - 1):
-                rows = out_1[GROUP * g : GROUP * (g + 1), :].rearrange("(p t) j -> p t j", t=PACK)
+            rows = out_1[GROUP * g : GROUP * (g + 1), :].rearrange("(p t) j -> p t j", t=PACK)
+            if (g, a, t) == (0, HALVES - 1, PACK - 1):
                 nc.sync.dma_start(out=rows, in_=h_sb[g][:])
+            if g > 0 and a == HALVES - 1 and t % 2 == 1:
+                nc.sync.dma_start(out=rows[:, t - 1 : t + 1, :], in_=h_sb[g][:, t - 1 : t + 1, :])
             if (g, a, t) == (0, 0, PACK - 1):
                 cols = GPSIMD_PIECE // PACK
                 for c in range(0, HALF, cols):
                     gpsimd_round(woven[0, 0][:, c : c + cols, :], h_sb[0][:, :, c : c + cols].rearrange("p t c -> p c t"))
-            if g < G - 1 and (a, t) == (HALVES - 1, 1):
+            if step in W1_STEPS:
                 quantize_w1(g + 1)
             if (g, a, t) == (1, HALVES - 1, PACK - 1):
                 weave(nc.scalar.copy, 1, 0)
-            if g == G - 1 and t == 1:
-                quantize_h(a, 0)
+            if step in H_STEPS:
+                quantize_h(H_STEPS.index(step), 0)
 
         scalar_weaves = ((0, 1), (1, 1))
         late = keep("w2_w", [P, len(scalar_weaves), HALF, PACK], BF16)
         for i, (g, a) in enumerate(scalar_weaves):
             woven[g, a] = late[:, i]
             weave(nc.scalar.copy, g, a)
+        words = out_2.rearrange("g p m t -> p g (m t)").bitcast(I32)
+
+        def store_words(a, groups):
+            nc.sync.dma_start(out=words[:, groups, half_cols(a)], in_=h_w[a][:, groups, :].bitcast(I32))
+
         weave(nc.vector.tensor_copy, 2, 0)
         quantize_h(2, 0)
-        weave(nc.vector.tensor_copy, 2, 1)
+        store_words(0, slice(0, G))
         quantize_h(0, 1)
-        quantize_h(2, 1)
-        words = out_2.rearrange("g p m t -> p g (m t)").bitcast(I32)
-        nc.sync.dma_start(out=words[:, 0:G:2, :], in_=early_w[:].bitcast(I32))
-        quantize_h(1, 1)
-        nc.sync.dma_start(out=words[:, 1, :], in_=late_w[:].bitcast(I32))
-        for r in range(PACK):
-            nc.sync.dma_start(
-                out=out_3[:, r:BLOCKS:PACK, :].rearrange("g q m -> q g m").bitcast(I32),
-                in_=live_rows(h_s, H_FIRST, r),
-            )
+        store_words(1, slice(0, 1))
+        weave(nc.vector.tensor_copy, 2, 1)
+        for g in range(1, G):
+            quantize_h(g, 1)
+            store_words(1, slice(g, g + 1))
 
         out_rows = out_0.rearrange("(c p) j -> p c j", p=P)
         acc = {}
 
-        def mix(c, a, groups):
+        def mix(c, a, groups, b):
             lines = slice(P * c, P * (c + 1))
             if 0 in groups:
-                acc[c, a] = bank((2 * RING + LINES * a + c) % BANKS)
+                acc[c, a] = bank(b % BANKS)
             for g in groups:
                 nc.tensor.matmul_mx(
                     out=acc[c, a][:], lhsT=w3_w[:, g, lines].bitcast(FP8X4), lhsT_scale=w3_s[W3_FIRST:P, g, lines],
-                    rhs=h_w[g][:, half_cols(a)].bitcast(FP8X4), rhs_scale=h_s[H_FIRST:P, g, half_cols(a)],
-                    start=(g == 0), stop=(g == closing[a]),
+                    rhs=h_w[a][:, g, :].bitcast(FP8X4), rhs_scale=h_s[H_FIRST:P, g, half_cols(a)],
+                    start=(g == 0), stop=(g == G - 1),
                 )
 
-        def add_prem(c, a):
-            part = y_sb[:, c, half_cols(a)]
-            if a == 0 and c < GPSIMD_SUMS:
-                sums = keep("sums%d" % c, [P, HALF], F32)
-                nc.scalar.copy(out=sums[:], in_=acc[c, a][:])
-                nc.gpsimd.tensor_tensor(out=part, in0=sums[:], in1=part, op=ADD)
-            else:
-                nc.vector.tensor_tensor(out=part, in0=acc[c, a][:], in1=part, op=ADD)
-
-        closing = (2, 1)
         for g in range(G):
             for c in range(LINES):
-                mix(c, 0, (g,))
-        for c in range(GPSIMD_SUMS):
-            add_prem(c, 0)
+                mix(c, 0, (g,), 2 * RING + c)
+        for c in range(LINES - GPSIMD_SUMS, LINES):
+            part = y_sb[:, c, half_cols(0)]
+            sums = keep("sums%d" % c, [P, HALF], F32)
+            nc.scalar.copy(out=sums[:], in_=acc[c, 0][:])
+            nc.gpsimd.tensor_tensor(out=part, in0=sums[:], in1=part, op=ADD)
         for c in range(LINES):
-            mix(c, 1, (0, 2, 1))
-            if c >= GPSIMD_SUMS:
-                add_prem(c, 0)
-            add_prem(c, 1)
+            for a in range(HALVES):
+                if a == 1:
+                    mix(c, a, range(G), SECOND_BANKS[c])
+                if a == 1 or c < LINES - GPSIMD_SUMS:
+                    part = y_sb[:, c, half_cols(a)]
+                    nc.vector.tensor_tensor(out=part, in0=acc[c, a][:], in1=part, op=ADD)
             if c + 1 in Y_STORES:
                 rows = slice(((0,) + Y_STORES)[Y_STORES.index(c + 1)], c + 1)
                 nc.sync.dma_start(out=out_rows[:, rows, :], in_=y_sb[:, rows, :])
+            if c == 0:
+                for r in range(PACK):
+                    nc.sync.dma_start(
+                        out=out_3[:, r:BLOCKS:PACK, :].rearrange("g q m -> q g m").bitcast(I32),
+                        in_=live_rows(h_s, H_FIRST, r),
+                    )

@@ -27,8 +27,7 @@ LINES = N // P
 QUAD = 32
 BLOCKS = 16
 SPREAD = P // BLOCKS
-BIAS_PITCH = 8
-H_FIRST, W3_FIRST = 4, 8
+H_FIRST, W3_FIRST = 12, 4
 TAB_LEAD = T // 4
 GPSIMD_SUMS = 3
 GPSIMD_PIECE = 512
@@ -67,8 +66,8 @@ def tile_list_treaty_pricing_kernel(
         def live_rows(plane, first, r):
             return plane[first + r : P : QUAD].bitcast(I32)
 
-        def deal(out, in_):
-            nc.vector.tensor_copy(
+        def deal(copy, out, in_):
+            copy(
                 out=out.rearrange("p (g t m) -> p t g m", g=G, t=PACK),
                 in_=in_.rearrange("p (g m t) -> p t g m", g=G, t=PACK),
             )
@@ -82,13 +81,13 @@ def tile_list_treaty_pricing_kernel(
         w2s_raw = zeroed_plane("w2s_raw", [P, H])
         nc.sync.dma_start(out=tab_s[0:P:SPREAD].bitcast(I32), in_=tab_scales[0].bitcast(I32))
         nc.sync.dma_start(out=w2s_raw[0:P:SPREAD].bitcast(I32), in_=w2_scales[0].bitcast(I32))
+        bias_rows = keep("bias_rows", [P, G, P], F32)
+        nc.vector.memset(bias_rows[:], 0.0)
+        for i, vec in enumerate((att, load)):
+            nc.sync.dma_start(out=bias_rows[i:P:QUAD], in_=vec.rearrange("(g q c) -> q g c", g=G, c=P))
         w2_raw = keep("w2_raw", [P, 2 * H], U8)
         nc.sync.dma_start(out=w2_raw[:].bitcast(I32), in_=w2_words[0].bitcast(I32))
         nc.sync.dma_start(out=tab_w[:, TAB_LEAD:].bitcast(I32), in_=tab_rows[:, TAB_LEAD:])
-        att_sb = keep("att_sb", [P, G, BIAS_PITCH], F32)
-        nc.sync.dma_start(out=att_sb[:, :, 0:PACK], in_=att.rearrange("(g p t) -> p g t", p=P, t=PACK))
-        load_sb = keep("load_sb", [P, G, BIAS_PITCH], F32)
-        nc.sync.dma_start(out=load_sb[:, :, 0:PACK], in_=load.rearrange("(g p t) -> p g t", p=P, t=PACK))
         w1_rows = w1.rearrange("(p j) c -> p j c", j=PACK)
         w1_raw = [keep("w1_raw%d" % g, [P, PACK, GROUP], F32) for g in range(G)]
         nc.sync.dma_start(out=w1_raw[0][:, 0:2, :], in_=w1_rows[:, 0:2, 0:GROUP])
@@ -96,7 +95,7 @@ def tile_list_treaty_pricing_kernel(
         planes = keep("planes", [P, S + H], U8)
         nc.vector.tensor_copy(picked_s[:], tab_s[:].indirect(offsets[:]))
         nc.vector.tensor_copy(out=planes[:, 0:S].bitcast(I32), in_=picked_s[:].bitcast(I32))
-        deal(planes[:, S:], w2s_raw[:])
+        deal(nc.vector.tensor_copy, planes[:, S:], w2s_raw[:])
         for r in range(1, PACK):
             nc.sync.dma_start(out=live_rows(planes, 0, r), in_=live_rows(planes, 0, SPREAD * r))
         v_s = planes[:, 0:S]
@@ -133,7 +132,20 @@ def tile_list_treaty_pricing_kernel(
                 in_=w1_b[g][:].rearrange("p t m j -> p (t m j)"),
             )
 
-        deal(w2_w[:].bitcast(U16), w2_raw[:].bitcast(U16))
+        deal(nc.scalar.copy, w2_w[:].bitcast(U16), w2_raw[:].bitcast(U16))
+        bias_blocks = keep("w2s_raw", [P, G * P], F32)
+        nc.vector.tensor_copy(
+            out=bias_blocks[:].rearrange("p (g t u) -> p t g u", g=G, t=PACK),
+            in_=bias_rows[:].rearrange("p g (u t) -> p t g u", t=PACK),
+        )
+        biases = keep("biases", [P, G * P], F32)
+        for cols in (slice(0, 2 * P), slice(2 * P, G * P)):
+            nc.vector.transpose(out=biases[:, cols], in_=bias_blocks[:, cols])
+
+        def bias(i, g, t):
+            c = QUAD * (PACK * g + t) + i
+            return biases[:, c : c + 1]
+
         for a in range(HALVES):
             nc.vector.tensor_copy(v_w[a][:], tab_w[:].indirect(offsets[:, HALF // 16 * a : HALF // 16 * (a + 1)]))
         round_w1(nc.vector.tensor_copy, 0, 0, P)
@@ -180,7 +192,7 @@ def tile_list_treaty_pricing_kernel(
                 rhs=v_w[a][:].bitcast(FP8X4), rhs_scale=v_s[:, half_cols(a)], start=True, stop=True,
             )
             nc.scalar.activation(
-                out=h_sb[g][:, t, half_cols(a)], in_=hit[:], func=SIGMOID, bias=att_sb[:, g, t : t + 1]
+                out=h_sb[g][:, t, half_cols(a)], in_=hit[:], func=SIGMOID, bias=bias(0, g, t)
             )
 
         for step in range(LEAD):
@@ -197,7 +209,7 @@ def tile_list_treaty_pricing_kernel(
             )
             part = h_sb[g][:, t, half_cols(a)]
             nc.vector.scalar_tensor_tensor(
-                out=part, in0=loss[:], scalar=load_sb[:, g, t : t + 1], in1=part, op0=ADD, op1=MULT,
+                out=part, in0=loss[:], scalar=bias(1, g, t), in1=part, op0=ADD, op1=MULT,
             )
             rows = out_1[GROUP * g : GROUP * (g + 1), :].rearrange("(p t) j -> p t j", t=PACK)
             if (g, a, t) == (0, HALVES - 1, PACK - 1):

@@ -28,16 +28,17 @@ QUAD = 32
 BLOCKS = 16
 SPREAD = P // BLOCKS
 H_FIRST, W3_FIRST = 12, 4
+BIAS_ROW = 20
 TAB_LEAD = T // 4
 GPSIMD_SUMS = 3
 GPSIMD_PIECE = 512
 LEAD = 6
 W1_STEPS = (5, 13)
 H_STEPS = (17, 21)
-RING = 3
-BANKS = 8
+HIT_RING, LOSS_RING = 5, 3
 Y_STORES = (1, 2, 3, 4, 6)
-SECOND_BANKS = (4, 5, 1, 2, 3, 6)
+FIRST_BANKS = (4, 0, 1, 2, 3, 5)
+SECOND_BANKS = (6, 7, 2, 3, 5, 4)
 
 
 def tile_list_treaty_pricing_kernel(
@@ -72,25 +73,25 @@ def tile_list_treaty_pricing_kernel(
                 in_=in_.rearrange("p (g m t) -> p t g m", g=G, t=PACK),
             )
 
-        offsets = held.tile([P, S // 16], U16, name="offsets")
-        nc.sync.dma_start(offsets[:], offs)
         tab_w = keep("tab_w", [P, T], U32)
         tab_rows = tab_words[0].rearrange("p n t -> p (n t)").bitcast(I32)
         nc.sync.dma_start(out=tab_w[:, 0:TAB_LEAD].bitcast(I32), in_=tab_rows[:, 0:TAB_LEAD])
+        offsets = held.tile([P, S // 16], U16, name="offsets")
+        nc.sync.dma_start(offsets[:], offs)
         tab_s = zeroed_plane("tab_s", [P, T])
         w2s_raw = zeroed_plane("w2s_raw", [P, H])
         nc.sync.dma_start(out=tab_s[0:P:SPREAD].bitcast(I32), in_=tab_scales[0].bitcast(I32))
+        w2_raw = keep("w2_raw", [P, 2 * H], U8)
+        nc.sync.dma_start(out=w2_raw[:].bitcast(I32), in_=w2_words[0].bitcast(I32))
         nc.sync.dma_start(out=w2s_raw[0:P:SPREAD].bitcast(I32), in_=w2_scales[0].bitcast(I32))
         bias_rows = keep("bias_rows", [P, G, P], F32)
         nc.vector.memset(bias_rows[:], 0.0)
         for i, vec in enumerate((att, load)):
-            nc.sync.dma_start(out=bias_rows[i:P:QUAD], in_=vec.rearrange("(g q c) -> q g c", g=G, c=P))
-        w2_raw = keep("w2_raw", [P, 2 * H], U8)
-        nc.sync.dma_start(out=w2_raw[:].bitcast(I32), in_=w2_words[0].bitcast(I32))
+            nc.sync.dma_start(out=bias_rows[BIAS_ROW + i : P : QUAD], in_=vec.rearrange("(g q c) -> q g c", g=G, c=P))
         nc.sync.dma_start(out=tab_w[:, TAB_LEAD:].bitcast(I32), in_=tab_rows[:, TAB_LEAD:])
         w1_rows = w1.rearrange("(p j) c -> p j c", j=PACK)
         w1_raw = [keep("w1_raw%d" % g, [P, PACK, GROUP], F32) for g in range(G)]
-        nc.sync.dma_start(out=w1_raw[0][:, 0:2, :], in_=w1_rows[:, 0:2, 0:GROUP])
+        nc.sync.dma_start(out=w1_raw[0][:], in_=w1_rows[:, :, 0:GROUP])
         picked_s = keep("picked_s", [P, S], U8)
         planes = keep("planes", [P, S + H], U8)
         nc.vector.tensor_copy(picked_s[:], tab_s[:].indirect(offsets[:]))
@@ -100,7 +101,6 @@ def tile_list_treaty_pricing_kernel(
             nc.sync.dma_start(out=live_rows(planes, 0, r), in_=live_rows(planes, 0, SPREAD * r))
         v_s = planes[:, 0:S]
         w2_s = planes[:, S:]
-        nc.sync.dma_start(out=w1_raw[0][:, 2:PACK, :], in_=w1_rows[:, 2:PACK, 0:GROUP])
         for g in range(1, G):
             nc.sync.dma_start(out=w1_raw[g][:], in_=w1_rows[:, :, GROUP * g : GROUP * (g + 1)])
         w3_w = keep("w3_w", [P, G, N], U32)
@@ -133,8 +133,8 @@ def tile_list_treaty_pricing_kernel(
             )
 
         deal(nc.scalar.copy, w2_w[:].bitcast(U16), w2_raw[:].bitcast(U16))
-        bias_blocks = keep("w2s_raw", [P, G * P], F32)
-        nc.vector.tensor_copy(
+        bias_blocks = keep("bias_blocks", [P, G * P], F32)
+        nc.scalar.copy(
             out=bias_blocks[:].rearrange("p (g t u) -> p t g u", g=G, t=PACK),
             in_=bias_rows[:].rearrange("p g (u t) -> p t g u", t=PACK),
         )
@@ -143,7 +143,7 @@ def tile_list_treaty_pricing_kernel(
             nc.vector.transpose(out=biases[:, cols], in_=bias_blocks[:, cols])
 
         def bias(i, g, t):
-            c = QUAD * (PACK * g + t) + i
+            c = QUAD * (PACK * g + t) + BIAS_ROW + i
             return biases[:, c : c + 1]
 
         for a in range(HALVES):
@@ -185,7 +185,7 @@ def tile_list_treaty_pricing_kernel(
         def make_gate(step):
             g, a, t = steps[step]
             first = GROUP * g + P * t
-            hit = bank(step % RING)
+            hit = bank(step % HIT_RING)
             nc.tensor.matmul_mx(
                 out=hit[:], lhsT=w2_w[:, 2 * first : 2 * (first + P)].bitcast(FP4X4),
                 lhsT_scale=w2_s[:, first : first + P],
@@ -202,7 +202,7 @@ def tile_list_treaty_pricing_kernel(
             places = slice(P * t, P * (t + 1))
             if step + LEAD < len(steps):
                 make_gate(step + LEAD)
-            loss = bank(RING + step % RING)
+            loss = bank(HIT_RING + step % LOSS_RING)
             nc.tensor.matmul_mx(
                 out=loss[:], lhsT=w1_w[g][:, places].bitcast(FP8X4), lhsT_scale=w1_s[g][:, places],
                 rhs=v_w[a][:].bitcast(FP8X4), rhs_scale=v_s[:, half_cols(a)], start=True, stop=True,
@@ -253,7 +253,7 @@ def tile_list_treaty_pricing_kernel(
         def mix(c, a, groups, b):
             lines = slice(P * c, P * (c + 1))
             if 0 in groups:
-                acc[c, a] = bank(b % BANKS)
+                acc[c, a] = bank(b)
             for g in groups:
                 nc.tensor.matmul_mx(
                     out=acc[c, a][:], lhsT=w3_w[:, g, lines].bitcast(FP8X4), lhsT_scale=w3_s[W3_FIRST:P, g, lines],
@@ -263,7 +263,7 @@ def tile_list_treaty_pricing_kernel(
 
         for g in range(G):
             for c in range(LINES):
-                mix(c, 0, (g,), 2 * RING + c)
+                mix(c, 0, (g,), FIRST_BANKS[c])
         for c in range(LINES - GPSIMD_SUMS, LINES):
             part = y_sb[:, c, half_cols(0)]
             sums = keep("sums%d" % c, [P, HALF], F32)

@@ -33,8 +33,9 @@ TAB_LEAD = T // 4
 GPSIMD_SUMS = 3
 GPSIMD_PIECE = 512
 LEAD = 6
+W1_ROUND_STEP = 2
 W1_STEPS = (5, 13)
-H_STEPS = (17, 21)
+H_STEP = 21
 HIT_RING, LOSS_RING = 5, 3
 Y_STORES = (1, 2, 3, 4, 6)
 FIRST_BANKS = (4, 0, 1, 2, 3, 5)
@@ -197,7 +198,6 @@ def tile_list_treaty_pricing_kernel(
 
         for step in range(LEAD):
             make_gate(step)
-        round_w1(nc.scalar.copy, 1, 0, P // 2)
         for step, (g, a, t) in enumerate(steps):
             places = slice(P * t, P * (t + 1))
             if step + LEAD < len(steps):
@@ -220,12 +220,14 @@ def tile_list_treaty_pricing_kernel(
                 cols = GPSIMD_PIECE // PACK
                 for c in range(0, HALF, cols):
                     gpsimd_round(woven[0, 0][:, c : c + cols, :], h_sb[0][:, :, c : c + cols].rearrange("p t c -> p c t"))
+            if step == W1_ROUND_STEP:
+                round_w1(nc.vector.tensor_copy, 1, 0, P // 2)
             if step in W1_STEPS:
                 quantize_w1(g + 1)
             if (g, a, t) == (1, HALVES - 1, PACK - 1):
                 weave(nc.scalar.copy, 1, 0)
-            if step in H_STEPS:
-                quantize_h(H_STEPS.index(step), 0)
+            if step == H_STEP:
+                quantize_h(1, 0)
 
         scalar_weaves = ((0, 1), (1, 1))
         late = keep("w2_w", [P, len(scalar_weaves), HALF, PACK], BF16)
@@ -237,6 +239,7 @@ def tile_list_treaty_pricing_kernel(
         def store_words(a, groups):
             nc.sync.dma_start(out=words[:, groups, half_cols(a)], in_=h_w[a][:, groups, :].bitcast(I32))
 
+        quantize_h(0, 0)
         weave(nc.vector.tensor_copy, 2, 0)
         quantize_h(2, 0)
         store_words(0, slice(0, G))
@@ -252,16 +255,17 @@ def tile_list_treaty_pricing_kernel(
 
         def mix(c, a, groups, b):
             lines = slice(P * c, P * (c + 1))
-            if 0 in groups:
+            if (c, a) not in acc:
                 acc[c, a] = bank(b)
             for g in groups:
                 nc.tensor.matmul_mx(
                     out=acc[c, a][:], lhsT=w3_w[:, g, lines].bitcast(FP8X4), lhsT_scale=w3_s[W3_FIRST:P, g, lines],
                     rhs=h_w[a][:, g, :].bitcast(FP8X4), rhs_scale=h_s[H_FIRST:P, g, half_cols(a)],
-                    start=(g == 0), stop=(g == G - 1),
+                    start=(g == opening[a]), stop=(g == G - 1),
                 )
 
-        for g in range(G):
+        opening = (1, 0)
+        for g in (1, 0, 2):
             for c in range(LINES):
                 mix(c, 0, (g,), FIRST_BANKS[c])
         for c in range(LINES - GPSIMD_SUMS, LINES):

from contextlib import ExitStack

import concourse.mybir as mybir

T, S, K, H, N = 4096, 1024, 512, 1536, 768
FLOPS = 2 * S * (2 * K * H + H * N)

F32 = mybir.dt.float32
BF16 = mybir.dt.bfloat16
I32 = mybir.dt.int32
U32 = mybir.dt.uint32
U16 = mybir.dt.uint16
U8 = mybir.dt.uint8
FP8X4 = mybir.dt.float8_e4m3fn_x4
FP4X4 = mybir.dt.float4_e2m1fn_x4
ADD = mybir.AluOpType.add
MULT = mybir.AluOpType.mult
SIGMOID = mybir.ActivationFunctionType.Sigmoid

P = 128
PACK = 4
GROUP = P * PACK
G = H // GROUP
HALF = 512
HALVES = S // HALF
LINES = N // P
QUAD = 32
BLOCKS = 16
SPREAD = P // BLOCKS
H_FIRST, W3_FIRST = 12, 4
BIAS_ROW = 20
TAB_LEAD = T // 4
GPSIMD_SUMS = 3
GPSIMD_PIECE = 512
LEAD = 6
W1_ROUND_STEP = 2
W1_STEPS = (5, 13)
H_STEP = 21
HIT_RING, LOSS_RING = 5, 3
Y_STORES = (1, 2, 3, 4, 6)
FIRST_BANKS = (4, 0, 1, 2, 3, 5)
SECOND_BANKS = (6, 7, 2, 3, 5, 4)


def tile_list_treaty_pricing_kernel(
    tc, tab_words, tab_scales, offs, w1, load, w2_words, w2_scales, att, w3_words, w3_scales, prem,
    out_0, out_1, out_2, out_3,
):
    nc = tc.nc
    with ExitStack() as ctx:
        held = ctx.enter_context(tc.tile_pool(name="held", bufs=1))
        psum = ctx.enter_context(tc.psum_pool(name="psum", bufs=1))

        def keep(name, shape, dtype):
            return held.tile(shape, dtype, name=name, align_bytes=64)

        def zeroed_plane(name, shape):
            plane = keep(name, shape, U8)
            nc.vector.memset(plane[:].bitcast(I32), 0)
            return plane

        def bank(b):
            return psum.tile([P, HALF], F32, name="bank%d" % b)

        def half_cols(a):
            return slice(HALF * a, HALF * (a + 1))

        def live_rows(plane, first, r):
            return plane[first + r : P : QUAD].bitcast(I32)

        def deal(copy, out, in_):
            copy(
                out=out.rearrange("p (g t m) -> p t g m", g=G, t=PACK),
                in_=in_.rearrange("p (g m t) -> p t g m", g=G, t=PACK),
            )

        tab_w = keep("tab_w", [P, T], U32)
        tab_rows = tab_words[0].rearrange("p n t -> p (n t)").bitcast(I32)
        nc.sync.dma_start(out=tab_w[:, 0:TAB_LEAD].bitcast(I32), in_=tab_rows[:, 0:TAB_LEAD])
        offsets = held.tile([P, S // 16], U16, name="offsets")
        nc.sync.dma_start(offsets[:], offs)
        tab_s = zeroed_plane("tab_s", [P, T])
        w2s_raw = zeroed_plane("w2s_raw", [P, H])
        nc.sync.dma_start(out=tab_s[0:P:SPREAD].bitcast(I32), in_=tab_scales[0].bitcast(I32))
        w2_raw = keep("w2_raw", [P, 2 * H], U8)
        nc.sync.dma_start(out=w2_raw[:].bitcast(I32), in_=w2_words[0].bitcast(I32))
        nc.sync.dma_start(out=w2s_raw[0:P:SPREAD].bitcast(I32), in_=w2_scales[0].bitcast(I32))
        bias_rows = keep("bias_rows", [P, G, P], F32)
        nc.vector.memset(bias_rows[:], 0.0)
        for i, vec in enumerate((att, load)):
            nc.sync.dma_start(out=bias_rows[BIAS_ROW + i : P : QUAD], in_=vec.rearrange("(g q c) -> q g c", g=G, c=P))
        nc.sync.dma_start(out=tab_w[:, TAB_LEAD:].bitcast(I32), in_=tab_rows[:, TAB_LEAD:])
        w1_rows = w1.rearrange("(p j) c -> p j c", j=PACK)
        w1_raw = [keep("w1_raw%d" % g, [P, PACK, GROUP], F32) for g in range(G)]
        nc.sync.dma_start(out=w1_raw[0][:], in_=w1_rows[:, :, 0:GROUP])
        picked_s = keep("picked_s", [P, S], U8)
        planes = keep("planes", [P, S + H], U8)
        nc.vector.tensor_copy(picked_s[:], tab_s[:].indirect(offsets[:]))
        nc.vector.tensor_copy(out=planes[:, 0:S].bitcast(I32), in_=picked_s[:].bitcast(I32))
        deal(nc.vector.tensor_copy, planes[:, S:], w2s_raw[:])
        for r in range(1, PACK):
            nc.sync.dma_start(out=live_rows(planes, 0, r), in_=live_rows(planes, 0, SPREAD * r))
        v_s = planes[:, 0:S]
        w2_s = planes[:, S:]
        for g in range(1, G):
            nc.sync.dma_start(out=w1_raw[g][:], in_=w1_rows[:, :, GROUP * g : GROUP * (g + 1)])
        w3_w = keep("w3_w", [P, G, N], U32)
        w3_s = zeroed_plane("w3_s", [P, G, N])
        for r in range(PACK):
            nc.sync.dma_start(
                out=live_rows(w3_s, W3_FIRST, r),
                in_=w3_scales[:, r:BLOCKS:PACK, :].rearrange("g q n -> q g n").bitcast(I32),
            )
        nc.sync.dma_start(out=w3_w[:].bitcast(I32), in_=w3_words.rearrange("g p n t -> p g (n t)").bitcast(I32))
        y_sb = keep("y_sb", [P, LINES, S], F32)
        nc.sync.dma_start(out=y_sb[:], in_=prem.rearrange("(c p) j -> p c j", p=P))

        w2_w = keep("w2_w", [P, 2 * H], U8)
        v_w = [keep("v_w%d" % a, [P, HALF], U32) for a in range(HALVES)]
        w1_b = [keep("w1_b%d" % g, [P, PACK, P, PACK], BF16) for g in range(G)]
        w1_w = [keep("w1_w%d" % g, [P, GROUP], U32) for g in range(G)]
        w1_s = [keep("w1_s%d" % g, [P, GROUP], U8) for g in range(G)]

        def round_w1(copy, g, m0, m1):
            copy(
                out=w1_b[g][:, :, m0:m1, :].rearrange("p t m j -> p m j t"),
                in_=w1_raw[g][:, :, PACK * m0 : PACK * m1].rearrange("p j (m t) -> p m j t", t=PACK),
            )

        def quantize_w1(g):
            nc.vector.quantize_mx(
                out=w1_w[g][:].bitcast(FP8X4), scales=w1_s[g][:],
                in_=w1_b[g][:].rearrange("p t m j -> p (t m j)"),
            )

        deal(nc.scalar.copy, w2_w[:].bitcast(U16), w2_raw[:].bitcast(U16))
        bias_blocks = keep("bias_blocks", [P, G * P], F32)
        nc.scalar.copy(
            out=bias_blocks[:].rearrange("p (g t u) -> p t g u", g=G, t=PACK),
            in_=bias_rows[:].rearrange("p g (u t) -> p t g u", t=PACK),
        )
        biases = keep("biases", [P, G * P], F32)
        for cols in (slice(0, 2 * P), slice(2 * P, G * P)):
            nc.vector.transpose(out=biases[:, cols], in_=bias_blocks[:, cols])

        def bias(i, g, t):
            c = QUAD * (PACK * g + t) + BIAS_ROW + i
            return biases[:, c : c + 1]

        for a in range(HALVES):
            nc.vector.tensor_copy(v_w[a][:], tab_w[:].indirect(offsets[:, HALF // 16 * a : HALF // 16 * (a + 1)]))
        round_w1(nc.vector.tensor_copy, 0, 0, P)
        quantize_w1(0)

        def gpsimd_round(out, in_):
            nc.gpsimd.tensor_scalar(out=out, in0=in_, scalar1=1.0, scalar2=0.0, op0=MULT, op1=ADD)

        piece = GPSIMD_PIECE // (PACK * PACK)
        for g, first in ((1, P // 2), (2, 0)):
            for m0 in range(first, P, piece):
                gpsimd_round(
                    w1_b[g][:, :, m0 : m0 + piece, :].rearrange("p t m j -> p m t j"),
                    w1_raw[g][:, :, PACK * m0 : PACK * (m0 + piece)].rearrange("p j (m t) -> p m t j", t=PACK),
                )

        h_sb = [keep("h%d" % g, [P, PACK, S], F32) for g in range(G)]
        h_w = [keep("h_w%d" % a, [P, G, HALF], U32) for a in range(HALVES)]
        h_s = keep("h_s", [P, G, S], U8)
        woven = {(g, a): keep("woven%d%d" % (g, a), [P, HALF, PACK], BF16)[:] for g, a in ((0, 0), (1, 0), (2, 0), (2, 1))}

        def weave(copy, g, a):
            copy(
                out=woven[g, a].rearrange("p (c i) t -> p c t i", i=4),
                in_=h_sb[g][:, :, half_cols(a)].rearrange("p t (c i) -> p c t i", i=4),
            )

        def quantize_h(g, a):
            nc.vector.quantize_mx(
                out=h_w[a][:, g, :].bitcast(FP8X4), scales=h_s[H_FIRST:P, g, half_cols(a)],
                in_=woven[g, a].rearrange("p c t -> p (c t)"),
            )

        steps = [(0, a, t) for a in range(HALVES) for t in range(PACK)]
        steps = steps + [(g, a, t) for g in range(1, G) for t in range(PACK) for a in range(HALVES)]

        def make_gate(step):
            g, a, t = steps[step]
            first = GROUP * g + P * t
            hit = bank(step % HIT_RING)
            nc.tensor.matmul_mx(
                out=hit[:], lhsT=w2_w[:, 2 * first : 2 * (first + P)].bitcast(FP4X4),
                lhsT_scale=w2_s[:, first : first + P],
                rhs=v_w[a][:].bitcast(FP8X4), rhs_scale=v_s[:, half_cols(a)], start=True, stop=True,
            )
            nc.scalar.activation(
                out=h_sb[g][:, t, half_cols(a)], in_=hit[:], func=SIGMOID, bias=bias(0, g, t)
            )

        for step in range(LEAD):
            make_gate(step)
        for step, (g, a, t) in enumerate(steps):
            places = slice(P * t, P * (t + 1))
            if step + LEAD < len(steps):
                make_gate(step + LEAD)
            loss = bank(HIT_RING + step % LOSS_RING)
            nc.tensor.matmul_mx(
                out=loss[:], lhsT=w1_w[g][:, places].bitcast(FP8X4), lhsT_scale=w1_s[g][:, places],
                rhs=v_w[a][:].bitcast(FP8X4), rhs_scale=v_s[:, half_cols(a)], start=True, stop=True,
            )
            part = h_sb[g][:, t, half_cols(a)]
            nc.vector.scalar_tensor_tensor(
                out=part, in0=loss[:], scalar=bias(1, g, t), in1=part, op0=ADD, op1=MULT,
            )
            rows = out_1[GROUP * g : GROUP * (g + 1), :].rearrange("(p t) j -> p t j", t=PACK)
            if (g, a, t) == (0, HALVES - 1, PACK - 1):
                nc.sync.dma_start(out=rows, in_=h_sb[g][:])
            if g > 0 and a == HALVES - 1 and t % 2 == 1:
                nc.sync.dma_start(out=rows[:, t - 1 : t + 1, :], in_=h_sb[g][:, t - 1 : t + 1, :])
            if (g, a, t) == (0, 0, PACK - 1):
                cols = GPSIMD_PIECE // PACK
                for c in range(0, HALF, cols):
                    gpsimd_round(woven[0, 0][:, c : c + cols, :], h_sb[0][:, :, c : c + cols].rearrange("p t c -> p c t"))
            if step == W1_ROUND_STEP:
                round_w1(nc.vector.tensor_copy, 1, 0, P // 2)
            if step in W1_STEPS:
                quantize_w1(g + 1)
            if (g, a, t) == (1, HALVES - 1, PACK - 1):
                weave(nc.scalar.copy, 1, 0)
            if step == H_STEP:
                quantize_h(1, 0)

        scalar_weaves = ((0, 1), (1, 1))
        late = keep("w2_w", [P, len(scalar_weaves), HALF, PACK], BF16)
        for i, (g, a) in enumerate(scalar_weaves):
            woven[g, a] = late[:, i]
            weave(nc.scalar.copy, g, a)
        words = out_2.rearrange("g p m t -> p g (m t)").bitcast(I32)

        def store_words(a, groups):
            nc.sync.dma_start(out=words[:, groups, half_cols(a)], in_=h_w[a][:, groups, :].bitcast(I32))

        quantize_h(0, 0)
        weave(nc.vector.tensor_copy, 2, 0)
        quantize_h(2, 0)
        store_words(0, slice(0, G))
        quantize_h(0, 1)
        store_words(1, slice(0, 1))
        weave(nc.vector.tensor_copy, 2, 1)
        for g in range(1, G):
            quantize_h(g, 1)
            store_words(1, slice(g, g + 1))

        out_rows = out_0.rearrange("(c p) j -> p c j", p=P)
        acc = {}

        def mix(c, a, groups, b):
            lines = slice(P * c, P * (c + 1))
            if (c, a) not in acc:
                acc[c, a] = bank(b)
            for g in groups:
                nc.tensor.matmul_mx(
                    out=acc[c, a][:], lhsT=w3_w[:, g, lines].bitcast(FP8X4), lhsT_scale=w3_s[W3_FIRST:P, g, lines],
                    rhs=h_w[a][:, g, :].bitcast(FP8X4), rhs_scale=h_s[H_FIRST:P, g, half_cols(a)],
                    start=(g == opening[a]), stop=(g == G - 1),
                )

        opening = (1, 0)
        for g in (1, 0, 2):
            for c in range(LINES):
                mix(c, 0, (g,), FIRST_BANKS[c])
        for c in range(LINES - GPSIMD_SUMS, LINES):
            part = y_sb[:, c, half_cols(0)]
            sums = keep("sums%d" % c, [P, HALF], F32)
            nc.scalar.copy(out=sums[:], in_=acc[c, 0][:])
            nc.gpsimd.tensor_tensor(out=part, in0=sums[:], in1=part, op=ADD)
        for c in range(LINES):
            for a in range(HALVES):
                if a == 1:
                    mix(c, a, range(G), SECOND_BANKS[c])
                if a == 1 or c < LINES - GPSIMD_SUMS:
                    part = y_sb[:, c, half_cols(a)]
                    nc.vector.tensor_tensor(out=part, in0=acc[c, a][:], in1=part, op=ADD)
            if c + 1 in Y_STORES:
                rows = slice(((0,) + Y_STORES)[Y_STORES.index(c + 1)], c + 1)
                nc.sync.dma_start(out=out_rows[:, rows, :], in_=y_sb[:, rows, :])
            if c == 0:
                for r in range(PACK):
                    nc.sync.dma_start(
                        out=out_3[:, r:BLOCKS:PACK, :].rearrange("g q m -> q g m").bitcast(I32),
                        in_=live_rows(h_s, H_FIRST, r),
                    )
